import numpy as np, ml_dtypes
CORES = [2,7,18,23,34]
N = 5
BF = ml_dtypes.bfloat16
def gentries(a):
    return np.ascontiguousarray(a.reshape(8, 16, -1).transpose(0, 2, 1)).reshape(8, -1)
def gtable(e):
    e = np.asarray(e); return np.ascontiguousarray(e.reshape(8, -1, 16).transpose(0, 2, 1)).reshape(128, -1).astype(np.int32)
W, L, P, T = 2048, 128, 32, 6
def place(z, e, kap):
    return ((z * (2 * e + 1)[..., None] >> 5) + z + kap) & (W - 1)
def parts(rng):
    low = rng.random((N, 8, 1, W)) < rng.choice(np.array([0.01, 0.03, 0.06, 0.15, 0.5]), (N, 8, 1, 1))
    x = np.where(low, rng.integers(0, 256, (N, 8, 16, W)), rng.integers(64, 256, (N, 8, 16, W)))
    c = rng.integers(0, W, (N, 8, L, 16)); o = rng.integers(0, W, (N, 8, L, P))
    d = np.where(rng.random((N, 8, 1, L)) < 0.5, rng.integers(1, 49, (N, 8, 16, L)), rng.integers(1, 256, (N, 8, 16, L)))
    return x, c, o, d, rng.integers(0, 16, (N, 8, 16, 1))
def pack(x, c, o, d, w):
    return {"xt": np.ascontiguousarray(x.reshape(N, 128, W)).astype(np.float32).astype(BF), "pk": np.stack([gtable(a.reshape(8, -1)) for a in c]), "po": np.stack([gtable(a.reshape(8, -1)) for a in o]),
            "dm": np.ascontiguousarray(d.reshape(N, 128, L)).astype(np.int32), "wt": np.ascontiguousarray(w.reshape(N, 128, 1)).astype(np.int32)}
def setup_inputs(rng):
    return pack(*parts(rng))
def setup_inputs_ties(rng):
    x, c, o, d, w = parts(rng)
    v = rng.integers(8, 200, (N, 8, 16, 1))
    x = v + np.where(rng.random((N, 8, 1, W)) < 0.75, rng.integers(-1, 2, (N, 8, 1, W)), rng.integers(-1, 2, (N, 8, 16, W)))
    d = v + rng.integers(-1, 2, (N, 8, 16, L))
    few = rng.integers(0, W, 8); few[0] = 0; few[7] = W - 1
    c[:, 1::2] = few[rng.integers(0, 8, (N, 4, L, 16))]; o[:, 1::2] = few[rng.integers(0, 8, (N, 4, L, P))]
    return pack(x, c, o, d, w)
def setup_inputs_corners(rng):
    x, c, o, d, w = parts(rng)
    d = rng.choice(np.array([1, 2, 4, 5, 6, 8, 9, 10, 128, 246, 247, 248, 251, 252, 255]), (N, 8, 16, L))
    d[:, :, :, :8] = 1; d[:, :, :, L - 8:] = 255
    x[:, 0] = x[:, 0, :, :1]
    c[:, 1] = c[:, 1, :, :1]; o[:, 1] = o[:, 1, :, :1]
    o[:, 2] = np.concatenate([c[:, 2, :, ::-1]] * (P // 16), axis=2)
    w[:, 3] = 0; w[:, 4] = 15; w[:, 5] = 0; w[:, 5, 15] = rng.integers(1, 16, (N, 1))
    x[:, 6] = 255 * rng.integers(0, 2, (N, 1, W))
    x[:, 7] = rng.integers(0, 256, (N, 16, W)); c[:, 7] = (W - 1) * rng.integers(0, 2, (N, L, 16)); o[:, 7] = (W - 1) * rng.integers(0, 2, (N, L, P))
    q = int(rng.integers(0, N)); x[q] = x[q, :, :, :1]
    return pack(x, c, o, d, w)
def setup_inputs_ends(rng):
    kind = rng.integers(0, 4, (N, 8, 1, W)); hole = rng.integers(0, 16, (N, 8, 1, W))
    x = np.where(kind == 0, 0, np.where(kind == 1, 1, np.where(kind == 2, rng.integers(0, 2, (N, 8, 16, W)), np.arange(16).reshape(16, 1) != hole)))
    w = rng.integers(0, 2, (N, 8, 16, 1)); w[:, 6] = 0; w[:, 7] = 1; w = 15 * w
    kd = rng.integers(0, 4, (N, 8, 1, L)); d = np.where(kd == 0, 0, np.where(kd == 1, 1, rng.integers(0, 2, (N, 8, 16, L))))
    d[:, :, :, L - 1] = 1; d[:, :, :, L - 2] = 0; d = 1 + 254 * d
    c = (W - 1) * rng.integers(0, 2, (N, 8, L, 16)); o = (W - 1) * rng.integers(0, 2, (N, 8, L, P))
    c[:, :, L - 2:] = 0; c[:, :, L - 2:, 15] = W - 1; c[:, :, L - 1, 2] = W - 1
    o[:, :, L - 2:] = W - 1; o[:, :, L - 2:, P - 1] = 0; o[:, :, L - 1, 1] = 0
    c[0, :, :, 7] = W - 1; o[0, :, :, P - 1] = 0; c[0, 3, 5] = 0
    c[N - 1, :, :, 15] = W - 1; o[N - 1, :, :, P - 1] = 0
    m = rng.random((8, L, 1)) < 0.5; c[1] = np.where(m, 0, W - 1); o[1] = np.where(m, o[1], W - 1)
    e = np.add.reduce(w * d, axis=2) & 1023
    p = place(np.full((N, 8, L, 1), W - 1), e, 0)[..., 0]
    tail = int(np.argmax(place(np.arange(W)[None, :], np.zeros(1, np.int64), 0)[0]))
    for q in (0, 1, N - 1):
        for g in range(8): x[q, g][:, p[q, g]] = 1
        x[q, :, :, 0] = 0
    for q in (0, N - 1):
        c[q, 6, L - 2:, 15] = tail; x[q, 6, :, W - 1] = 1
    return pack(255 * x, c, o, d, w)
def setup_inputs_lull(rng):
    x, c, o, d, w = parts(rng)
    q = int(rng.integers(0, N)); p = (q - 1) % N
    x[q] = np.maximum(x[q], 1); x[:, :, :, :32] = 255; x[p, :, :, :32] = 0; x[q, :, :, :32] = 0
    c[p] = 0; o[q, :, :, P - 2:] = 0; o[q] = rng.permuted(o[q], axis=2)
    still = rng.permutation(8 * L)[:int(rng.integers(1, 32))]; c[q, still // L, still % L] = 0
    return pack(x, c, o, d, w)
def setup_inputs_spread(rng):
    x = np.minimum((np.exp2(8 * rng.random((N, 8, 1, W))) * (0.5 + 0.5 * rng.random((N, 8, 16, W)))).astype(np.int64), 255) * (rng.random((N, 8, 1, W)) > 0.0625)
    c = np.minimum((W * rng.random((N, 8, L, 16)) ** 4).astype(np.int64), W - 1); o = np.minimum((W * rng.random((N, 8, L, P)) ** 4).astype(np.int64), W - 1)
    d = np.minimum(np.maximum(np.exp2(8 * rng.random((N, 8, 16, L))).astype(np.int64), 1), 255)
    w = rng.integers(0, 16, (N, 8, 16, 1)) * (rng.random((N, 8, 16, 1)) < 0.4)
    return pack(x, c, o, d, w)
def check_inputs(d):
    bad = []
    for k, lo, hi in (("xt", 0, 255), ("pk", 0, W - 1), ("po", 0, W - 1), ("dm", 1, 255), ("wt", 0, 15)):
        v = np.asarray(d[k]).astype(np.float64)
        if not np.all((v >= lo) & (v <= hi) & (v == np.floor(v))): bad.append("range of " + k)
    return bad
def picks(x, z, e, kap):
    return np.take(x, place(z, e, kap) + (W * np.arange(8 * N)).reshape(N, 8, 1, 1), axis=0)
def reference(xt, pk, po, dm, wt):
    x = np.ascontiguousarray(xt.astype(np.float32).astype(np.int32).reshape(8 * N, 16, W).transpose(0, 2, 1)).reshape(-1, 16)
    c = np.stack([gentries(a) for a in pk]).astype(np.int64).reshape(N, 8, L, 16)
    o = np.stack([gentries(a) for a in po]).astype(np.int64).reshape(N, 8, L, P)
    D = np.ascontiguousarray(dm.astype(np.int32).reshape(N, 8, 16, L).transpose(0, 1, 3, 2))
    w = wt.astype(np.int32).reshape(N, 8, 1, 16)
    kap = np.zeros((N, 1, 1, 1), np.int64); left = []
    for t in range(T):
        if t > 0: c = np.roll(c, 1, axis=0)
        e = (np.add.reduce(w * D, axis=3) & 1023).astype(np.int64)
        a = picks(x, c, e, kap); b = picks(x, o, e, kap)
        if t >= N:
            m = left[t - N]; y = picks(x, m, e, kap); gone = (m != c)[..., None]
            up = np.max(np.where(gone, -1, a), axis=3) >= np.max(np.where(gone, y, -1), axis=3)
            D = np.minimum(np.maximum(np.where(up, D + 8, D - 8), 1), 255)
        sa = np.add.reduce(np.minimum(a, D[:, :, :, None, :]), axis=4); sb = np.add.reduce(np.minimum(b, D[:, :, :, None, :]), axis=4)
        k = np.argmax(sa, axis=3)[..., None]; j = np.argmin(sb, axis=3)[..., None]
        swap = np.take_along_axis(sa, k, 3) > np.take_along_axis(sb, j, 3)
        ck = np.take_along_axis(c, k, 3); oj = np.take_along_axis(o, j, 3)
        np.put_along_axis(c, k, np.where(swap, oj, ck), 3); np.put_along_axis(o, j, np.where(swap, ck, oj), 3)
        xk = np.take_along_axis(a, k[..., None], 3)[:, :, :, 0]
        D = np.where(swap & (xk >= D), np.maximum(D - 4, 1), D)
        kap = np.add.reduce(swap.reshape(N, -1).astype(np.int64), axis=1).reshape(N, 1, 1, 1) & 31
        left.append(c)
    return {"yc": np.stack([gtable(v.reshape(8, -1)) for v in c]).astype(np.float32), "yo": np.stack([gtable(v.reshape(8, -1)) for v in o]).astype(np.float32),
            "yd": np.ascontiguousarray(D.transpose(0, 1, 3, 2)).reshape(N, 128, L).astype(np.float32)}

@@ -1,0 +1,561 @@
+from concourse.bass import DstId, RemoteDMATransfer
+from concourse.mybir import dt, AluOpType, AxisListType, ActivationFunctionType
+
+OP = AluOpType
+AF = ActivationFunctionType
+NV = 6
+ZC = 2080
+TW = 2096
+
+SCRATCH = {
+    "pk_i": ("sbuf", [128, 128], "int32"), "po_i": ("sbuf", [128, 256], "int32"),
+    "dm_i": ("sbuf", [128, 128], "int32"), "wt_i": ("sbuf", [128, 1], "int32"),
+    "tab": ("sbuf", [128, TW], "bfloat16"),
+    "ic": ("sbuf", [128, 240], "float32"), "i8": ("sbuf", [128, 128], "float32"),
+    "iperm": ("sbuf", [128, 128], "float32"), "ipermf": ("sbuf", [128, 128], "float32"),
+    "ienc": ("sbuf", [128, 128], "float32"), "ip": ("sbuf", [128, 1], "int32"),
+    "pint": ("sbuf", [128, 4], "int32"), "pf": ("sbuf", [128, 4], "float32"),
+    "prev": ("sbuf", [128, 1], "float32"), "pcol": ("sbuf", [128, 1], "float32"),
+    "eye16": ("sbuf", [128, 128], "float16"), "meye16": ("sbuf", [128, 128], "float16"),
+    "r16": ("sbuf", [128, 128], "float16"), "perm16": ("sbuf", [128, 128], "float16"),
+    "permf16": ("sbuf", [128, 128], "float16"),
+    "zb": ("sbuf", [128, 240], "float16"), "zfp": ("sbuf", [128, 240], "float16"),
+    "zfo": ("sbuf", [128, 240], "float16"), "enc16": ("sbuf", [128, 128], "float16"),
+    "mb": ("sbuf", [128, 8], "float32"), "mf": ("sbuf", [128, 8], "float32"),
+    "bc": ("sbuf", [128, 4], "uint16"),
+    "eyeb": ("sbuf", [128, 128], "bfloat16"), "m4eye": ("sbuf", [128, 128], "bfloat16"),
+    "ones": ("sbuf", [128, 128], "bfloat16"), "onesn": ("sbuf", [128, 128], "bfloat16"),
+    "cpool": ("sbuf", [128, 256], "bfloat16"),
+    "sel": ("sbuf", [128, 2048], "bfloat16"), "wsel": ("sbuf", [128, 2048], "bfloat16"),
+    "wcol": ("sbuf", [128, 1], "float32"),
+    "pk16": ("sbuf", [128, 128], "float16"), "poa16": ("sbuf", [128, 128], "float16"),
+    "pob16": ("sbuf", [128, 128], "float16"),
+    "q0": ("sbuf", [128, 128], "float16"), "q1": ("sbuf", [128, 128], "float16"),
+    "q2": ("sbuf", [128, 128], "float16"),
+    "rw0": ("sbuf", [128, 1024], "float16"), "rw1": ("sbuf", [128, 1024], "float16"),
+    "rw2": ("sbuf", [128, 1024], "float16"),
+    "o16": ("sbuf", [128, 256], "float16"),
+    "dt_": ("sbuf", [128, 128], "bfloat16"), "dt2": ("sbuf", [128, 256], "bfloat16"),
+    "e1": ("sbuf", [128, 8], "int32"), "e2": ("sbuf", [128, 8], "int32"),
+    "e33": ("sbuf", [128, 64], "float32"),
+    "kf": ("sbuf", [128, 1], "float32"), "kr": ("sbuf", [128, 1], "int32"),
+    "cnt": ("sbuf", [128, 1], "float32"), "cscr": ("sbuf", [128, 8], "float32"),
+    "oq": ("sbuf", [128, 256], "int32"), "of": ("sbuf", [128, 256], "int32"), "ou": ("sbuf", [128, 256], "uint16"),
+    "pq": ("sbuf", [128, 128], "int32"), "pfc": ("sbuf", [128, 128], "int32"), "pu": ("sbuf", [128, 128], "uint16"),
+    "xo": ("sbuf", [128, 4096], "bfloat16"), "yo_": ("sbuf", [128, 4096], "bfloat16"),
+    "xp": ("sbuf", [128, 2048], "bfloat16"), "yp": ("sbuf", [128, 2080], "bfloat16"),
+    "losb": ("sbuf", [128, 64], "float32"), "w64": ("sbuf", [128, 64], "float32"),
+    "w32": ("sbuf", [128, 32], "float32"), "w16": ("sbuf", [128, 16], "float32"), "m1": ("sbuf", [128, 8], "float32"),
+    "sohi": ("sbuf", [128, 128], "float32"), "p128": ("sbuf", [128, 128], "float32"),
+    "p64": ("sbuf", [128, 64], "float32"), "p32": ("sbuf", [128, 32], "float32"),
+    "p16": ("sbuf", [128, 16], "float32"), "omin": ("sbuf", [128, 8], "float32"),
+    "thi": ("sbuf", [128, 8], "int32"), "offi": ("sbuf", [128, 8], "int32"), "offu": ("sbuf", [128, 8], "uint16"),
+    "thf": ("sbuf", [128, 8], "float32"), "th2": ("sbuf", [128, 8], "float32"),
+    "thr": ("sbuf", [128, 64], "float32"), "thr2": ("sbuf", [128, 64], "float32"),
+    "swp": ("sbuf", [128, 8], "bfloat16"), "gt": ("sbuf", [128, 128], "bfloat16"),
+    "ohc": ("sbuf", [128, 128], "bfloat16"), "oho": ("sbuf", [128, 256], "bfloat16"),
+    "cm": ("sbuf", [128, 128], "float16"), "om": ("sbuf", [128, 256], "float16"),
+    "tc16": ("sbuf", [128, 128], "float16"), "to16": ("sbuf", [128, 256 * NV], "float16"),
+    "oend": ("sbuf", [128, 256], "float16"),
+    "mu": ("sbuf", [128, 128], "uint16"), "mz": ("sbuf", [128, 128], "float32"),
+    "stay": ("sbuf", [128, 128], "float32"), "sz": ("sbuf", [128, 128], "float32"),
+    "au": ("sbuf", [128, 128], "uint16"),
+    "acc0": ("sbuf", [128, 256], "bfloat16"), "acc1": ("sbuf", [128, 256], "bfloat16"),
+    "amax": ("sbuf", [128, 128], "bfloat16"), "bmax": ("sbuf", [128, 128], "bfloat16"),
+    "up": ("sbuf", [128, 128], "bfloat16"), "up8": ("sbuf", [128, 128], "bfloat16"),
+    "dsum": ("sbuf", [128, 128], "float32"),
+    "yc_f": ("sbuf", [128, 128], "float32"), "yo_f": ("sbuf", [128, 256], "float32"),
+    "yd_f": ("sbuf", [128, 128], "float32"),
+}
+for _t in range(NV):
+    SCRATCH["c%d" % _t] = ("sbuf", [128, 128], "float16")
+    SCRATCH["n%d" % _t] = ("sbuf", [128, 128], "float16")
+for _b in range(8):
+    SCRATCH["b%d" % _b] = ("psum", [128, 512], "float32")
+
+LOADS = ["ld_pk", "ld_po", "ld_dm", "ld_wt", "ld_xt"]
+STORES = ["st_yc", "st_yo", "st_yd"]
+SEMAPHORES = ["sv", "sa", "sp", "sg", "loc"] + LOADS + STORES + ["arr%d" % t for t in range(1, NV)]
+
+
+def rank_program(g, core, T, topo):
+    rank = T.rank_of(core)
+    if rank is None:
+        return
+    nxt = T.cores[(rank + 1) % len(T.cores)]
+    prv = T.cores[(rank - 1) % len(T.cores)]
+    NENG = 8
+
+    queues = {"V": g.vector, "A": g.scalar, "P": g.tensor, "G": g, "Y": g.sync}
+    sems = {"V": "sv", "A": "sa", "P": "sp", "G": "sg"}
+    count = {"V": 0, "A": 0, "P": 0, "G": 0}
+    waited = {e: {} for e in queues}
+    lastw, readers, bankacc = {}, {}, {}
+
+    def need(eng, tok):
+        s, n = tok
+        if waited[eng].get(s, 0) < n:
+            queues[eng].wait_ge(T.sem[s], n)
+            waited[eng][s] = n
+
+    def order(eng, reads, writes):
+        own = sems.get(eng)
+        toks = {}
+
+        def add(tok):
+            if tok[1] > toks.get(tok[0], 0):
+                toks[tok[0]] = tok[1]
+        for k in reads:
+            if k in lastw:
+                add(lastw[k])
+        for k in writes:
+            if k in lastw and lastw[k][0] != own:
+                add(lastw[k])
+            for s, n in readers.get(k, {}).items():
+                if s != own:
+                    add((s, n))
+        for k in reads + writes:
+            if k[0] == "B":
+                for s, n in bankacc.get(k[:2], {}).items():
+                    if s != own:
+                        add((s, n))
+        for s in toks:
+            need(eng, (s, toks[s]))
+
+    def done(tok, reads, writes):
+        for k in reads:
+            readers.setdefault(k, {})[tok[0]] = tok[1]
+        for k in writes:
+            lastw[k] = tok
+            readers[k] = {}
+        for k in reads + writes:
+            if k[0] == "B":
+                bankacc.setdefault(k[:2], {})[tok[0]] = tok[1]
+
+    def do(eng, call, reads, writes):
+        order(eng, reads, writes)
+        count[eng] += 1
+        call().then_inc(T.sem[sems[eng]], 1)
+        done((sems[eng], count[eng]), reads, writes)
+
+    v, a_, pe = g.vector, g.scalar, g.tensor
+
+    def tt(out, x, y, op, r, w):
+        do("V", lambda: v.tensor_tensor(out, x, y, op), r, w)
+
+    def ts(out, x, s1, s2, op0, op1, r, w):
+        if op1 is None:
+            do("V", lambda: v.tensor_scalar(out, x, s1, None, op0), r, w)
+        else:
+            do("V", lambda: v.tensor_scalar(out, x, s1, s2, op0, op1), r, w)
+
+    def cp(out, x, r, w):
+        do("V", lambda: v.tensor_copy(out, x), r, w)
+
+    def fill(ap, c, w):
+        do("V", lambda: v.memset(ap, c), [], w)
+
+    def act(out, x, r, w, acc=None):
+        do("A", lambda: a_.activation(out, x, AF.Copy, accum_out=acc), r, w)
+
+    def mm(out, l, x, st, sp, r, w):
+        do("P", lambda: pe.matmul(out, l, x, st, sp), r, w)
+
+    def load(eng, sem, out, x, w):
+        queues[eng].dma_start(out, x).then_inc(T.sem[sem], 16)
+        lastw[w] = (sem, 16)
+
+    def store(eng, sem, out, x, r):
+        order(eng, r, [])
+        queues[eng].dma_start(out, x).then_inc(T.sem[sem], 16)
+
+    load("Y", "ld_pk", T.pk_i[:], T.pk[:], "pk_i")
+    load("A", "ld_po", T.po_i[:], T.po[:], "po_i")
+    load("Y", "ld_dm", T.dm_i[:], T.dm[:], "dm_i")
+    load("A", "ld_wt", T.wt_i[:], T.wt[:], "wt_i")
+    load("Y", "ld_xt", T.tab[:, 0:2048], T.xt[:], "tab")
+
+    def iota(out, pat, base, cm, w, small=True):
+        if small:
+            do("G", lambda: g.iota(out, pat, base, cm, allow_small_or_imprecise_dtypes=True), [], w)
+        else:
+            do("G", lambda: g.iota(out, pat, base, cm), [], w)
+    iota(T.ip[:], [[0, 1]], 0, 1, ["ip"], False)
+    iota(T.i8[:], [[0, 16], [1, 8]], 0, 0, ["i8"])
+    iota(T.ic[:], [[1, 240]], -112, 0, ["ic"])
+    iota(T.iperm[:], [[16, 8], [-1, 16]], 15, 0, ["iperm"])
+    iota(T.ienc[:], [[128, 16], [16, 8]], 0, 0, ["ienc"])
+    iota(T.cpool[:], [[2, 32], [0, 8]], 0, 0, ["cpool1"])
+    iota(T.ipermf[:], [[1, 16], [16, 8]], 0, 0, ["ipermf"])
+
+    fill(T.wsel[:], 0.0, ["wsel"])
+    for j, (op, s) in enumerate([(OP.bitwise_and, 15), (OP.bitwise_and, 7),
+                                 (OP.arith_shift_right, 4), (OP.arith_shift_right, 3)]):
+        ts(T.pint[:, j:j + 1], T.ip[:], s, None, op, None, ["ip"], ["pint"])
+    cp(T.pcol[:], T.ip[:], ["ip"], ["pcol"])
+    cp(T.pf[:], T.pint[:], ["pint"], ["pf"])
+    ic0 = T.ic[:, 112:240]
+    P16, P8, D16, D8 = (T.pf[:, j:j + 1] for j in range(4))
+    ts(T.mb[:], T.i8[:, 0:8], D16, None, OP.is_equal, None, ["i8", "pf"], ["mb"])
+    ts(T.zb[:], T.ic[:], P16, None, OP.is_equal, None, ["ic", "pf"], ["zb"])
+    ts(T.eyeb[:], ic0, T.pcol[:], None, OP.is_equal, None, ["ic", "pcol"], ["eyeb"])
+    ts(T.eye16[:], ic0, T.pcol[:], None, OP.is_equal, None, ["ic", "pcol"], ["eye16"])
+    ts(T.bc[:], T.i8[:, 0:4], 0.0, P8, OP.mult, OP.add, ["i8", "pf"], ["bc"])
+    ts(T.perm16[:], T.iperm[:], T.pcol[:], None, OP.is_equal, None, ["iperm", "pcol"], ["perm16"])
+    cp(T.pk16[:], T.pk_i[:], ["pk_i"], ["pk16"])
+    mm(T.b6[:, 0:128], T.pk16[:], T.perm16[:], True, True, ["pk16", "perm16"], ["B6.q0"])
+    cp(T.dt_[:], T.dm_i[:], ["dm_i"], ["dt"])
+    ts(T.wcol[:], T.wt_i[:], 2.0, None, OP.mult, None, ["wt_i"], ["wcol"])
+    ts(T.wsel[:, 0:2048:16], T.i8[:], D16, T.wcol[:], OP.is_equal, OP.mult, ["i8", "pf", "wcol", "wsel"], ["wsel"])
+
+    def seats_e():
+        for a in range(16):
+            mm(T.b7[:, 128:136], T.wsel[:, 127 * a:127 * a + 128], T.dt_[:, a:128:16], a == 0, a == 15,
+               ["wsel", "dt"], ["B7.e"])
+
+    def spread_d():
+        for i in range(4):
+            mm(T.b5[:, 128 * i:128 * i + 128], T.eyeb[:], T.dt_[:], True, True, ["eyeb", "dt"], ["B5.d"])
+        act(T.dt2[:], T.b5[:, 0:256], ["B5.d"], ["dt2"])
+
+    def e_one():
+        cp(T.e1[:], T.b7[:, 128:136], ["B7.e"], ["e1"])
+
+    def e_two():
+        ts(T.e2[:], T.e1[:], 2046, None, OP.bitwise_and, None, ["e1"], ["e2"])
+
+    def e_three():
+        ts(T.e33[:], T.e2[:, 0:8].indirect(T.bc[:, 0:4]), 1.0, 33.0, OP.mult, OP.add, ["e2", "bc"], ["e33"])
+        act(T.b7[:, 144:208], T.e33[:], ["e33"], ["B7.e33"])
+
+    seats_e()
+    Q = [T.q0, T.q1, T.q2]
+    RW = [T.rw0, T.rw1, T.rw2]
+
+    def lanes_to_seats(i, src, out, w):
+        cp(Q[i][:], src[0], [src[1]], ["q%d" % i])
+        for b in range(8):
+            ts(RW[i][:, b:1024:8], Q[i][:], T.mb[:, b:b + 1], None, OP.mult, None, ["q%d" % i, "mb"], ["rw%d" % i])
+        for h in range(8):
+            mm(out, T.zb[:, 112 - 16 * h:240 - 16 * h], RW[i][:, 128 * h:128 * h + 128], h == 0, h == 7,
+               ["zb", "rw%d" % i], [w])
+    lanes_to_seats(0, (T.b6[:, 0:128], "B6.q0"), T.b4[:, 0:128], "B4.c")
+    e_one()
+    fill(T.kf[:], 0.0, ["kf"])
+    e_two()
+    fill(T.tab[:, 2080:TW], 0.0, ["tabz"])
+    e_three()
+    act(T.tab[:, 2048:2080], T.tab[:, 0:32], ["tab"], ["tabx"])
+    spread_d()
+    cp(T.c0[:], T.b4[:, 0:128], ["B4.c"], ["c0"])
+
+    tabk = ["tab", "tabx", "tabz"]
+    win = T.tab[:, 0:TW]
+
+    def index(cards, ck, esrc, ek, qb, fb, outs, n0, n1, nm):
+        for c in range(n0, n1, 64):
+            tt(qb[:, c:c + 64], cards[:, c:c + 64], esrc, OP.mult, [ck, ek], [nm + "q"])
+        ts(fb[:, n0:n1], qb[:, n0:n1], 5, 2047, OP.arith_shift_right, OP.bitwise_and, [nm + "q"], [nm + "f"])
+        for out, z, key in outs:
+            if z is None:
+                ts(out[:, n0:n1], fb[:, n0:n1], T.kf[:], None, OP.add, None, [nm + "f", "kf"], [key])
+            else:
+                ts(out[:, n0:n1], fb[:, n0:n1], T.kf[:], z, OP.add, OP.add, [nm + "f", "kf"], [key])
+
+    def pool_index(c0, c1):
+        index(T.b3, "B3.o", T.e33[:], "e33", T.oq, T.of, [(T.ou, None, "ou%d" % c0)], 64 * c0, 64 * c1, "o%d" % c0)
+
+    def pack_index(t, h):
+        index(T["c%d" % t], "c%d" % t, T.b7[:, 144:208], "B7.e33", T.pq, T.pfc, [(T.pu, None, "pu%d" % h)],
+              64 * h, 64 * h + 64, "p%d" % h)
+
+    def ouk(c):
+        return "ou0" if c == 0 else "ou1"
+
+    def s_gather(dst, off, okey, lo, hi, key):
+        act(dst[:, lo:hi], win.indirect(off[:, lo // 16:hi // 16]), tabk + [okey], [key + "%d" % lo])
+
+    def v_fused(dst, off, okey, lo, hi, key):
+        tt(dst[:, lo:hi], win.indirect(off[:, lo // 16:hi // 16]), T.dt2[:, 0:hi - lo], OP.min,
+           tabk + [okey, "dt2"], [key])
+
+    def v_min(dst, src, skey, lo, hi, key):
+        tt(dst[:, lo:hi], src[:, lo:hi], T.b5[:, 0:hi - lo], OP.min, [skey + "%d" % lo, "B5.d"], [key])
+
+    def pool_scores(c):
+        out = T.b0[:, 64 * c:64 * c + 64]
+        mm(out, T.onesn[:], T.cpool[:, 64 * c:64 * c + 64], True, False, ["onesn", "cpool0", "cpool1"], ["B0.s"])
+        for a in range(16):
+            mm(out, T.sel[:, 127 * a:127 * a + 128], T.yo_[:, 1024 * c + a:1024 * (c + 1):16], False, a == 15,
+               ["sel", "yo%d" % c], ["B0.s"])
+
+    def pack_scores(h):
+        out = (T.b1, T.b2)[h][:, 0:64]
+        key = "B%d.s" % (1 + h)
+        mm(out, T.eye16[:], T.enc16[:, 64 * h:64 * h + 64], True, False, ["eye16", "enc16"], [key])
+        for a in range(16):
+            mm(out, T.sel[:, 127 * a:127 * a + 128], T.yp[:, 1024 * h + a:1024 * (h + 1):16], False, a == 15,
+               ["sel", "yp%d" % h], [key])
+        if h == 0:
+            act(T.losb[:], T.b1[:, 0:64], ["B1.s"], ["losb"])
+
+    SP = [(0, 384), (384, 768)]
+    FU = (768, 1024)
+
+    def pool_min():
+        tt(T.p128[:], T.b0[:, 0:128], T.sohi[:], OP.min, ["B0.s", "sohi"], ["p128"])
+        tt(T.p64[:], T.p128[:, 0:64], T.p128[:, 64:128], OP.min, ["p128"], ["p64"])
+        tt(T.p32[:], T.p64[:, 0:32], T.p64[:, 32:64], OP.min, ["p64"], ["p32"])
+        tt(T.p16[:], T.p32[:, 0:16], T.p32[:, 16:32], OP.min, ["p32"], ["p16"])
+        tt(T.omin[:], T.p16[:, 0:8], T.p16[:, 8:16], OP.min, ["p16"], ["omin"])
+
+    def pool_s(c):
+        for lo, hi in SP:
+            s_gather(T.xo, T.ou, ouk(c), 1024 * c + lo, 1024 * c + hi, "xo")
+
+    def pool_f(c):
+        v_fused(T.yo_, T.ou, ouk(c), 1024 * c + FU[0], 1024 * c + FU[1], "yo%d" % c)
+
+    def pool_m(c):
+        for lo, hi in SP:
+            v_min(T.yo_, T.xo, "xo", 1024 * c + lo, 1024 * c + hi, "yo%d" % c)
+        pool_scores(c)
+
+    def pack_s(h):
+        for lo, hi in SP:
+            s_gather(T.xp, T.pu, "pu%d" % h, 1024 * h + lo, 1024 * h + hi, "xp")
+
+    def pack_f(h):
+        v_fused(T.yp, T.pu, "pu%d" % h, 1024 * h + FU[0], 1024 * h + FU[1], "yp%d" % h)
+
+    def pack_m(h, part):
+        lo, hi = SP[part]
+        v_min(T.yp, T.xp, "xp", 1024 * h + lo, 1024 * h + hi, "yp%d" % h)
+
+    def pool_copy():
+        act(T.sohi[:], T.b0[:, 128:256], ["B0.s"], ["sohi"])
+
+    def pack_to_psum(t):
+        mm(T.b4[:, 0:128], T.eye16[:], T["c%d" % t][:], True, True, ["eye16", "c%d" % t], ["B4.c"])
+
+    def exchange(t):
+        last = t == NV - 1
+        tt(T.w64[:], T.b2[:, 0:64], T.losb[:], OP.max, ["B2.s", "losb"], ["w64"])
+        tt(T.w32[:], T.w64[:, 0:32], T.w64[:, 32:64], OP.max, ["w64"], ["w32"])
+        tt(T.w16[:], T.w32[:, 0:16], T.w32[:, 16:32], OP.max, ["w32"], ["w16"])
+        tt(T.m1[:], T.w16[:, 0:8], T.w16[:, 8:16], OP.max, ["w16"], ["m1"])
+        tt(T.thi[:], T.m1[:], T.omin[:], OP.max, ["m1", "omin"], ["thi"])
+        tt(T.thf[:], T.m1[:], T.omin[:], OP.max, ["m1", "omin"], ["thf"])
+        ts(T.offi[:], T.thi[:], 4095, None, OP.bitwise_and, None, ["thi"], ["offi"])
+        tt(T.th2[:], T.m1[:], T.omin[:], OP.min, ["m1", "omin"], ["th2"])
+        cp(T.offu[:], T.offi[:], ["offi"], ["offu"])
+        if not last:
+            tt(T.swp[:], T.m1[:], T.omin[:], OP.is_gt, ["m1", "omin"], ["swp"])
+        act(T.thr[:], T.thf[:, 0:8].indirect(T.bc[:, 0:4]), ["thf", "bc"], ["thr"])
+        act(T.thr2[:], T.th2[:, 0:8].indirect(T.bc[:, 0:4]), ["th2", "bc"], ["thr2"])
+        tt(T.gt[:], T.yp[:, 0:2080].indirect(T.offu[:, 0:8]), T.dt_[:], OP.is_ge,
+           ["yp0", "yp1", "ypz", "offu", "dt"], ["gt"])
+        mm(T.b7[:, 0:128], T.eyeb[:], T.dt_[:], True, False, ["eyeb", "dt"], ["B7.d"])
+        mm(T.b7[:, 0:128], T.m4eye[:], T.gt[:], False, True, ["m4eye", "gt"], ["B7.d"])
+        tt(T.ohc[:, 0:64], T.b1[:, 0:64], T.thr[:], OP.is_ge, ["B1.s", "thr"], ["ohc"])
+        tt(T.ohc[:, 64:128], T.b2[:, 0:64], T.thr[:], OP.is_ge, ["B2.s", "thr"], ["ohc"])
+        ts(T.dt_[:], T.b7[:, 0:128], 1.0, None, OP.max, None, ["B7.d"], ["dt"])
+        if not last:
+            mm(T.b6[:, 384:392], T.ones[:], T.swp[:], True, True, ["ones", "swp"], ["B6.k"])
+            act(T.cscr[:], T.b6[:, 384:392], ["B6.k"], ["cnt", "cscr"], T.cnt[:])
+            seats_e()
+        else:
+            act(T.yd_f[:], T.dt_[:], ["dt"], ["yd_f"])
+            store("Y", "st_yd", T.yd[:], T.yd_f[:], ["yd_f"])
+        for c in range(4):
+            tt(T.oho[:, 64 * c:64 * c + 64], T.b0[:, 64 * c:64 * c + 64], T.thr2[:], OP.is_le, ["B0.s", "thr2"], ["oho"])
+        tt(T.cm[:], T.ohc[:], T.b4[:, 0:128], OP.mult, ["ohc", "B4.c"], ["cm"])
+        tt(T.om[:], T.oho[:], T.b3[:, 0:256], OP.mult, ["oho", "B3.o"], ["om"])
+        mm(T.b6[:, 0:128], T.cm[:], T.meye16[:], True, False, ["cm", "meye16"], ["B6.t"])
+        mm(T.b6[:, 0:128], T.om[:, 0:128], T.eye16[:], False, False, ["om", "eye16"], ["B6.t"])
+        mm(T.b6[:, 0:128], T.om[:, 128:256], T.eye16[:], False, True, ["om", "eye16"], ["B6.t"])
+        if not last:
+            spread_d()
+            ts(T.kr[:], T.cnt[:], 0.03125, -0.484375, OP.mult, OP.add, ["cnt"], ["kr"])
+            e_one()
+            ts(T.kf[:], T.kr[:], -32.0, T.cnt[:], OP.mult, OP.add, ["kr", "cnt"], ["kf"])
+            e_two()
+        cp(T.tc16[:], T.b6[:, 0:128], ["B6.t"], ["tc16"])
+        mm(T.b6[:, 128:256], T.tc16[:], T.r16[:], True, True, ["tc16", "r16"], ["B6.d"])
+        mm(T.b3[:, 0:256], T.eye16[:], T.o16[:], True, False, ["eye16", "o16"], ["B3.o"])
+        for u in range(t):
+            mm(T.b3[:, 0:256], T.meye16[:], T.to16[:, 256 * u:256 * u + 256], False, False, ["meye16", "to%d" % u],
+               ["B3.o"])
+        if not last:
+            e_three()
+        tt(T.b4[:, 128:256], T.ohc[:], T.b6[:, 128:256], OP.mult, ["ohc", "B6.d"], ["B4.t"])
+        tt(T["n%d" % t][:], T["c%d" % t][:], T.b4[:, 128:256], OP.add, ["c%d" % t, "B4.t"], ["n%d" % t])
+        if not last:
+            order("G", ["n%d" % t], [])
+            rid, pid, _ = topo.addr(nxt)
+            m = 0
+            for en in topo.engines(core, nxt)[:NENG]:
+                m |= 1 << en
+            g.remote_dma(T["c%d" % (t + 1)][:], T["n%d" % t][:], T.sem["arr%d" % (t + 1)], T.sem.loc, pid, rid, m)
+            lastw["c%d" % (t + 1)] = ("arr%d" % (t + 1), NENG)
+        for h in range(2):
+            tt(T.to16[:, 256 * t + 128 * h:256 * t + 128 * h + 128], T.oho[:, 128 * h:128 * h + 128], T.b6[:, 128:256],
+               OP.mult, ["oho", "B6.d"], ["to%d" % t])
+        mm(T.b3[:, 0:256], T.meye16[:], T.to16[:, 256 * t:256 * t + 256], False, True, ["meye16", "to%d" % t], ["B3.o"])
+
+    pack_index(0, 0)
+    pack_s(0)
+    pack_index(0, 1)
+    pack_s(1)
+    cp(T.poa16[:], T.po_i[:, 0:256:2], ["po_i"], ["poa16"])
+    cp(T.pob16[:], T.po_i[:, 1:256:2], ["po_i"], ["pob16"])
+    mm(T.b6[:, 128:256], T.poa16[:], T.eye16[:], True, True, ["poa16", "eye16"], ["B6.q1"])
+    mm(T.b6[:, 256:384], T.pob16[:], T.eye16[:], True, True, ["pob16", "eye16"], ["B6.q2"])
+    lanes_to_seats(1, (T.b6[:, 128:256], "B6.q1"), T.b7[:, 256:384], "B7.o1")
+    lanes_to_seats(2, (T.b6[:, 256:384], "B6.q2"), T.b7[:, 384:512], "B7.o2")
+    fill(T.sel[:], 0.0, ["sel"])
+    cp(T.o16[:], T.b7[:, 256:512], ["B7.o1", "B7.o2"], ["o16"])
+    mm(T.b3[:, 0:256], T.eye16[:], T.o16[:], True, True, ["eye16", "o16"], ["B3.o"])
+    ts(T.sel[:, 0:2048:16], T.i8[:], D16, 4096.0, OP.is_equal, OP.mult, ["i8", "pf", "sel"], ["sel"])
+    ts(T.enc16[:], T.ienc[:], P16, None, OP.add, None, ["ienc", "pf"], ["enc16"])
+    pool_index(0, 1)
+    pool_s(0)
+    pool_index(1, 4)
+    for c in range(1, 4):
+        pool_s(c)
+    pack_f(0)
+    pack_m(0, 0)
+    pack_m(0, 1)
+    pack_scores(0)
+    pack_f(1)
+    pack_m(1, 0)
+    pack_m(1, 1)
+    pack_scores(1)
+    fill(T.onesn[:], 0.0078125, ["onesn"])
+    fill(T.cpool[0:64, :], 4096.0, ["cpool0", "cpool1"])
+    fill(T.yp[:, 2048:2080], 0.0, ["ypz"])
+    fill(T.ones[:], 1.0, ["ones"])
+    for c in range(4):
+        pool_f(c)
+        if c == 0:
+            ts(T.meye16[:], ic0, T.pcol[:], -1.0, OP.is_equal, OP.mult, ["ic", "pcol"], ["meye16"])
+            ts(T.m4eye[:], ic0, T.pcol[:], -4.0, OP.is_equal, OP.mult, ["ic", "pcol"], ["m4eye"])
+            ts(T.r16[:], T.i8[:], P8, None, OP.is_equal, None, ["i8", "pf"], ["r16"])
+        pool_m(c)
+    pool_copy()
+    pool_min()
+    exchange(0)
+
+    for t in range(1, NV - 1):
+        pool_index(0, 1)
+        pool_s(0)
+        pool_index(1, 4)
+        for c in range(1, 4):
+            pool_s(c)
+        pack_to_psum(t)
+        for c in range(3):
+            pool_f(c)
+            pool_m(c)
+        pool_f(3)
+        pack_index(t, 0)
+        pack_s(0)
+        pack_index(t, 1)
+        pool_m(3)
+        pack_f(0)
+        pack_m(0, 0)
+        pack_f(1)
+        pack_m(0, 1)
+        pool_copy()
+        pack_s(1)
+        pool_min()
+        pack_scores(0)
+        pack_m(1, 0)
+        pack_m(1, 1)
+        pack_scores(1)
+        exchange(t)
+
+    t = NV - 1
+    HALF = [(i, i + 512) for i in range(0, 4096, 512)]
+    QUAR = [(i, i + 256) for i in range(0, 2048, 256)]
+
+    def chain(off, okey, out, key):
+        acc = [T.acc0, T.acc1]
+        for i, (lo, hi) in enumerate(QUAR):
+            src = win.indirect(off[:, lo // 16:hi // 16])
+            if i == 0:
+                cp(acc[0][:], src, tabk + [okey], ["acc0"])
+            else:
+                tt(acc[i % 2][:], src, acc[(i + 1) % 2][:], OP.max, tabk + [okey, "acc%d" % ((i + 1) % 2)],
+                   ["acc%d" % (i % 2)])
+        tt(out[:], acc[1][:, 0:128], acc[1][:, 128:256], OP.max, ["acc1"], [key])
+
+    pool_index(0, 1)
+    for lo, hi in HALF[0:2]:
+        s_gather(T.xo, T.ou, "ou0", lo, hi, "xo")
+    pool_index(1, 4)
+    for lo, hi in HALF[2:]:
+        s_gather(T.xo, T.ou, "ou1", lo, hi, "xo")
+    index(T.n0, "n0", T.b7[:, 144:208], "B7.e33", T.pq, T.pfc, [(T.mu, None, "mu"), (T.mz, -float(ZC), "mz")], 0, 128, "m")
+    chain(T.mu, "mu", T.bmax, "bmax")
+    ts(T.permf16[:], T.ipermf[:], T.pcol[:], None, OP.is_equal, None, ["ipermf", "pcol"], ["permf16"])
+    ts(T.prev[:], D8, -1.0, 15.0, OP.mult, OP.add, ["pf"], ["prev"])
+    ts(T.mf[:], T.i8[:, 0:8], P8, None, OP.is_equal, None, ["i8", "pf"], ["mf"])
+    ts(T.zfo[:], T.ic[:], D8, None, OP.is_equal, None, ["ic", "pf"], ["zfo"])
+    ts(T.zfp[:], T.ic[:], T.prev[:], None, OP.is_equal, None, ["ic", "prev"], ["zfp"])
+    pack_to_psum(t)
+    pack_index(t, 0)
+    for lo, hi in HALF[0:2]:
+        s_gather(T.xp, T.pu, "pu0", lo, hi, "xp")
+    pack_index(t, 1)
+    for lo, hi in HALF[2:4]:
+        s_gather(T.xp, T.pu, "pu1", lo, hi, "xp")
+    tt(T.stay[:], T.n0[:], T["c%d" % t][:], OP.is_equal, ["n0", "c%d" % t], ["stay"])
+    tt(T.sz[:], T.stay[:], T.mz[:], OP.mult, ["stay", "mz"], ["sz"])
+    ts(T.au[:], T.sz[:], float(ZC), None, OP.add, None, ["sz"], ["au"])
+    chain(T.au, "au", T.amax, "amax")
+    tt(T.up[:], T.amax[:], T.bmax[:], OP.is_ge, ["amax", "bmax"], ["up"])
+    ts(T.up8[:], T.up[:], 16.0, -8.0, OP.mult, OP.add, ["up"], ["up8"])
+    tt(T.dsum[:], T.dt_[:], T.up8[:], OP.add, ["dt", "up8"], ["dsum"])
+    ts(T.dt_[:], T.dsum[:], 1.0, 255.0, OP.max, OP.min, ["dsum"], ["dt"])
+    for i in range(4):
+        mm(T.b5[:, 128 * i:128 * i + 128], T.eyeb[:], T.dt_[:], True, True, ["eyeb", "dt"], ["B5.d"])
+    for c in range(4):
+        for lo, hi in HALF[2 * c:2 * c + 2]:
+            v_min(T.yo_, T.xo, "xo", lo, hi, "yo%d" % c)
+        pool_scores(c)
+    for lo, hi in HALF[0:2]:
+        v_min(T.yp, T.xp, "xp", lo, hi, "yp0")
+    pool_copy()
+    pack_scores(0)
+    pool_min()
+    for lo, hi in HALF[2:4]:
+        v_min(T.yp, T.xp, "xp", lo, hi, "yp1")
+    pack_scores(1)
+    exchange(t)
+
+    def seats_to_list(i, src, skey, z, zk, tcol, out, key):
+        mm(T.b7[:, tcol:tcol + 128], src, T.permf16[:], True, True, [skey, "permf16"], ["B7.f%d" % i])
+        cp(Q[i][:], T.b7[:, tcol:tcol + 128], ["B7.f%d" % i], ["q%d" % i])
+        for b in range(8):
+            ts(RW[i][:, 128 * b:128 * b + 128], Q[i][:], T.mf[:, b:b + 1], None, OP.mult, None,
+               ["q%d" % i, "mf"], ["rw%d" % i])
+        for h in range(8):
+            mm(out, z[:, 112 - 16 * h:240 - 16 * h], RW[i][:, h:1024:8], h == 0, h == 7, ["rw%d" % i, zk], [key])
+
+    seats_to_list(0, T["n%d" % t][:], "n%d" % t, T.zfp, "zfp", 0, T.b0[:, 0:128], "B0.y")
+    act(T.yc_f[:], T.b0[:, 0:128], ["B0.y"], ["yc_f"])
+    store("Y", "st_yc", T.yc[:], T.yc_f[:], ["yc_f"])
+    cp(T.oend[:], T.b3[:, 0:256], ["B3.o"], ["oend"])
+    seats_to_list(1, T.oend[:, 0:128], "oend", T.zfo, "zfo", 128, T.b1[:, 0:128], "B1.y")
+    act(T.yo_f[:, 0:256:2], T.b1[:, 0:128], ["B1.y"], ["yo_f"])
+    seats_to_list(2, T.oend[:, 128:256], "oend", T.zfo, "zfo", 256, T.b2[:, 0:128], "B2.y")
+    act(T.yo_f[:, 1:256:2], T.b2[:, 0:128], ["B2.y"], ["yo_f"])
+    store("Y", "st_yo", T.yo[:], T.yo_f[:], ["yo_f"])
+
+    for e in sems:
+        need("G", (sems[e], count[e]))
+    for s in LOADS + STORES:
+        need("G", (s, 16))
+    need("G", ("loc", NENG * (NV - 1)))
+    for k in range(1, NV):
+        need("G", ("arr%d" % k, NENG))

@@ -34,7 +34,7 @@ SCRATCH = {
     "q2": ("sbuf", [128, 128], "float16"),
     "rw0": ("sbuf", [128, 1024], "float16"), "rw1": ("sbuf", [128, 1024], "float16"),
     "rw2": ("sbuf", [128, 1024], "float16"),
-    "o16": ("sbuf", [128, 256], "float16"),
+    "o16": ("sbuf", [128, 512], "float16"),
     "dt_": ("sbuf", [128, 128], "bfloat16"), "dt2": ("sbuf", [128, 256], "bfloat16"),
     "e1": ("sbuf", [128, 8], "int32"), "e2": ("sbuf", [128, 8], "int32"),
     "e33": ("sbuf", [128, 64], "float32"),
@@ -55,8 +55,8 @@ SCRATCH = {
     "swp": ("sbuf", [128, 8], "bfloat16"), "gt": ("sbuf", [128, 128], "bfloat16"),
     "ohc": ("sbuf", [128, 128], "bfloat16"), "oho": ("sbuf", [128, 256], "bfloat16"),
     "cm": ("sbuf", [128, 128], "float16"), "om": ("sbuf", [128, 256], "float16"),
-    "tc16": ("sbuf", [128, 128], "float16"), "to16": ("sbuf", [128, 256 * NV], "float16"),
-    "oend": ("sbuf", [128, 256], "float16"),
+    "tc16": ("sbuf", [128, 128], "float16"),
+
     "mu": ("sbuf", [128, 128], "uint16"), "mz": ("sbuf", [128, 128], "float32"),
     "stay": ("sbuf", [128, 128], "float32"), "sz": ("sbuf", [128, 128], "float32"),
     "au": ("sbuf", [128, 128], "uint16"),
@@ -208,8 +208,8 @@ def rank_program(g, core, T, topo):
     ts(T.wcol[:], T.wt_i[:], 2.0, None, OP.mult, None, ["wt_i"], ["wcol"])
     ts(T.wsel[:, 0:2048:16], T.i8[:], D16, T.wcol[:], OP.is_equal, OP.mult, ["i8", "pf", "wcol", "wsel"], ["wsel"])
 
-    def seats_e():
-        for a in range(16):
+    def seats_e(a0=0, a1=16):
+        for a in range(a0, a1):
             mm(T.b7[:, 128:136], T.wsel[:, 127 * a:127 * a + 128], T.dt_[:, a:128:16], a == 0, a == 15,
                ["wsel", "dt"], ["B7.e"])
 
@@ -255,19 +255,35 @@ def rank_program(g, core, T, topo):
     def index(cards, ck, esrc, ek, qb, fb, outs, n0, n1, nm):
         for c in range(n0, n1, 64):
             tt(qb[:, c:c + 64], cards[:, c:c + 64], esrc, OP.mult, [ck, ek], [nm + "q"])
+        yield
         ts(fb[:, n0:n1], qb[:, n0:n1], 5, 2047, OP.arith_shift_right, OP.bitwise_and, [nm + "q"], [nm + "f"])
+        yield
         for out, z, key in outs:
             if z is None:
                 ts(out[:, n0:n1], fb[:, n0:n1], T.kf[:], None, OP.add, None, [nm + "f", "kf"], [key])
             else:
                 ts(out[:, n0:n1], fb[:, n0:n1], T.kf[:], z, OP.add, OP.add, [nm + "f", "kf"], [key])
+        yield
 
-    def pool_index(c0, c1):
-        index(T.b3, "B3.o", T.e33[:], "e33", T.oq, T.of, [(T.ou, None, "ou%d" % c0)], 64 * c0, 64 * c1, "o%d" % c0)
+    def ocards(t):
+        return T.o16[:, 256 * (t % 2):256 * (t % 2) + 256], "o16.%d" % (t % 2)
 
-    def pack_index(t, h):
-        index(T["c%d" % t], "c%d" % t, T.b7[:, 144:208], "B7.e33", T.pq, T.pfc, [(T.pu, None, "pu%d" % h)],
-              64 * h, 64 * h + 64, "p%d" % h)
+    def pool_index(t):
+        o, ok = ocards(t)
+        e, ek = T.b7[:, 144:208], "B7.e33"
+        x = index(o, ok, e, ek, T.oq, T.of, [(T.ou, None, "ou0")], 0, 64, "o0")
+        y = index(o, ok, e, ek, T.oq, T.of, [(T.ou, None, "ou1")], 64, 256, "o1")
+        for z in (x, y, x, x, y, y):
+            next(z)
+
+    def pack_index(t, between=()):
+        parts = [index(T["c%d" % t], "c%d" % t, T.b7[:, 144:208], "B7.e33", T.pq, T.pfc, [(T.pu, None, "pu%d" % h)],
+                       64 * h, 64 * h + 64, "p%d" % h) for h in range(2)]
+        for i in range(3):
+            for x in parts:
+                next(x)
+            if between:
+                between[i]()
 
     def ouk(c):
         return "ou0" if c == 0 else "ou1"
@@ -338,12 +354,16 @@ def rank_program(g, core, T, topo):
     def pack_to_psum(t):
         mm(T.b4[:, 0:128], T.eye16[:], T["c%d" % t][:], True, True, ["eye16", "c%d" % t], ["B4.c"])
 
-    def exchange(t):
-        last = t == NV - 1
+    def pack_max():
         tt(T.w64[:], T.b2[:, 0:64], T.losb[:], OP.max, ["B2.s", "losb"], ["w64"])
         tt(T.w32[:], T.w64[:, 0:32], T.w64[:, 32:64], OP.max, ["w64"], ["w32"])
         tt(T.w16[:], T.w32[:, 0:16], T.w32[:, 16:32], OP.max, ["w32"], ["w16"])
         tt(T.m1[:], T.w16[:, 0:8], T.w16[:, 8:16], OP.max, ["w16"], ["m1"])
+
+    ESPLIT = 8
+
+    def exchange(t):
+        last = t == NV - 1
         tt(T.thi[:], T.m1[:], T.omin[:], OP.max, ["m1", "omin"], ["thi"])
         tt(T.thf[:], T.m1[:], T.omin[:], OP.max, ["m1", "omin"], ["thf"])
         ts(T.offi[:], T.thi[:], 4095, None, OP.bitwise_and, None, ["thi"], ["offi"])
@@ -359,38 +379,46 @@ def rank_program(g, core, T, topo):
         mm(T.b7[:, 0:128], T.m4eye[:], T.gt[:], False, True, ["m4eye", "gt"], ["B7.d"])
         tt(T.ohc[:, 0:64], T.b1[:, 0:64], T.thr[:], OP.is_ge, ["B1.s", "thr"], ["ohc"])
         tt(T.ohc[:, 64:128], T.b2[:, 0:64], T.thr[:], OP.is_ge, ["B2.s", "thr"], ["ohc"])
+        for c in range(4):
+            tt(T.oho[:, 64 * c:64 * c + 64], T.b0[:, 64 * c:64 * c + 64], T.thr2[:], OP.is_le, ["B0.s", "thr2"], ["oho"])
         ts(T.dt_[:], T.b7[:, 0:128], 1.0, None, OP.max, None, ["B7.d"], ["dt"])
         if not last:
             mm(T.b6[:, 384:392], T.ones[:], T.swp[:], True, True, ["ones", "swp"], ["B6.k"])
             act(T.cscr[:], T.b6[:, 384:392], ["B6.k"], ["cnt", "cscr"], T.cnt[:])
-            seats_e()
+            seats_e(0, ESPLIT)
         else:
             act(T.yd_f[:], T.dt_[:], ["dt"], ["yd_f"])
             store("Y", "st_yd", T.yd[:], T.yd_f[:], ["yd_f"])
-        for c in range(4):
-            tt(T.oho[:, 64 * c:64 * c + 64], T.b0[:, 64 * c:64 * c + 64], T.thr2[:], OP.is_le, ["B0.s", "thr2"], ["oho"])
         tt(T.cm[:], T.ohc[:], T.b4[:, 0:128], OP.mult, ["ohc", "B4.c"], ["cm"])
         tt(T.om[:], T.oho[:], T.b3[:, 0:256], OP.mult, ["oho", "B3.o"], ["om"])
         mm(T.b6[:, 0:128], T.cm[:], T.meye16[:], True, False, ["cm", "meye16"], ["B6.t"])
         mm(T.b6[:, 0:128], T.om[:, 0:128], T.eye16[:], False, False, ["om", "eye16"], ["B6.t"])
         mm(T.b6[:, 0:128], T.om[:, 128:256], T.eye16[:], False, True, ["om", "eye16"], ["B6.t"])
         if not last:
-            spread_d()
+            seats_e(ESPLIT, 16)
             ts(T.kr[:], T.cnt[:], 0.03125, -0.484375, OP.mult, OP.add, ["cnt"], ["kr"])
-            e_one()
-            ts(T.kf[:], T.kr[:], -32.0, T.cnt[:], OP.mult, OP.add, ["kr", "cnt"], ["kf"])
-            e_two()
         cp(T.tc16[:], T.b6[:, 0:128], ["B6.t"], ["tc16"])
         mm(T.b6[:, 128:256], T.tc16[:], T.r16[:], True, True, ["tc16", "r16"], ["B6.d"])
-        mm(T.b3[:, 0:256], T.eye16[:], T.o16[:], True, False, ["eye16", "o16"], ["B3.o"])
-        for u in range(t):
-            mm(T.b3[:, 0:256], T.meye16[:], T.to16[:, 256 * u:256 * u + 256], False, False, ["meye16", "to%d" % u],
-               ["B3.o"])
+        if not last:
+            ts(T.kf[:], T.kr[:], -32.0, T.cnt[:], OP.mult, OP.add, ["kr", "cnt"], ["kf"])
+            e_one()
+        o, ok = ocards(t)
+        on, onk = ocards(t + 1)
+        tt(T.b4[:, 128:256], T.ohc[:], T.b6[:, 128:256], OP.mult, ["ohc", "B6.d"], ["B4.t"])
+        tt(T.b4[:, 256:384], T.oho[:, 0:128], T.b6[:, 128:256], OP.mult, ["oho", "B6.d"], ["B4.u"])
+        tt(T["n%d" % t][:], T["c%d" % t][:], T.b4[:, 128:256], OP.add, ["c%d" % t, "B4.t"], ["n%d" % t])
+        tt(T.b4[:, 384:512], T.oho[:, 128:256], T.b6[:, 128:256], OP.mult, ["oho", "B6.d"], ["B4.v"])
+        if last:
+            to_lanes(0, T["n%d" % t][:], "n%d" % t)
+        if not last:
+            e_two()
+        tt(on[:, 0:128], o[:, 0:128], T.b4[:, 256:384], OP.subtract, [ok, "B4.u"], [onk])
         if not last:
             e_three()
-        tt(T.b4[:, 128:256], T.ohc[:], T.b6[:, 128:256], OP.mult, ["ohc", "B6.d"], ["B4.t"])
-        tt(T["n%d" % t][:], T["c%d" % t][:], T.b4[:, 128:256], OP.add, ["c%d" % t, "B4.t"], ["n%d" % t])
+            spread_d()
+        tt(on[:, 128:256], o[:, 128:256], T.b4[:, 384:512], OP.subtract, [ok, "B4.v"], [onk])
         if not last:
+            mm(T.b3[:, 0:256], T.eye16[:], on, True, True, ["eye16", onk], ["B3.o"])
             order("G", ["n%d" % t], [])
             rid, pid, _ = topo.addr(nxt)
             m = 0
@@ -398,14 +426,14 @@ def rank_program(g, core, T, topo):
                 m |= 1 << en
             g.remote_dma(T["c%d" % (t + 1)][:], T["n%d" % t][:], T.sem["arr%d" % (t + 1)], T.sem.loc, pid, rid, m)
             lastw["c%d" % (t + 1)] = ("arr%d" % (t + 1), NENG)
-        for h in range(2):
-            tt(T.to16[:, 256 * t + 128 * h:256 * t + 128 * h + 128], T.oho[:, 128 * h:128 * h + 128], T.b6[:, 128:256],
-               OP.mult, ["oho", "B6.d"], ["to%d" % t])
-        mm(T.b3[:, 0:256], T.meye16[:], T.to16[:, 256 * t:256 * t + 256], False, True, ["meye16", "to%d" % t], ["B3.o"])
 
-    pack_index(0, 0)
+    def to_lanes(i, src, skey):
+        out = (T.b7, T.b1, T.b2)[i][:, 256:384]
+        mm(out, src, T.permf16[:], True, True, [skey, "permf16"], ["B%d.f" % (7, 1, 2)[i]])
+        return out, "B%d.f" % (7, 1, 2)[i]
+
+    pack_index(0)
     pack_s(0)
-    pack_index(0, 1)
     pack_s(1)
     cp(T.poa16[:], T.po_i[:, 0:256:2], ["po_i"], ["poa16"])
     cp(T.pob16[:], T.po_i[:, 1:256:2], ["po_i"], ["pob16"])
@@ -413,16 +441,14 @@ def rank_program(g, core, T, topo):
     mm(T.b6[:, 256:384], T.pob16[:], T.eye16[:], True, True, ["pob16", "eye16"], ["B6.q2"])
     lanes_to_seats(1, (T.b6[:, 128:256], "B6.q1"), T.b7[:, 256:384], "B7.o1")
     lanes_to_seats(2, (T.b6[:, 256:384], "B6.q2"), T.b7[:, 384:512], "B7.o2")
+    cp(T.o16[:, 0:256], T.b7[:, 256:512], ["B7.o1", "B7.o2"], ["o16.0"])
+    mm(T.b3[:, 0:256], T.eye16[:], T.o16[:, 0:256], True, True, ["eye16", "o16.0"], ["B3.o"])
+    pool_index(0)
+    for c in range(4):
+        pool_s(c)
     fill(T.sel[:], 0.0, ["sel"])
-    cp(T.o16[:], T.b7[:, 256:512], ["B7.o1", "B7.o2"], ["o16"])
-    mm(T.b3[:, 0:256], T.eye16[:], T.o16[:], True, True, ["eye16", "o16"], ["B3.o"])
     ts(T.sel[:, 0:2048:16], T.i8[:], D16, 4096.0, OP.is_equal, OP.mult, ["i8", "pf", "sel"], ["sel"])
     ts(T.enc16[:], T.ienc[:], P16, None, OP.add, None, ["ienc", "pf"], ["enc16"])
-    pool_index(0, 1)
-    pool_s(0)
-    pool_index(1, 4)
-    for c in range(1, 4):
-        pool_s(c)
     pack_f(0)
     pack_m(0, 0)
     pack_m(0, 1)
@@ -443,35 +469,34 @@ def rank_program(g, core, T, topo):
             ts(T.r16[:], T.i8[:], P8, None, OP.is_equal, None, ["i8", "pf"], ["r16"])
         pool_m(c)
     pool_copy()
+    pack_max()
     pool_min()
     exchange(0)
 
     for t in range(1, NV - 1):
-        pool_index(0, 1)
-        pool_s(0)
-        pool_index(1, 4)
-        for c in range(1, 4):
+        pool_index(t)
+        for c in range(4):
             pool_s(c)
         pack_to_psum(t)
         for c in range(3):
             pool_f(c)
             pool_m(c)
         pool_f(3)
-        pack_index(t, 0)
+        pack_index(t)
         pack_s(0)
-        pack_index(t, 1)
+        pack_s(1)
         pool_m(3)
         pack_f(0)
         pack_m(0, 0)
         pack_f(1)
         pack_m(0, 1)
         pool_copy()
-        pack_s(1)
-        pool_min()
         pack_scores(0)
         pack_m(1, 0)
         pack_m(1, 1)
         pack_scores(1)
+        pool_min()
+        pack_max()
         exchange(t)
 
     t = NV - 1
@@ -489,13 +514,11 @@ def rank_program(g, core, T, topo):
                    ["acc%d" % (i % 2)])
         tt(out[:], acc[1][:, 0:128], acc[1][:, 128:256], OP.max, ["acc1"], [key])
 
-    pool_index(0, 1)
-    for lo, hi in HALF[0:2]:
-        s_gather(T.xo, T.ou, "ou0", lo, hi, "xo")
-    pool_index(1, 4)
-    for lo, hi in HALF[2:]:
-        s_gather(T.xo, T.ou, "ou1", lo, hi, "xo")
-    index(T.n0, "n0", T.b7[:, 144:208], "B7.e33", T.pq, T.pfc, [(T.mu, None, "mu"), (T.mz, -float(ZC), "mz")], 0, 128, "m")
+    pool_index(t)
+    for i, (lo, hi) in enumerate(HALF):
+        s_gather(T.xo, T.ou, ouk(i // 2), lo, hi, "xo")
+    for x in index(T.n0, "n0", T.b7[:, 144:208], "B7.e33", T.pq, T.pfc, [(T.mu, None, "mu"), (T.mz, -float(ZC), "mz")], 0, 128, "m"):
+        pass
     chain(T.mu, "mu", T.bmax, "bmax")
     ts(T.permf16[:], T.ipermf[:], T.pcol[:], None, OP.is_equal, None, ["ipermf", "pcol"], ["permf16"])
     ts(T.prev[:], D8, -1.0, 15.0, OP.mult, OP.add, ["pf"], ["prev"])
@@ -503,15 +526,12 @@ def rank_program(g, core, T, topo):
     ts(T.zfo[:], T.ic[:], D8, None, OP.is_equal, None, ["ic", "pf"], ["zfo"])
     ts(T.zfp[:], T.ic[:], T.prev[:], None, OP.is_equal, None, ["ic", "prev"], ["zfp"])
     pack_to_psum(t)
-    pack_index(t, 0)
-    for lo, hi in HALF[0:2]:
-        s_gather(T.xp, T.pu, "pu0", lo, hi, "xp")
-    pack_index(t, 1)
-    for lo, hi in HALF[2:4]:
-        s_gather(T.xp, T.pu, "pu1", lo, hi, "xp")
-    tt(T.stay[:], T.n0[:], T["c%d" % t][:], OP.is_equal, ["n0", "c%d" % t], ["stay"])
-    tt(T.sz[:], T.stay[:], T.mz[:], OP.mult, ["stay", "mz"], ["sz"])
-    ts(T.au[:], T.sz[:], float(ZC), None, OP.add, None, ["sz"], ["au"])
+    pack_index(t, [
+        lambda: tt(T.stay[:], T.n0[:], T.b4[:, 0:128], OP.is_equal, ["n0", "B4.c"], ["stay"]),
+        lambda: tt(T.sz[:], T.stay[:], T.mz[:], OP.mult, ["stay", "mz"], ["sz"]),
+        lambda: ts(T.au[:], T.sz[:], float(ZC), None, OP.add, None, ["sz"], ["au"])])
+    for i, (lo, hi) in enumerate(HALF[0:4]):
+        s_gather(T.xp, T.pu, "pu%d" % (i // 2), lo, hi, "xp")
     chain(T.au, "au", T.amax, "amax")
     tt(T.up[:], T.amax[:], T.bmax[:], OP.is_ge, ["amax", "bmax"], ["up"])
     ts(T.up8[:], T.up[:], 16.0, -8.0, OP.mult, OP.add, ["up"], ["up8"])
@@ -527,29 +547,32 @@ def rank_program(g, core, T, topo):
         v_min(T.yp, T.xp, "xp", lo, hi, "yp0")
     pool_copy()
     pack_scores(0)
-    pool_min()
     for lo, hi in HALF[2:4]:
         v_min(T.yp, T.xp, "xp", lo, hi, "yp1")
     pack_scores(1)
+    pool_min()
+    pack_max()
     exchange(t)
 
-    def seats_to_list(i, src, skey, z, zk, tcol, out, key):
-        mm(T.b7[:, tcol:tcol + 128], src, T.permf16[:], True, True, [skey, "permf16"], ["B7.f%d" % i])
-        cp(Q[i][:], T.b7[:, tcol:tcol + 128], ["B7.f%d" % i], ["q%d" % i])
+    def seats_to_list(i, z, zk, out, key):
+        src, skey = (T.b7, T.b1, T.b2)[i][:, 256:384], "B%d.f" % (7, 1, 2)[i]
+        cp(Q[i][:], src, [skey], ["q%d" % i])
         for b in range(8):
             ts(RW[i][:, 128 * b:128 * b + 128], Q[i][:], T.mf[:, b:b + 1], None, OP.mult, None,
                ["q%d" % i, "mf"], ["rw%d" % i])
         for h in range(8):
             mm(out, z[:, 112 - 16 * h:240 - 16 * h], RW[i][:, h:1024:8], h == 0, h == 7, ["rw%d" % i, zk], [key])
 
-    seats_to_list(0, T["n%d" % t][:], "n%d" % t, T.zfp, "zfp", 0, T.b0[:, 0:128], "B0.y")
+    oe, oek = ocards(NV)
+    to_lanes(1, oe[:, 0:128], oek)
+    to_lanes(2, oe[:, 128:256], oek)
+    seats_to_list(0, T.zfp, "zfp", T.b0[:, 0:128], "B0.y")
     act(T.yc_f[:], T.b0[:, 0:128], ["B0.y"], ["yc_f"])
     store("Y", "st_yc", T.yc[:], T.yc_f[:], ["yc_f"])
-    cp(T.oend[:], T.b3[:, 0:256], ["B3.o"], ["oend"])
-    seats_to_list(1, T.oend[:, 0:128], "oend", T.zfo, "zfo", 128, T.b1[:, 0:128], "B1.y")
-    act(T.yo_f[:, 0:256:2], T.b1[:, 0:128], ["B1.y"], ["yo_f"])
-    seats_to_list(2, T.oend[:, 128:256], "oend", T.zfo, "zfo", 256, T.b2[:, 0:128], "B2.y")
-    act(T.yo_f[:, 1:256:2], T.b2[:, 0:128], ["B2.y"], ["yo_f"])
+    seats_to_list(1, T.zfo, "zfo", T.b3[:, 0:128], "B3.y")
+    act(T.yo_f[:, 0:256:2], T.b3[:, 0:128], ["B3.y"], ["yo_f"])
+    seats_to_list(2, T.zfo, "zfo", T.b5[:, 0:128], "B5.y")
+    act(T.yo_f[:, 1:256:2], T.b5[:, 0:128], ["B5.y"], ["yo_f"])
     store("Y", "st_yo", T.yo[:], T.yo_f[:], ["yo_f"])
 
     for e in sems:

@@ -6,76 +6,61 @@ AF = ActivationFunctionType
 NV = 6
 ZC = 2080
 TW = 2096
+FULL = [(0, 512), (512, 1024)]
+PART = [(0, 512)]
+SHARE = [PART, PART, FULL, PART, FULL, PART]
 
+
+def sb(n, d):
+    return ("sbuf", [128, n], d)
+
+
+F32, B16, F16, I32, U16 = "float32", "bfloat16", "float16", "int32", "uint16"
 SCRATCH = {
-    "pk_i": ("sbuf", [128, 128], "int32"), "po_i": ("sbuf", [128, 256], "int32"),
-    "dm_i": ("sbuf", [128, 128], "int32"), "wt_i": ("sbuf", [128, 1], "int32"),
-    "tab": ("sbuf", [128, TW], "bfloat16"),
-    "ic": ("sbuf", [128, 240], "float32"), "i8": ("sbuf", [128, 128], "float32"),
-    "iperm": ("sbuf", [128, 128], "float32"), "ipermf": ("sbuf", [128, 128], "float32"),
-    "ienc": ("sbuf", [128, 128], "float32"), "ip": ("sbuf", [128, 1], "int32"),
-    "pint": ("sbuf", [128, 4], "int32"), "pf": ("sbuf", [128, 4], "float32"),
-    "prev": ("sbuf", [128, 1], "float32"), "pcol": ("sbuf", [128, 1], "float32"),
-    "eye16": ("sbuf", [128, 128], "float16"), "meye16": ("sbuf", [128, 128], "float16"),
-    "r16": ("sbuf", [128, 128], "float16"), "perm16": ("sbuf", [128, 128], "float16"),
-    "permf16": ("sbuf", [128, 128], "float16"),
-    "zb": ("sbuf", [128, 240], "float16"), "zfp": ("sbuf", [128, 240], "float16"),
-    "zfo": ("sbuf", [128, 240], "float16"), "enc16": ("sbuf", [128, 128], "float16"),
-    "mb": ("sbuf", [128, 8], "float32"), "mf": ("sbuf", [128, 8], "float32"),
-    "bc": ("sbuf", [128, 4], "uint16"),
-    "eyeb": ("sbuf", [128, 128], "bfloat16"), "m4eye": ("sbuf", [128, 128], "bfloat16"),
-    "ones": ("sbuf", [128, 128], "bfloat16"), "onesn": ("sbuf", [128, 128], "bfloat16"),
-    "cpool": ("sbuf", [128, 256], "bfloat16"),
-    "sel": ("sbuf", [128, 2048], "bfloat16"), "wsel": ("sbuf", [128, 2048], "bfloat16"),
-    "wcol": ("sbuf", [128, 1], "float32"),
-    "pk16": ("sbuf", [128, 128], "float16"), "poa16": ("sbuf", [128, 128], "float16"),
-    "pob16": ("sbuf", [128, 128], "float16"),
-    "q0": ("sbuf", [128, 128], "float16"), "q1": ("sbuf", [128, 128], "float16"),
-    "q2": ("sbuf", [128, 128], "float16"),
-    "rw0": ("sbuf", [128, 1024], "float16"), "rw1": ("sbuf", [128, 1024], "float16"),
-    "rw2": ("sbuf", [128, 1024], "float16"),
-    "o16": ("sbuf", [128, 512], "float16"),
-    "dt_": ("sbuf", [128, 128], "bfloat16"), "dt2": ("sbuf", [128, 256], "bfloat16"),
-    "e1": ("sbuf", [128, 8], "int32"), "e2": ("sbuf", [128, 8], "int32"),
-    "e33": ("sbuf", [128, 64], "float32"),
-    "kf": ("sbuf", [128, 1], "float32"), "kr": ("sbuf", [128, 1], "int32"),
-    "cnt": ("sbuf", [128, 1], "float32"), "cscr": ("sbuf", [128, 8], "float32"),
-    "oq": ("sbuf", [128, 256], "int32"), "of": ("sbuf", [128, 256], "int32"), "ou": ("sbuf", [128, 256], "uint16"),
-    "pq": ("sbuf", [128, 128], "int32"), "pfc": ("sbuf", [128, 128], "int32"), "pu": ("sbuf", [128, 128], "uint16"),
-    "xo": ("sbuf", [128, 4096], "bfloat16"), "yo_": ("sbuf", [128, 4096], "bfloat16"),
-    "xp": ("sbuf", [128, 2048], "bfloat16"), "yp": ("sbuf", [128, 2080], "bfloat16"),
-    "losb": ("sbuf", [128, 64], "float32"), "w64": ("sbuf", [128, 64], "float32"),
-    "w32": ("sbuf", [128, 32], "float32"), "w16": ("sbuf", [128, 16], "float32"), "m1": ("sbuf", [128, 8], "float32"),
-    "sohi": ("sbuf", [128, 128], "float32"), "p128": ("sbuf", [128, 128], "float32"),
-    "p64": ("sbuf", [128, 64], "float32"), "p32": ("sbuf", [128, 32], "float32"),
-    "p16": ("sbuf", [128, 16], "float32"), "omin": ("sbuf", [128, 8], "float32"),
-    "thi": ("sbuf", [128, 8], "int32"), "offi": ("sbuf", [128, 8], "int32"), "offu": ("sbuf", [128, 8], "uint16"),
-    "thf": ("sbuf", [128, 8], "float32"), "th2": ("sbuf", [128, 8], "float32"),
-    "thr": ("sbuf", [128, 64], "float32"), "thr2": ("sbuf", [128, 64], "float32"),
-    "swp": ("sbuf", [128, 8], "bfloat16"), "gt": ("sbuf", [128, 128], "bfloat16"),
-    "ohc": ("sbuf", [128, 128], "bfloat16"), "oho": ("sbuf", [128, 256], "bfloat16"),
-    "cm": ("sbuf", [128, 128], "float16"), "om": ("sbuf", [128, 256], "float16"),
-    "tc16": ("sbuf", [128, 128], "float16"),
-
-    "mu": ("sbuf", [128, 128], "uint16"), "mz": ("sbuf", [128, 128], "float32"),
-    "stay": ("sbuf", [128, 128], "float32"), "sz": ("sbuf", [128, 128], "float32"),
-    "au": ("sbuf", [128, 128], "uint16"),
-    "acc0": ("sbuf", [128, 256], "bfloat16"), "acc1": ("sbuf", [128, 256], "bfloat16"),
-    "amax": ("sbuf", [128, 128], "bfloat16"), "bmax": ("sbuf", [128, 128], "bfloat16"),
-    "up": ("sbuf", [128, 128], "bfloat16"), "up8": ("sbuf", [128, 128], "bfloat16"),
-    "dsum": ("sbuf", [128, 128], "float32"),
-    "yc_f": ("sbuf", [128, 128], "float32"), "yo_f": ("sbuf", [128, 256], "float32"),
-    "yd_f": ("sbuf", [128, 128], "float32"),
+    "pk_i": sb(128, I32), "po_i": sb(256, I32), "dm_i": sb(128, I32), "wt_i": sb(1, I32), "tab": sb(TW, B16),
+    "ic": sb(240, F32), "i8": sb(128, F32), "iperm": sb(128, F32), "ipermf": sb(128, F32), "ienc": sb(128, F32),
+    "ip": sb(1, I32), "pint": sb(4, I32), "pf": sb(4, F32), "pcol": sb(1, F32), "prev": sb(1, F32),
+    "eye16": sb(128, F16), "meye16": sb(128, F16), "r384": sb(384, F16), "perm16": sb(128, F16),
+    "permf16": sb(128, F16), "zb": sb(240, F16), "zfp": sb(240, F16), "zfo": sb(240, F16),
+    "enc16": sb(128, F16), "cpool": sb(256, B16), "onesn": sb(128, B16), "mb": sb(8, F32), "mf": sb(8, F32),
+    "bc": sb(8, U16), "eyeb": sb(128, B16), "m4eye": sb(128, B16), "ones": sb(128, B16),
+    "sel": sb(2048, B16), "wsel": sb(2048, B16), "wcol": sb(1, F32),
+    "pk16": sb(128, F16), "poa16": sb(128, F16), "pob16": sb(128, F16),
+    "q3": sb(384, F16), "rw3": sb(3072, F16), "ya": sb(2048, B16), "yb": sb(2048, B16),
+    "o16": sb(512, F16), "dt_": sb(128, B16), "dt2": sb(512, B16),
+    "e1": sb(8, I32), "e2": sb(8, I32), "e33": sb(64, F32),
+    "kf": sb(1, F32), "kr": sb(1, I32), "cnt": sb(1, F32), "cscr": sb(128, F32),
+    "oq": sb(256, I32), "of": sb(256, I32), "ou": sb(256, U16),
+    "pq": sb(128, I32), "pfc": sb(128, I32), "pu": sb(128, U16),
+    "xo": sb(4096, B16), "yo_": sb(4096, B16), "xp": sb(2048, B16), "yp": sb(2080, B16),
+    "losb": sb(64, F32), "w64": sb(64, F32), "w32": sb(32, F32), "w16": sb(16, F32), "m1": sb(8, F32),
+    "sohi": sb(128, F32), "p128": sb(128, F32), "p64": sb(64, F32), "p32": sb(32, F32), "p16": sb(16, F32),
+    "omin": sb(8, F32),
+    "thi": sb(8, I32), "offi": sb(8, I32), "offu": sb(8, U16), "thf": sb(8, F32), "th2": sb(8, F32),
+    "thr": sb(128, F32), "thr2": sb(128, F32), "gt": sb(128, B16),
+    "oh": sb(384, B16), "com": sb(384, F16), "tc16": sb(128, F16),
+    "mq": sb(128, I32), "mfc": sb(128, I32), "mu": sb(128, U16), "mz": sb(128, F32),
+    "stay": sb(128, F32), "sz": sb(128, F32), "au": sb(128, U16),
+    "acc0": sb(512, B16), "acc1": sb(512, B16), "acc2": sb(512, B16), "acc3": sb(512, B16),
+    "ah": sb(256, B16), "bh": sb(256, B16), "amax": sb(128, B16), "bmax": sb(128, B16),
+    "up": sb(128, B16), "up8": sb(128, B16), "dsum": sb(128, F32),
+    "yc_f": sb(128, F32), "yo_f": sb(256, F32), "yd_f": sb(128, F32),
 }
 for _t in range(NV):
-    SCRATCH["c%d" % _t] = ("sbuf", [128, 128], "float16")
-    SCRATCH["n%d" % _t] = ("sbuf", [128, 128], "float16")
+    SCRATCH["c%d" % _t] = sb(128, F16)
+    SCRATCH["n%d" % _t] = sb(128, F16)
 for _b in range(8):
-    SCRATCH["b%d" % _b] = ("psum", [128, 512], "float32")
+    SCRATCH["b%d" % _b] = ("psum", [128, 512], F32)
 
 LOADS = ["ld_pk", "ld_po", "ld_dm", "ld_wt", "ld_xt"]
 STORES = ["st_yc", "st_yo", "st_yd"]
-SEMAPHORES = ["sv", "sa", "sp", "sg", "loc"] + LOADS + STORES + ["arr%d" % t for t in range(1, NV)]
+ARR = ["arr%d" % t for t in range(1, NV)]
+SEMAPHORES = ["sv", "sa", "sp", "sg", "loc"] + LOADS + STORES + ARR
+
+CYC, PCYC, CALL, HOP, GATH, WIRE = 0.00091, 0.00079, 0.05, 0.06, 1.5, 3.0
+
+
+EARLY = 4.0
 
 
 def rank_program(g, core, T, topo):
@@ -83,502 +68,452 @@ def rank_program(g, core, T, topo):
     if rank is None:
         return
     nxt = T.cores[(rank + 1) % len(T.cores)]
-    prv = T.cores[(rank - 1) % len(T.cores)]
     NENG = 8
-
     queues = {"V": g.vector, "A": g.scalar, "P": g.tensor, "G": g, "Y": g.sync}
-    sems = {"V": "sv", "A": "sa", "P": "sp", "G": "sg"}
-    count = {"V": 0, "A": 0, "P": 0, "G": 0}
-    waited = {e: {} for e in queues}
-    lastw, readers, bankacc = {}, {}, {}
-
-    def need(eng, tok):
-        s, n = tok
-        if waited[eng].get(s, 0) < n:
-            queues[eng].wait_ge(T.sem[s], n)
-            waited[eng][s] = n
-
-    def order(eng, reads, writes):
-        own = sems.get(eng)
-        toks = {}
-
-        def add(tok):
-            if tok[1] > toks.get(tok[0], 0):
-                toks[tok[0]] = tok[1]
-        for k in reads:
-            if k in lastw:
-                add(lastw[k])
-        for k in writes:
-            if k in lastw and lastw[k][0] != own:
-                add(lastw[k])
-            for s, n in readers.get(k, {}).items():
-                if s != own:
-                    add((s, n))
-        for k in reads + writes:
-            if k[0] == "B":
-                for s, n in bankacc.get(k[:2], {}).items():
-                    if s != own:
-                        add((s, n))
-        for s in toks:
-            need(eng, (s, toks[s]))
-
-    def done(tok, reads, writes):
-        for k in reads:
-            readers.setdefault(k, {})[tok[0]] = tok[1]
-        for k in writes:
-            lastw[k] = tok
-            readers[k] = {}
-        for k in reads + writes:
-            if k[0] == "B":
-                bankacc.setdefault(k[:2], {})[tok[0]] = tok[1]
-
-    def do(eng, call, reads, writes):
-        order(eng, reads, writes)
-        count[eng] += 1
-        call().then_inc(T.sem[sems[eng]], 1)
-        done((sems[eng], count[eng]), reads, writes)
-
+    counters = {"V": "sv", "A": "sa", "P": "sp", "G": "sg"}
     v, a_, pe = g.vector, g.scalar, g.tensor
+    boost, boosts = [0.0], []
+    ops = []
 
-    def tt(out, x, y, op, r, w):
-        do("V", lambda: v.tensor_tensor(out, x, y, op), r, w)
+    def do(eng, call, reads, writes, dur, lat=0.0, tok=None):
+        ops.append((eng, call, reads, writes, dur, lat, tok))
+        boosts.append(boost[0])
 
-    def ts(out, x, s1, s2, op0, op1, r, w):
+    def vec(n):
+        return CALL + max(64, n) * CYC
+
+    def gat(n):
+        return 0.05 + n * GATH * CYC
+
+    def tt(out, x, y, op, r, w, n):
+        do("V", lambda: v.tensor_tensor(out, x, y, op), r, w, vec(n))
+
+    def ttg(out, x, y, op, r, w, n):
+        do("V", lambda: v.tensor_tensor(out, x, y, op), r, w, gat(n))
+
+    def ts(out, x, s1, s2, op0, op1, r, w, n):
         if op1 is None:
-            do("V", lambda: v.tensor_scalar(out, x, s1, None, op0), r, w)
+            do("V", lambda: v.tensor_scalar(out, x, s1, None, op0), r, w, vec(n))
         else:
-            do("V", lambda: v.tensor_scalar(out, x, s1, s2, op0, op1), r, w)
+            do("V", lambda: v.tensor_scalar(out, x, s1, s2, op0, op1), r, w, vec(n))
 
-    def cp(out, x, r, w):
-        do("V", lambda: v.tensor_copy(out, x), r, w)
+    def cp(out, x, r, w, n):
+        do("V", lambda: v.tensor_copy(out, x), r, w, vec(n))
 
-    def fill(ap, c, w):
-        do("V", lambda: v.memset(ap, c), [], w)
+    def fill(ap, c, w, n):
+        do("V", lambda: v.memset(ap, c), [], w, vec(n))
 
-    def act(out, x, r, w, acc=None):
-        do("A", lambda: a_.activation(out, x, AF.Copy, accum_out=acc), r, w)
+    def act(out, x, r, w, n, acc=None, scale=1.0, bias=0.0):
+        do("A", lambda: a_.activation(out, x, AF.Copy, bias=bias, scale=scale, accum_out=acc), r, w, vec(n))
 
-    def mm(out, l, x, st, sp, r, w):
-        do("P", lambda: pe.matmul(out, l, x, st, sp), r, w)
+    def actg(out, x, r, w, n):
+        do("A", lambda: a_.activation(out, x, AF.Copy), r, w, gat(n) + 0.015)
 
-    def load(eng, sem, out, x, w):
-        queues[eng].dma_start(out, x).then_inc(T.sem[sem], 16)
-        lastw[w] = (sem, 16)
+    def mm(out, l, x, st, sp, r, w, n):
+        do("P", lambda: pe.matmul(out, l, x, st, sp), r, w, max(64, n) * PCYC)
+
+    def load(eng, sem, out, x, w, lat):
+        do(eng, lambda: queues[eng].dma_start(out, x).then_inc(T.sem[sem], 16), [], [w], 0.1, lat, (sem, 16))
 
     def store(eng, sem, out, x, r):
-        order(eng, r, [])
-        queues[eng].dma_start(out, x).then_inc(T.sem[sem], 16)
+        do(eng, lambda: queues[eng].dma_start(out, x).then_inc(T.sem[sem], 16), r, [], 0.1, 2.0, (sem, 16))
 
-    load("Y", "ld_pk", T.pk_i[:], T.pk[:], "pk_i")
-    load("A", "ld_po", T.po_i[:], T.po[:], "po_i")
-    load("Y", "ld_dm", T.dm_i[:], T.dm[:], "dm_i")
-    load("A", "ld_wt", T.wt_i[:], T.wt[:], "wt_i")
-    load("Y", "ld_xt", T.tab[:, 0:2048], T.xt[:], "tab")
+    load("Y", "ld_pk", T.pk_i[:], T.pk[:], "pk_i", 2.0)
+    load("A", "ld_po", T.po_i[:], T.po[:], "po_i", 2.3)
+    load("Y", "ld_dm", T.dm_i[:], T.dm[:], "dm_i", 2.0)
+    load("A", "ld_wt", T.wt_i[:], T.wt[:], "wt_i", 2.0)
+    load("Y", "ld_xt", T.tab[:, 0:2048], T.xt[:], "tab", 3.5)
 
-    def iota(out, pat, base, cm, w, small=True):
+    def iota(out, pat, base, cm, w, n, small=True):
         if small:
-            do("G", lambda: g.iota(out, pat, base, cm, allow_small_or_imprecise_dtypes=True), [], w)
+            do("G", lambda: g.iota(out, pat, base, cm, allow_small_or_imprecise_dtypes=True), [], w, 0.13 + 2 * n * CYC)
         else:
-            do("G", lambda: g.iota(out, pat, base, cm), [], w)
-    iota(T.ip[:], [[0, 1]], 0, 1, ["ip"], False)
-    iota(T.i8[:], [[0, 16], [1, 8]], 0, 0, ["i8"])
-    iota(T.ic[:], [[1, 240]], -112, 0, ["ic"])
-    iota(T.iperm[:], [[16, 8], [-1, 16]], 15, 0, ["iperm"])
-    iota(T.ienc[:], [[128, 16], [16, 8]], 0, 0, ["ienc"])
-    iota(T.cpool[:], [[2, 32], [0, 8]], 0, 0, ["cpool1"])
-    iota(T.ipermf[:], [[1, 16], [16, 8]], 0, 0, ["ipermf"])
-
-    fill(T.wsel[:], 0.0, ["wsel"])
+            do("G", lambda: g.iota(out, pat, base, cm), [], w, 0.13 + 2 * n * CYC)
+    iota(T.ip[:], [[0, 1]], 0, 1, ["ip"], 1, False)
+    iota(T.i8[:], [[0, 16], [1, 8]], 0, 0, ["i8"], 128)
+    iota(T.ic[:], [[1, 240]], -112, 0, ["ic"], 240)
+    iota(T.iperm[:], [[16, 8], [-1, 16]], 15, 0, ["iperm"], 128)
+    iota(T.ienc[:], [[128, 16], [16, 8]], 0, 0, ["ienc"], 128)
+    iota(T.cpool[:], [[2, 32], [0, 8]], 0, 0, ["cpool"], 256)
+    iota(T.ipermf[:], [[1, 16], [16, 8]], 0, 0, ["ipermf"], 128)
+    fill(T.wsel[:], 0.0, ["wsel"], 1024)
+    fill(T.kf[:], 0.0, ["kf"], 1)
     for j, (op, s) in enumerate([(OP.bitwise_and, 15), (OP.bitwise_and, 7),
                                  (OP.arith_shift_right, 4), (OP.arith_shift_right, 3)]):
-        ts(T.pint[:, j:j + 1], T.ip[:], s, None, op, None, ["ip"], ["pint"])
-    cp(T.pcol[:], T.ip[:], ["ip"], ["pcol"])
-    cp(T.pf[:], T.pint[:], ["pint"], ["pf"])
+        ts(T.pint[:, j:j + 1], T.ip[:], s, None, op, None, ["ip"], ["pint%d" % j], 1)
+    cp(T.pcol[:], T.ip[:], ["ip"], ["pcol"], 1)
+    cp(T.pf[:], T.pint[:], ["pint%d" % j for j in range(4)], ["pf"], 4)
     ic0 = T.ic[:, 112:240]
     P16, P8, D16, D8 = (T.pf[:, j:j + 1] for j in range(4))
-    ts(T.mb[:], T.i8[:, 0:8], D16, None, OP.is_equal, None, ["i8", "pf"], ["mb"])
-    ts(T.zb[:], T.ic[:], P16, None, OP.is_equal, None, ["ic", "pf"], ["zb"])
-    ts(T.eyeb[:], ic0, T.pcol[:], None, OP.is_equal, None, ["ic", "pcol"], ["eyeb"])
-    ts(T.eye16[:], ic0, T.pcol[:], None, OP.is_equal, None, ["ic", "pcol"], ["eye16"])
-    ts(T.bc[:], T.i8[:, 0:4], 0.0, P8, OP.mult, OP.add, ["i8", "pf"], ["bc"])
-    ts(T.perm16[:], T.iperm[:], T.pcol[:], None, OP.is_equal, None, ["iperm", "pcol"], ["perm16"])
-    cp(T.pk16[:], T.pk_i[:], ["pk_i"], ["pk16"])
-    mm(T.b6[:, 0:128], T.pk16[:], T.perm16[:], True, True, ["pk16", "perm16"], ["B6.q0"])
-    cp(T.dt_[:], T.dm_i[:], ["dm_i"], ["dt"])
-    ts(T.wcol[:], T.wt_i[:], 2.0, None, OP.mult, None, ["wt_i"], ["wcol"])
-    ts(T.wsel[:, 0:2048:16], T.i8[:], D16, T.wcol[:], OP.is_equal, OP.mult, ["i8", "pf", "wcol", "wsel"], ["wsel"])
-
-    def seats_e(a0=0, a1=16):
-        for a in range(a0, a1):
-            mm(T.b7[:, 128:136], T.wsel[:, 127 * a:127 * a + 128], T.dt_[:, a:128:16], a == 0, a == 15,
-               ["wsel", "dt"], ["B7.e"])
-
-    def spread_d():
-        for i in range(4):
-            mm(T.b5[:, 128 * i:128 * i + 128], T.eyeb[:], T.dt_[:], True, True, ["eyeb", "dt"], ["B5.d"])
-        act(T.dt2[:], T.b5[:, 0:256], ["B5.d"], ["dt2"])
-
-    def e_one():
-        cp(T.e1[:], T.b7[:, 128:136], ["B7.e"], ["e1"])
-
-    def e_two():
-        ts(T.e2[:], T.e1[:], 2046, None, OP.bitwise_and, None, ["e1"], ["e2"])
-
-    def e_three():
-        ts(T.e33[:], T.e2[:, 0:8].indirect(T.bc[:, 0:4]), 1.0, 33.0, OP.mult, OP.add, ["e2", "bc"], ["e33"])
-        act(T.b7[:, 144:208], T.e33[:], ["e33"], ["B7.e33"])
-
-    seats_e()
-    Q = [T.q0, T.q1, T.q2]
-    RW = [T.rw0, T.rw1, T.rw2]
-
-    def lanes_to_seats(i, src, out, w):
-        cp(Q[i][:], src[0], [src[1]], ["q%d" % i])
-        for b in range(8):
-            ts(RW[i][:, b:1024:8], Q[i][:], T.mb[:, b:b + 1], None, OP.mult, None, ["q%d" % i, "mb"], ["rw%d" % i])
-        for h in range(8):
-            mm(out, T.zb[:, 112 - 16 * h:240 - 16 * h], RW[i][:, 128 * h:128 * h + 128], h == 0, h == 7,
-               ["zb", "rw%d" % i], [w])
-    lanes_to_seats(0, (T.b6[:, 0:128], "B6.q0"), T.b4[:, 0:128], "B4.c")
-    e_one()
-    fill(T.kf[:], 0.0, ["kf"])
-    e_two()
-    fill(T.tab[:, 2080:TW], 0.0, ["tabz"])
-    e_three()
-    act(T.tab[:, 2048:2080], T.tab[:, 0:32], ["tab"], ["tabx"])
-    spread_d()
-    cp(T.c0[:], T.b4[:, 0:128], ["B4.c"], ["c0"])
-
+    PC, EQ = T.pcol[:], OP.is_equal
+    ts(T.mb[:], T.i8[:, 0:8], D16, None, EQ, None, ["i8", "pf"], ["mb"], 8)
+    ts(T.zb[:], T.ic[:], P16, None, EQ, None, ["ic", "pf"], ["zb"], 240)
+    ts(T.eyeb[:], ic0, PC, None, EQ, None, ["ic", "pcol"], ["eyeb"], 128)
+    ts(T.eye16[:], ic0, PC, None, EQ, None, ["ic", "pcol"], ["eye16"], 128)
+    ts(T.bc[:], T.i8[:, 0:8], 0.0, P8, OP.mult, OP.add, ["i8", "pf"], ["bc"], 8)
+    ts(T.perm16[:], T.iperm[:], PC, None, EQ, None, ["iperm", "pcol"], ["perm16"], 128)
+    selz = ["selz%d" % i for i in range(0, 2048, 240)]
+    for i in range(0, 2048, 240):
+        n = min(240, 2048 - i)
+        act(T.sel[:, i:i + n], T.ic[:, 0:n], ["ic"], ["selz%d" % i], n, None, 0.0)
+    act(T.tab[:, 2080:TW], T.ic[:, 0:16], ["ic"], ["tabz"], 16, None, 0.0)
+    act(T.yp[:, 2048:2080], T.ic[:, 0:32], ["ic"], ["ypz"], 32, None, 0.0)
+    act(T.ones[:], T.ic[:, 0:128], ["ic"], ["ones"], 128, None, 0.0, 1.0)
+    act(T.onesn[:], T.ic[:, 0:128], ["ic"], ["onesn"], 128, None, 0.0, 0.0078125)
+    act(T.cpool[0:64, 0:240], T.ic[0:64, :], ["ic"], ["cpool"], 240, None, 0.0, 4096.0)
+    act(T.cpool[0:64, 240:256], T.ic[0:64, 0:16], ["ic"], ["cpool"], 16, None, 0.0, 4096.0)
+    act(T.m4eye[:], T.eyeb[:], ["eyeb"], ["m4eye"], 128, None, -4.0)
+    ts(T.sel[:, 0:2048:16], T.i8[:], D16, 4096.0, EQ, OP.mult, ["i8", "pf"] + selz, ["sel"], 128)
+    ts(T.enc16[:], T.ienc[:], P16, None, OP.add, None, ["ienc", "pf"], ["enc16"], 128)
+    ts(T.meye16[:], ic0, PC, -1.0, EQ, OP.mult, ["ic", "pcol"], ["meye16"], 128)
+    for j in range(3):
+        ts(T.r384[:, 128 * j:128 * j + 128], T.i8[:], P8, -1.0 if j else 1.0, EQ, OP.mult, ["i8", "pf"], ["r384"], 128)
+    boost[0] = EARLY
+    cp(T.dt_[:], T.dm_i[:], ["dm_i"], ["dt"], 128)
+    ts(T.wcol[:], T.wt_i[:], 2.0, None, OP.mult, None, ["wt_i"], ["wcol"], 1)
+    ts(T.wsel[:, 0:2048:16], T.i8[:], D16, T.wcol[:], EQ, OP.mult, ["i8", "pf", "wcol", "wsel"], ["wsel"], 128)
+    boost[0] = 0.0
+    act(T.tab[:, 2048:2080], T.tab[:, 0:32], ["tab"], ["tabx"], 32)
     tabk = ["tab", "tabx", "tabz"]
     win = T.tab[:, 0:TW]
 
-    def index(cards, ck, esrc, ek, qb, fb, outs, n0, n1, nm):
-        for c in range(n0, n1, 64):
-            tt(qb[:, c:c + 64], cards[:, c:c + 64], esrc, OP.mult, [ck, ek], [nm + "q"])
-        yield
-        ts(fb[:, n0:n1], qb[:, n0:n1], 5, 2047, OP.arith_shift_right, OP.bitwise_and, [nm + "q"], [nm + "f"])
-        yield
+    def seats_e():
+        for a in range(16):
+            mm(T.b7[:, 128:136], T.wsel[:, 127 * a:127 * a + 128], T.dt_[:, a:128:16], a == 0, a == 15,
+               ["wsel", "dt"], ["B7.e"], 8)
+        cp(T.e1[:], T.b7[:, 128:136], ["B7.e"], ["e1"], 8)
+        ts(T.e2[:], T.e1[:], 2046, None, OP.bitwise_and, None, ["e1"], ["e2"], 8)
+        do("V", lambda: v.tensor_scalar(T.e33[:], T.e2[:].indirect(T.bc[:, 0:4]), 1.0, 33.0, OP.mult, OP.add),
+           ["e2", "bc"], ["e33"], gat(64))
+        for i in range(4):
+            act(T.b7[:, 144 + 64 * i:208 + 64 * i], T.e33[:], ["e33"], ["B7.e%d" % i], 64)
+
+    def spread_d(fused=True):
+        for i in range(4):
+            mm(T.b5[:, 128 * i:128 * i + 128], T.eyeb[:], T.dt_[:], True, True, ["eyeb", "dt"], ["B5.d"], 128)
+        if fused:
+            act(T.dt2[:], T.b5[:], ["B5.d", "e33"], ["dt2"], 512)
+
+    def index(cards, ck, qb, fb, n0, n1, outs, nm):
+        s, n = slice(n0, n1), n1 - n0
+        ek = ["B7.e%d" % i for i in range((n + 63) // 64)]
+        if nm == "oa":
+            tt(qb[:, s], cards, T.e33[:], OP.mult, [ck, "e33"], [nm + "q"], 2 * n)
+        else:
+            tt(qb[:, s], cards, T.b7[:, 144:144 + n], OP.mult, [ck] + ek, [nm + "q"], n)
+        ts(fb[:, s], qb[:, s], 5, 2047, OP.arith_shift_right, OP.bitwise_and, [nm + "q"], [nm + "f"], n)
         for out, z, key in outs:
             if z is None:
-                ts(out[:, n0:n1], fb[:, n0:n1], T.kf[:], None, OP.add, None, [nm + "f", "kf"], [key])
+                ts(out[:, s], fb[:, s], T.kf[:], None, OP.add, None, [nm + "f", "kf"], [key], n)
             else:
-                ts(out[:, n0:n1], fb[:, n0:n1], T.kf[:], z, OP.add, OP.add, [nm + "f", "kf"], [key])
-        yield
+                ts(out[:, s], fb[:, s], T.kf[:], z, OP.add, OP.add, [nm + "f", "kf"], [key], n)
 
     def ocards(t):
         return T.o16[:, 256 * (t % 2):256 * (t % 2) + 256], "o16.%d" % (t % 2)
 
-    def pool_index(t):
+    def block(x, y, off, base, pieces, nm, uk):
+        keys = []
+        end = base + pieces[-1][1]
+        for lo, hi in pieces:
+            lo, hi = lo + base, hi + base
+            actg(x[:, lo:hi], win.indirect(off[:, lo // 16:hi // 16]), tabk + [uk], [nm + "x%d" % lo], hi - lo)
+        if end < base + 1024:
+            ttg(y[:, end:base + 1024], win.indirect(off[:, end // 16:(base + 1024) // 16]),
+                T.dt2[:, 0:base + 1024 - end], OP.min, tabk + [uk, "dt2"], [nm + "f%d" % end], base + 1024 - end)
+            keys.append(nm + "f%d" % end)
+        for lo, hi in pieces:
+            lo, hi = lo + base, hi + base
+            tt(y[:, lo:hi], x[:, lo:hi], T.b5[:, 0:hi - lo], OP.min, [nm + "x%d" % lo, "B5.d"], [nm + "y%d" % lo], hi - lo)
+            keys.append(nm + "y%d" % lo)
+        return keys
+
+    def scores(out, k, const, l, ck, y, base, keys):
+        mm(out, l, const, True, False, ck, [k], 64)
+        for a in range(16):
+            mm(out, T.sel[:, 127 * a:127 * a + 128], y[:, base + a:base + 1024:16], False, a == 15, ["sel"] + keys, [k], 64)
+
+    def pools(t, share):
         o, ok = ocards(t)
-        e, ek = T.b7[:, 144:208], "B7.e33"
-        x = index(o, ok, e, ek, T.oq, T.of, [(T.ou, None, "ou0")], 0, 64, "o0")
-        y = index(o, ok, e, ek, T.oq, T.of, [(T.ou, None, "ou1")], 64, 256, "o1")
-        for z in (x, y, x, x, y, y):
-            next(z)
-
-    def pack_index(t, between=()):
-        parts = [index(T["c%d" % t], "c%d" % t, T.b7[:, 144:208], "B7.e33", T.pq, T.pfc, [(T.pu, None, "pu%d" % h)],
-                       64 * h, 64 * h + 64, "p%d" % h) for h in range(2)]
-        for i in range(3):
-            for x in parts:
-                next(x)
-            if between:
-                between[i]()
-
-    def ouk(c):
-        return "ou0" if c == 0 else "ou1"
-
-    def s_gather(dst, off, okey, lo, hi, key):
-        act(dst[:, lo:hi], win.indirect(off[:, lo // 16:hi // 16]), tabk + [okey], [key + "%d" % lo])
-
-    def v_fused(dst, off, okey, lo, hi, key):
-        tt(dst[:, lo:hi], win.indirect(off[:, lo // 16:hi // 16]), T.dt2[:, 0:hi - lo], OP.min,
-           tabk + [okey, "dt2"], [key])
-
-    def v_min(dst, src, skey, lo, hi, key):
-        tt(dst[:, lo:hi], src[:, lo:hi], T.b5[:, 0:hi - lo], OP.min, [skey + "%d" % lo, "B5.d"], [key])
-
-    def pool_scores(c):
-        out = T.b0[:, 64 * c:64 * c + 64]
-        mm(out, T.onesn[:], T.cpool[:, 64 * c:64 * c + 64], True, False, ["onesn", "cpool0", "cpool1"], ["B0.s"])
-        for a in range(16):
-            mm(out, T.sel[:, 127 * a:127 * a + 128], T.yo_[:, 1024 * c + a:1024 * (c + 1):16], False, a == 15,
-               ["sel", "yo%d" % c], ["B0.s"])
-
-    def pack_scores(h):
-        out = (T.b1, T.b2)[h][:, 0:64]
-        key = "B%d.s" % (1 + h)
-        mm(out, T.eye16[:], T.enc16[:, 64 * h:64 * h + 64], True, False, ["eye16", "enc16"], [key])
-        for a in range(16):
-            mm(out, T.sel[:, 127 * a:127 * a + 128], T.yp[:, 1024 * h + a:1024 * (h + 1):16], False, a == 15,
-               ["sel", "yp%d" % h], [key])
-        if h == 0:
-            act(T.losb[:], T.b1[:, 0:64], ["B1.s"], ["losb"])
-
-    SP = [(0, 384), (384, 768)]
-    FU = (768, 1024)
+        index(o[:, 0:64], ok, T.oq, T.of, 0, 64, [(T.ou, None, "oua")], "oa")
+        index(o[:, 64:256], ok, T.oq, T.of, 64, 256, [(T.ou, None, "oub")], "ob")
+        for c in range(4):
+            keys = block(T.xo, T.yo_, T.ou, 1024 * c, share[c], "o", "oub" if c else "oua")
+            scores(T.b0[:, 64 * c:64 * c + 64], "B0.s", T.cpool[:, 64 * c:64 * c + 64], T.onesn[:], ["onesn", "cpool"],
+                   T.yo_, 1024 * c, keys)
 
     def pool_min():
-        tt(T.p128[:], T.b0[:, 0:128], T.sohi[:], OP.min, ["B0.s", "sohi"], ["p128"])
-        tt(T.p64[:], T.p128[:, 0:64], T.p128[:, 64:128], OP.min, ["p128"], ["p64"])
-        tt(T.p32[:], T.p64[:, 0:32], T.p64[:, 32:64], OP.min, ["p64"], ["p32"])
-        tt(T.p16[:], T.p32[:, 0:16], T.p32[:, 16:32], OP.min, ["p32"], ["p16"])
-        tt(T.omin[:], T.p16[:, 0:8], T.p16[:, 8:16], OP.min, ["p16"], ["omin"])
+        act(T.sohi[:], T.b0[:, 128:256], ["B0.s"], ["sohi"], 128)
+        tt(T.p128[:], T.b0[:, 0:128], T.sohi[:], OP.min, ["B0.s", "sohi"], ["p128"], 128)
+        tt(T.p64[:], T.p128[:, 0:64], T.p128[:, 64:128], OP.min, ["p128"], ["p64"], 128)
+        tt(T.p32[:], T.p64[:, 0:32], T.p64[:, 32:64], OP.min, ["p64"], ["p32"], 64)
+        tt(T.p16[:], T.p32[:, 0:16], T.p32[:, 16:32], OP.min, ["p32"], ["p16"], 32)
+        tt(T.omin[:], T.p16[:, 0:8], T.p16[:, 8:16], OP.min, ["p16"], ["omin"], 16)
 
-    def pool_s(c):
-        for lo, hi in SP:
-            s_gather(T.xo, T.ou, ouk(c), 1024 * c + lo, 1024 * c + hi, "xo")
+    def pack_index(t):
+        boost[0] = 5.0
+        index(T["c%d" % t][:], "c%d" % t, T.pq, T.pfc, 0, 128, [(T.pu, None, "pu")], "p")
+        boost[0] = 0.0
 
-    def pool_f(c):
-        v_fused(T.yo_, T.ou, ouk(c), 1024 * c + FU[0], 1024 * c + FU[1], "yo%d" % c)
-
-    def pool_m(c):
-        for lo, hi in SP:
-            v_min(T.yo_, T.xo, "xo", 1024 * c + lo, 1024 * c + hi, "yo%d" % c)
-        pool_scores(c)
-
-    def pack_s(h):
-        for lo, hi in SP:
-            s_gather(T.xp, T.pu, "pu%d" % h, 1024 * h + lo, 1024 * h + hi, "xp")
-
-    def pack_f(h):
-        v_fused(T.yp, T.pu, "pu%d" % h, 1024 * h + FU[0], 1024 * h + FU[1], "yp%d" % h)
-
-    def pack_m(h, part):
-        lo, hi = SP[part]
-        v_min(T.yp, T.xp, "xp", 1024 * h + lo, 1024 * h + hi, "yp%d" % h)
-
-    def pool_copy():
-        act(T.sohi[:], T.b0[:, 128:256], ["B0.s"], ["sohi"])
+    def packs(t, share):
+        all_keys = []
+        for c in range(2):
+            keys = block(T.xp, T.yp, T.pu, 1024 * c, share[4 + c], "p", "pu")
+            scores(T.b1[:, 64 * c:64 * c + 64], "B1.s%d" % c, T.enc16[:, 64 * c:64 * c + 64], T.eye16[:],
+                   ["eye16", "enc16"], T.yp, 1024 * c, keys)
+            all_keys += keys
+            if c == 0:
+                act(T.losb[:], T.b1[:, 0:64], ["B1.s0"], ["losb"], 64)
+        tt(T.w64[:], T.b1[:, 64:128], T.losb[:], OP.max, ["B1.s1", "losb"], ["w64"], 64)
+        tt(T.w32[:], T.w64[:, 0:32], T.w64[:, 32:64], OP.max, ["w64"], ["w32"], 64)
+        tt(T.w16[:], T.w32[:, 0:16], T.w32[:, 16:32], OP.max, ["w32"], ["w16"], 32)
+        tt(T.m1[:], T.w16[:, 0:8], T.w16[:, 8:16], OP.max, ["w16"], ["m1"], 16)
+        return all_keys
 
     def pack_to_psum(t):
-        mm(T.b4[:, 0:128], T.eye16[:], T["c%d" % t][:], True, True, ["eye16", "c%d" % t], ["B4.c"])
+        mm(T.b4[:, 0:128], T.eye16[:], T["c%d" % t][:], True, True, ["eye16", "c%d" % t], ["B4.c"], 128)
 
-    def pack_max():
-        tt(T.w64[:], T.b2[:, 0:64], T.losb[:], OP.max, ["B2.s", "losb"], ["w64"])
-        tt(T.w32[:], T.w64[:, 0:32], T.w64[:, 32:64], OP.max, ["w64"], ["w32"])
-        tt(T.w16[:], T.w32[:, 0:16], T.w32[:, 16:32], OP.max, ["w32"], ["w16"])
-        tt(T.m1[:], T.w16[:, 0:8], T.w16[:, 8:16], OP.max, ["w16"], ["m1"])
+    def pools_to_psum(t):
+        o, ok = ocards(t)
+        mm(T.b4[:, 128:384], T.eye16[:], o, True, True, ["eye16", ok], ["B4.o"], 256)
 
-    ESPLIT = 8
+    def send(t):
+        rid, pid, _ = topo.addr(nxt)
+        m = 0
+        for en in topo.engines(core, nxt)[:NENG]:
+            m |= 1 << en
+        sem = "arr%d" % (t + 1)
+        src, dst = T["n%d" % t][:], T["c%d" % (t + 1)][:]
+        do("G", lambda: g.remote_dma(dst, src, T.sem[sem], T.sem.loc, pid, rid, m), ["n%d" % t], ["c%d" % (t + 1)],
+           1.0, WIRE, (sem, NENG))
 
-    def exchange(t):
+    def exchange(t, ykeys):
         last = t == NV - 1
-        tt(T.thi[:], T.m1[:], T.omin[:], OP.max, ["m1", "omin"], ["thi"])
-        tt(T.thf[:], T.m1[:], T.omin[:], OP.max, ["m1", "omin"], ["thf"])
-        ts(T.offi[:], T.thi[:], 4095, None, OP.bitwise_and, None, ["thi"], ["offi"])
-        tt(T.th2[:], T.m1[:], T.omin[:], OP.min, ["m1", "omin"], ["th2"])
-        cp(T.offu[:], T.offi[:], ["offi"], ["offu"])
-        if not last:
-            tt(T.swp[:], T.m1[:], T.omin[:], OP.is_gt, ["m1", "omin"], ["swp"])
-        act(T.thr[:], T.thf[:, 0:8].indirect(T.bc[:, 0:4]), ["thf", "bc"], ["thr"])
-        act(T.thr2[:], T.th2[:, 0:8].indirect(T.bc[:, 0:4]), ["th2", "bc"], ["thr2"])
-        tt(T.gt[:], T.yp[:, 0:2080].indirect(T.offu[:, 0:8]), T.dt_[:], OP.is_ge,
-           ["yp0", "yp1", "ypz", "offu", "dt"], ["gt"])
-        mm(T.b7[:, 0:128], T.eyeb[:], T.dt_[:], True, False, ["eyeb", "dt"], ["B7.d"])
-        mm(T.b7[:, 0:128], T.m4eye[:], T.gt[:], False, True, ["m4eye", "gt"], ["B7.d"])
-        tt(T.ohc[:, 0:64], T.b1[:, 0:64], T.thr[:], OP.is_ge, ["B1.s", "thr"], ["ohc"])
-        tt(T.ohc[:, 64:128], T.b2[:, 0:64], T.thr[:], OP.is_ge, ["B2.s", "thr"], ["ohc"])
-        for c in range(4):
-            tt(T.oho[:, 64 * c:64 * c + 64], T.b0[:, 64 * c:64 * c + 64], T.thr2[:], OP.is_le, ["B0.s", "thr2"], ["oho"])
-        ts(T.dt_[:], T.b7[:, 0:128], 1.0, None, OP.max, None, ["B7.d"], ["dt"])
-        if not last:
-            mm(T.b6[:, 384:392], T.ones[:], T.swp[:], True, True, ["ones", "swp"], ["B6.k"])
-            act(T.cscr[:], T.b6[:, 384:392], ["B6.k"], ["cnt", "cscr"], T.cnt[:])
-            seats_e(0, ESPLIT)
-        else:
-            act(T.yd_f[:], T.dt_[:], ["dt"], ["yd_f"])
+        mo = ["m1", "omin"]
+        tt(T.thi[:], T.m1[:], T.omin[:], OP.max, mo, ["thi"], 16)
+        tt(T.thf[:], T.m1[:], T.omin[:], OP.max, mo, ["thf"], 16)
+        tt(T.th2[:], T.m1[:], T.omin[:], OP.min, mo, ["th2"], 16)
+        ts(T.offi[:], T.thi[:], 4095, None, OP.bitwise_and, None, ["thi"], ["offi"], 8)
+        cp(T.offu[:], T.offi[:], ["offi"], ["offu"], 8)
+        actg(T.thr[:], T.thf[:].indirect(T.bc[:]), ["thf", "bc"], ["thr"], 128)
+        actg(T.thr2[:], T.th2[:].indirect(T.bc[:]), ["th2", "bc"], ["thr2"], 128)
+        ttg(T.gt[:], T.yp[:].indirect(T.offu[:]), T.dt_[:], OP.is_ge, ykeys + ["ypz", "offu", "dt"], ["gt"], 128)
+        mm(T.b7[:, 0:128], T.eyeb[:], T.dt_[:], True, False, ["eyeb", "dt"], ["B7.d"], 128)
+        mm(T.b7[:, 0:128], T.m4eye[:], T.gt[:], False, True, ["m4eye", "gt"], ["B7.d"], 128)
+        ts(T.dt_[:], T.b7[:, 0:128], 1.0, None, OP.max, None, ["B7.d"], ["dt"], 128)
+        if last:
+            act(T.yd_f[:], T.dt_[:], ["dt"], ["yd_f"], 128)
             store("Y", "st_yd", T.yd[:], T.yd_f[:], ["yd_f"])
-        tt(T.cm[:], T.ohc[:], T.b4[:, 0:128], OP.mult, ["ohc", "B4.c"], ["cm"])
-        tt(T.om[:], T.oho[:], T.b3[:, 0:256], OP.mult, ["oho", "B3.o"], ["om"])
-        mm(T.b6[:, 0:128], T.cm[:], T.meye16[:], True, False, ["cm", "meye16"], ["B6.t"])
-        mm(T.b6[:, 0:128], T.om[:, 0:128], T.eye16[:], False, False, ["om", "eye16"], ["B6.t"])
-        mm(T.b6[:, 0:128], T.om[:, 128:256], T.eye16[:], False, True, ["om", "eye16"], ["B6.t"])
+        tt(T.oh[:, 0:128], T.b1[:, 0:128], T.thr[:], OP.is_ge, ["B1.s0", "B1.s1", "thr"], ["ohc"], 128)
+        for c in range(2):
+            tt(T.oh[:, 128 + 128 * c:256 + 128 * c], T.b0[:, 128 * c:128 * c + 128], T.thr2[:], OP.is_le,
+               ["B0.s", "thr2"], ["oho%d" % c], 128)
+        ohk = ["ohc", "oho0", "oho1"]
+        tt(T.com[:], T.oh[:], T.b4[:, 0:384], OP.mult, ohk + ["B4.c", "B4.o"], ["com"], 384)
+        for j in range(3):
+            mm(T.b6[:, 0:128], T.com[:, 128 * j:128 * j + 128], (T.eye16 if j else T.meye16)[:], j == 0, j == 2,
+               ["com", "eye16", "meye16"], ["B6.t"], 128)
         if not last:
-            seats_e(ESPLIT, 16)
-            ts(T.kr[:], T.cnt[:], 0.03125, -0.484375, OP.mult, OP.add, ["cnt"], ["kr"])
-        cp(T.tc16[:], T.b6[:, 0:128], ["B6.t"], ["tc16"])
-        mm(T.b6[:, 128:256], T.tc16[:], T.r16[:], True, True, ["tc16", "r16"], ["B6.d"])
-        if not last:
-            ts(T.kf[:], T.kr[:], -32.0, T.cnt[:], OP.mult, OP.add, ["kr", "cnt"], ["kf"])
-            e_one()
+            mm(T.b2[:, 0:128], T.ones[:], T.oh[:, 0:128], True, True, ["ones", "ohc"], ["B2.k"], 128)
+            act(T.cscr[:], T.b2[:, 0:128], ["B2.k"], ["cnt", "cscr"], 128, T.cnt[:])
+            ts(T.kr[:], T.cnt[:], 0.03125, -0.484375, OP.mult, OP.add, ["cnt"], ["kr"], 1)
+            ts(T.kf[:], T.kr[:], -32.0, T.cnt[:], OP.mult, OP.add, ["kr", "cnt"], ["kf"], 1)
+            seats_e()
+        cp(T.tc16[:], T.b6[:, 0:128], ["B6.t"], ["tc16"], 128)
+        mm(T.b6[:, 128:512], T.tc16[:], T.r384[:], True, True, ["tc16", "r384"], ["B6.d"], 384)
+        tt(T.b3[:, 0:384], T.oh[:], T.b6[:, 128:512], OP.mult, ohk + ["B6.d"], ["B3.u"], 384)
+        tt(T["n%d" % t][:], T["c%d" % t][:], T.b3[:, 0:128], OP.add, ["c%d" % t, "B3.u"], ["n%d" % t], 128)
         o, ok = ocards(t)
         on, onk = ocards(t + 1)
-        tt(T.b4[:, 128:256], T.ohc[:], T.b6[:, 128:256], OP.mult, ["ohc", "B6.d"], ["B4.t"])
-        tt(T.b4[:, 256:384], T.oho[:, 0:128], T.b6[:, 128:256], OP.mult, ["oho", "B6.d"], ["B4.u"])
-        tt(T["n%d" % t][:], T["c%d" % t][:], T.b4[:, 128:256], OP.add, ["c%d" % t, "B4.t"], ["n%d" % t])
-        tt(T.b4[:, 384:512], T.oho[:, 128:256], T.b6[:, 128:256], OP.mult, ["oho", "B6.d"], ["B4.v"])
-        if last:
-            to_lanes(0, T["n%d" % t][:], "n%d" % t)
+        tt(on, o, T.b3[:, 128:384], OP.add, [ok, "B3.u"], [onk], 256)
         if not last:
-            e_two()
-        tt(on[:, 0:128], o[:, 0:128], T.b4[:, 256:384], OP.subtract, [ok, "B4.u"], [onk])
-        if not last:
-            e_three()
-            spread_d()
-        tt(on[:, 128:256], o[:, 128:256], T.b4[:, 384:512], OP.subtract, [ok, "B4.v"], [onk])
-        if not last:
-            mm(T.b3[:, 0:256], T.eye16[:], on, True, True, ["eye16", onk], ["B3.o"])
-            order("G", ["n%d" % t], [])
-            rid, pid, _ = topo.addr(nxt)
-            m = 0
-            for en in topo.engines(core, nxt)[:NENG]:
-                m |= 1 << en
-            g.remote_dma(T["c%d" % (t + 1)][:], T["n%d" % t][:], T.sem["arr%d" % (t + 1)], T.sem.loc, pid, rid, m)
-            lastw["c%d" % (t + 1)] = ("arr%d" % (t + 1), NENG)
+            send(t)
+            spread_d(t < NV - 2)
+            pools_to_psum(t + 1)
 
-    def to_lanes(i, src, skey):
-        out = (T.b7, T.b1, T.b2)[i][:, 256:384]
-        mm(out, src, T.permf16[:], True, True, [skey, "permf16"], ["B%d.f" % (7, 1, 2)[i]])
-        return out, "B%d.f" % (7, 1, 2)[i]
-
+    Q = [T.q3[:, 128 * i:128 * i + 128] for i in range(3)]
+    RW = [T.rw3[:, 1024 * i:1024 * i + 1024] for i in range(3)]
+    BK = [T.b0, T.b1, T.b2]
+    cp(T.pk16[:], T.pk_i[:], ["pk_i"], ["pk16"], 128)
+    cp(T.poa16[:], T.po_i[:, 0:256:2], ["po_i"], ["poa16"], 128)
+    cp(T.pob16[:], T.po_i[:, 1:256:2], ["po_i"], ["pob16"], 128)
+    boost[0] = EARLY
+    seats_e()
+    boost[0] = 0.0
+    for i, (src, p) in enumerate([("pk16", "perm16"), ("poa16", "eye16"), ("pob16", "eye16")]):
+        mm(T.b0[:, 128 * i:128 * i + 128], T[src][:], T[p][:], True, True, [src, p], ["B0.q%d" % i], 128)
+    cp(T.q3[:], T.b0[:, 0:384], ["B0.q0", "B0.q1", "B0.q2"], ["q3"], 384)
+    for b in range(8):
+        ts(T.rw3[:, b:3072:8], T.q3[:], T.mb[:, b:b + 1], None, OP.mult, None, ["q3", "mb"], ["rw%d" % b], 192)
+    for i, (out, k) in enumerate([(T.b4[:, 0:128], "B4.c"), (T.b3[:, 0:128], "B3.a"), (T.b3[:, 128:256], "B3.b")]):
+        for x in range(8):
+            mm(out, T.zb[:, 112 - 16 * x:240 - 16 * x], T.rw3[:, 1024 * i + 128 * x:1024 * i + 128 * x + 128],
+               x == 0, x == 7, ["zb"] + ["rw%d" % b for b in range(8)], [k], 128)
+    cp(T.c0[:], T.b4[:, 0:128], ["B4.c"], ["c0"], 128)
+    spread_d()
     pack_index(0)
-    pack_s(0)
-    pack_s(1)
-    cp(T.poa16[:], T.po_i[:, 0:256:2], ["po_i"], ["poa16"])
-    cp(T.pob16[:], T.po_i[:, 1:256:2], ["po_i"], ["pob16"])
-    mm(T.b6[:, 128:256], T.poa16[:], T.eye16[:], True, True, ["poa16", "eye16"], ["B6.q1"])
-    mm(T.b6[:, 256:384], T.pob16[:], T.eye16[:], True, True, ["pob16", "eye16"], ["B6.q2"])
-    lanes_to_seats(1, (T.b6[:, 128:256], "B6.q1"), T.b7[:, 256:384], "B7.o1")
-    lanes_to_seats(2, (T.b6[:, 256:384], "B6.q2"), T.b7[:, 384:512], "B7.o2")
-    cp(T.o16[:, 0:256], T.b7[:, 256:512], ["B7.o1", "B7.o2"], ["o16.0"])
-    mm(T.b3[:, 0:256], T.eye16[:], T.o16[:, 0:256], True, True, ["eye16", "o16.0"], ["B3.o"])
-    pool_index(0)
-    for c in range(4):
-        pool_s(c)
-    fill(T.sel[:], 0.0, ["sel"])
-    ts(T.sel[:, 0:2048:16], T.i8[:], D16, 4096.0, OP.is_equal, OP.mult, ["i8", "pf", "sel"], ["sel"])
-    ts(T.enc16[:], T.ienc[:], P16, None, OP.add, None, ["ienc", "pf"], ["enc16"])
-    pack_f(0)
-    pack_m(0, 0)
-    pack_m(0, 1)
-    pack_scores(0)
-    pack_f(1)
-    pack_m(1, 0)
-    pack_m(1, 1)
-    pack_scores(1)
-    fill(T.onesn[:], 0.0078125, ["onesn"])
-    fill(T.cpool[0:64, :], 4096.0, ["cpool0", "cpool1"])
-    fill(T.yp[:, 2048:2080], 0.0, ["ypz"])
-    fill(T.ones[:], 1.0, ["ones"])
-    for c in range(4):
-        pool_f(c)
-        if c == 0:
-            ts(T.meye16[:], ic0, T.pcol[:], -1.0, OP.is_equal, OP.mult, ["ic", "pcol"], ["meye16"])
-            ts(T.m4eye[:], ic0, T.pcol[:], -4.0, OP.is_equal, OP.mult, ["ic", "pcol"], ["m4eye"])
-            ts(T.r16[:], T.i8[:], P8, None, OP.is_equal, None, ["i8", "pf"], ["r16"])
-        pool_m(c)
-    pool_copy()
-    pack_max()
-    pool_min()
-    exchange(0)
+    cp(T.o16[:, 0:256], T.b3[:, 0:256], ["B3.a", "B3.b"], ["o16.0"], 256)
+    pools_to_psum(0)
 
-    for t in range(1, NV - 1):
-        pool_index(t)
-        for c in range(4):
-            pool_s(c)
-        pack_to_psum(t)
-        for c in range(3):
-            pool_f(c)
-            pool_m(c)
-        pool_f(3)
-        pack_index(t)
-        pack_s(0)
-        pack_s(1)
-        pool_m(3)
-        pack_f(0)
-        pack_m(0, 0)
-        pack_f(1)
-        pack_m(0, 1)
-        pool_copy()
-        pack_scores(0)
-        pack_m(1, 0)
-        pack_m(1, 1)
-        pack_scores(1)
+    for t in range(NV - 1):
+        share = SHARE
+        if t:
+            pack_to_psum(t)
+        pools(t, share)
         pool_min()
-        pack_max()
-        exchange(t)
+        if t:
+            pack_index(t)
+        exchange(t, packs(t, share))
 
     t = NV - 1
-    HALF = [(i, i + 512) for i in range(0, 4096, 512)]
-    QUAR = [(i, i + 256) for i in range(0, 2048, 256)]
 
-    def chain(off, okey, out, key):
-        acc = [T.acc0, T.acc1]
-        for i, (lo, hi) in enumerate(QUAR):
-            src = win.indirect(off[:, lo // 16:hi // 16])
-            if i == 0:
-                cp(acc[0][:], src, tabk + [okey], ["acc0"])
-            else:
-                tt(acc[i % 2][:], src, acc[(i + 1) % 2][:], OP.max, tabk + [okey, "acc%d" % ((i + 1) % 2)],
-                   ["acc%d" % (i % 2)])
-        tt(out[:], acc[1][:, 0:128], acc[1][:, 128:256], OP.max, ["acc1"], [key])
-
-    pool_index(t)
-    for i, (lo, hi) in enumerate(HALF):
-        s_gather(T.xo, T.ou, ouk(i // 2), lo, hi, "xo")
-    for x in index(T.n0, "n0", T.b7[:, 144:208], "B7.e33", T.pq, T.pfc, [(T.mu, None, "mu"), (T.mz, -float(ZC), "mz")], 0, 128, "m"):
-        pass
-    chain(T.mu, "mu", T.bmax, "bmax")
-    ts(T.permf16[:], T.ipermf[:], T.pcol[:], None, OP.is_equal, None, ["ipermf", "pcol"], ["permf16"])
-    ts(T.prev[:], D8, -1.0, 15.0, OP.mult, OP.add, ["pf"], ["prev"])
-    ts(T.mf[:], T.i8[:, 0:8], P8, None, OP.is_equal, None, ["i8", "pf"], ["mf"])
-    ts(T.zfo[:], T.ic[:], D8, None, OP.is_equal, None, ["ic", "pf"], ["zfo"])
-    ts(T.zfp[:], T.ic[:], T.prev[:], None, OP.is_equal, None, ["ic", "prev"], ["zfp"])
+    def chain(off, okey, y, acc, half, out, key):
+        for i in range(3):
+            actg(y[:, 512 * i:512 * i + 512], win.indirect(off[:, 32 * i:32 * i + 32]), tabk + [okey], [key + "g%d" % i], 512)
+        ttg(acc[0][:], win.indirect(off[:, 96:128]), y[:, 0:512], OP.max, tabk + [okey, key + "g0"], [key + "0"], 512)
+        for i, b in ((1, T.b2), (2, T.b3)):
+            bk = "B%d.%s" % (i + 1, key)
+            mm(b[:], T.eyeb[:], y[:, 512 * i:512 * i + 512], True, True, ["eyeb", key + "g%d" % i], [bk], 512)
+            tt(acc[i % 2][:], acc[1 - i % 2][:], b[:], OP.max, [key + str(1 - i % 2), bk], [key + str(i % 2)], 512)
+        acc = [acc[1], acc[0]]
+        tt(half[:], acc[1][:, 0:256], acc[1][:, 256:512], OP.max, [key + "0"], [key + "h"], 512)
+        tt(out[:], half[:, 0:128], half[:, 128:256], OP.max, [key + "h"], [key + "m"], 256)
+    index(T.n0[:], "n0", T.mq, T.mfc, 0, 128, [(T.mu, None, "mu"), (T.mz, -float(ZC), "mz")], "m")
+    chain(T.mu, "mu", T.yb, [T.acc0, T.acc1], T.bh, T.bmax, "cb")
     pack_to_psum(t)
-    pack_index(t, [
-        lambda: tt(T.stay[:], T.n0[:], T.b4[:, 0:128], OP.is_equal, ["n0", "B4.c"], ["stay"]),
-        lambda: tt(T.sz[:], T.stay[:], T.mz[:], OP.mult, ["stay", "mz"], ["sz"]),
-        lambda: ts(T.au[:], T.sz[:], float(ZC), None, OP.add, None, ["sz"], ["au"])])
-    for i, (lo, hi) in enumerate(HALF[0:4]):
-        s_gather(T.xp, T.pu, "pu%d" % (i // 2), lo, hi, "xp")
-    chain(T.au, "au", T.amax, "amax")
-    tt(T.up[:], T.amax[:], T.bmax[:], OP.is_ge, ["amax", "bmax"], ["up"])
-    ts(T.up8[:], T.up[:], 16.0, -8.0, OP.mult, OP.add, ["up"], ["up8"])
-    tt(T.dsum[:], T.dt_[:], T.up8[:], OP.add, ["dt", "up8"], ["dsum"])
-    ts(T.dt_[:], T.dsum[:], 1.0, 255.0, OP.max, OP.min, ["dsum"], ["dt"])
-    for i in range(4):
-        mm(T.b5[:, 128 * i:128 * i + 128], T.eyeb[:], T.dt_[:], True, True, ["eyeb", "dt"], ["B5.d"])
-    for c in range(4):
-        for lo, hi in HALF[2 * c:2 * c + 2]:
-            v_min(T.yo_, T.xo, "xo", lo, hi, "yo%d" % c)
-        pool_scores(c)
-    for lo, hi in HALF[0:2]:
-        v_min(T.yp, T.xp, "xp", lo, hi, "yp0")
-    pool_copy()
-    pack_scores(0)
-    for lo, hi in HALF[2:4]:
-        v_min(T.yp, T.xp, "xp", lo, hi, "yp1")
-    pack_scores(1)
+    pack_index(t)
+    tt(T.stay[:], T.n0[:], T.b4[:, 0:128], EQ, ["n0", "B4.c"], ["stay"], 128)
+    tt(T.sz[:], T.stay[:], T.mz[:], OP.mult, ["stay", "mz"], ["sz"], 256)
+    ts(T.au[:], T.sz[:], float(ZC), None, OP.add, None, ["sz"], ["au"], 128)
+    chain(T.au, "au", T.ya, [T.acc2, T.acc3], T.ah, T.amax, "ca")
+    tt(T.up[:], T.amax[:], T.bmax[:], OP.is_ge, ["cam", "cbm"], ["up"], 256)
+    ts(T.up8[:], T.up[:], 16.0, -8.0, OP.mult, OP.add, ["up"], ["up8"], 64)
+    tt(T.dsum[:], T.dt_[:], T.up8[:], OP.add, ["dt", "up8"], ["dsum"], 256)
+    ts(T.dt_[:], T.dsum[:], 1.0, 255.0, OP.max, OP.min, ["dsum"], ["dt"], 128)
+    spread_d(False)
+    pools(t, [FULL] * 6)
     pool_min()
-    pack_max()
-    exchange(t)
+    exchange(t, packs(t, [FULL] * 6))
 
-    def seats_to_list(i, z, zk, out, key):
-        src, skey = (T.b7, T.b1, T.b2)[i][:, 256:384], "B%d.f" % (7, 1, 2)[i]
-        cp(Q[i][:], src, [skey], ["q%d" % i])
+    ts(T.permf16[:], T.ipermf[:], PC, None, EQ, None, ["ipermf", "pcol"], ["permf16"], 128)
+    ts(T.prev[:], D8, -1.0, 15.0, OP.mult, OP.add, ["pf"], ["prev"], 1)
+    ts(T.mf[:], T.i8[:, 0:8], P8, None, EQ, None, ["i8", "pf"], ["mf"], 8)
+    ts(T.zfo[:], T.ic[:], D8, None, EQ, None, ["ic", "pf"], ["zfo"], 240)
+    ts(T.zfp[:], T.ic[:], T.prev[:], None, EQ, None, ["ic", "prev"], ["zfp"], 240)
+
+    def seats_to_list(i, src, skey, z, zk, out, ok, dst, dk):
+        k = "B%d.f" % i
+        mm(BK[i][:, 384:512], src, T.permf16[:], True, True, [skey, "permf16"], [k], 128)
+        cp(Q[i], BK[i][:, 384:512], [k], ["q%d" % i], 128)
         for b in range(8):
-            ts(RW[i][:, 128 * b:128 * b + 128], Q[i][:], T.mf[:, b:b + 1], None, OP.mult, None,
-               ["q%d" % i, "mf"], ["rw%d" % i])
-        for h in range(8):
-            mm(out, z[:, 112 - 16 * h:240 - 16 * h], RW[i][:, h:1024:8], h == 0, h == 7, ["rw%d" % i, zk], [key])
-
+            ts(RW[i][:, 128 * b:128 * b + 128], Q[i], T.mf[:, b:b + 1], None, OP.mult, None, ["q%d" % i, "mf"],
+               ["rx%d%d" % (i, b)], 64)
+        for x in range(8):
+            mm(out, z[:, 112 - 16 * x:240 - 16 * x], RW[i][:, x:1024:8], x == 0, x == 7,
+               [zk] + ["rx%d%d" % (i, b) for b in range(8)], [ok], 128)
+        act(dst, out, [ok], [dk], 128)
     oe, oek = ocards(NV)
-    to_lanes(1, oe[:, 0:128], oek)
-    to_lanes(2, oe[:, 128:256], oek)
-    seats_to_list(0, T.zfp, "zfp", T.b0[:, 0:128], "B0.y")
-    act(T.yc_f[:], T.b0[:, 0:128], ["B0.y"], ["yc_f"])
+    seats_to_list(0, T["n%d" % t][:], "n%d" % t, T.zfp, "zfp", T.b4[:, 0:128], "B4.y", T.yc_f[:], "yc_f")
+    seats_to_list(1, oe[:, 0:128], oek, T.zfo, "zfo", T.b5[:, 0:128], "B5.y", T.yo_f[:, 0:256:2], "yo_f0")
+    seats_to_list(2, oe[:, 128:256], oek, T.zfo, "zfo", T.b7[:, 0:128], "B7.y", T.yo_f[:, 1:256:2], "yo_f1")
     store("Y", "st_yc", T.yc[:], T.yc_f[:], ["yc_f"])
-    seats_to_list(1, T.zfo, "zfo", T.b3[:, 0:128], "B3.y")
-    act(T.yo_f[:, 0:256:2], T.b3[:, 0:128], ["B3.y"], ["yo_f"])
-    seats_to_list(2, T.zfo, "zfo", T.b5[:, 0:128], "B5.y")
-    act(T.yo_f[:, 1:256:2], T.b5[:, 0:128], ["B5.y"], ["yo_f"])
-    store("Y", "st_yo", T.yo[:], T.yo_f[:], ["yo_f"])
+    store("Y", "st_yo", T.yo[:], T.yo_f[:], ["yo_f0", "yo_f1"])
 
-    for e in sems:
-        need("G", (sems[e], count[e]))
+    n = len(ops)
+    preds = [{} for _ in range(n)]
+    lastw, readers, bankacc = {}, {}, {}
+    for i, (eng, call, reads, writes, dur, lat, tok) in enumerate(ops):
+        def edge(j, wait, i=i):
+            if j != i:
+                preds[i][j] = preds[i].get(j, False) or wait
+        for k in reads:
+            if k in lastw:
+                edge(lastw[k], True)
+        for k in writes:
+            if k in lastw:
+                edge(lastw[k], ops[lastw[k]][0] != eng)
+            for j in readers.get(k, []):
+                edge(j, ops[j][0] != eng or ops[j][6] is not None)
+        for k in sorted({k[:2] for k in reads + writes if k[0] == "B"}):
+            turn = bankacc.setdefault(k, [eng, [], []])
+            if turn[0] != eng:
+                turn[0], turn[1], turn[2] = eng, turn[2], []
+            for j in turn[1]:
+                edge(j, True)
+            if eng == "P" and turn[2]:
+                edge(turn[2][-1], False)
+            turn[2].append(i)
+        for k in reads:
+            readers.setdefault(k, []).append(i)
+        for k in writes:
+            lastw[k] = i
+            readers[k] = []
+    succs = [[] for _ in range(n)]
+    for i in range(n):
+        for j in preds[i]:
+            succs[j].append(i)
+    prio = [0.0] * n
+    for i in range(n - 1, -1, -1):
+        own = ops[i][4] + ops[i][5]
+        best = 0.0
+        for s in succs[i]:
+            best = max(best, prio[s] + (own + HOP if preds[s][i] else ops[i][4]))
+        prio[i] = max(best, own)
+
+    left = [len(p) for p in preds]
+    est = [0.0] * n
+    ready = {e: [] for e in queues}
+    free = {e: 0.0 for e in queues}
+    for i in range(n):
+        if left[i] == 0:
+            ready[ops[i][0]].append(i)
+    sequence = []
+    for _ in range(n):
+        pick = None
+        for e in queues:
+            if ready[e]:
+                st = max(free[e], min(est[i] for i in ready[e]))
+                i = max((i for i in ready[e] if est[i] <= st + 1e-9), key=lambda i: (prio[i] + boosts[i], -i))
+                if pick is None or st < pick[0]:
+                    pick = (st, e, i)
+        st, e, i = pick
+        ready[e].remove(i)
+        sequence.append(i)
+        free[e] = st + ops[i][4]
+        for s in succs[i]:
+            est[s] = max(est[s], free[e] + (ops[i][5] + HOP if preds[s][i] else 0.0))
+            left[s] -= 1
+            if left[s] == 0:
+                ready[ops[s][0]].append(s)
+
+    count = {e: 0 for e in counters}
+    waited = {e: {} for e in queues}
+    token = {}
+
+    def need(e, tok):
+        s, c = tok
+        if waited[e].get(s, 0) < c:
+            queues[e].wait_ge(T.sem[s], c)
+            waited[e][s] = c
+
+    for i in sequence:
+        eng, call, reads, writes, dur, lat, tok = ops[i]
+        toks = {}
+        for j, w in preds[i].items():
+            if w and token[j][1] > toks.get(token[j][0], 0):
+                toks[token[j][0]] = token[j][1]
+        for s in toks:
+            need(eng, (s, toks[s]))
+        if tok is None:
+            count[eng] += 1
+            call().then_inc(T.sem[counters[eng]], 1)
+            token[i] = (counters[eng], count[eng])
+        else:
+            call()
+            token[i] = tok
+    for e in counters:
+        need("G", (counters[e], count[e]))
     for s in LOADS + STORES:
         need("G", (s, 16))
-    need("G", ("loc", NENG * (NV - 1)))
-    for k in range(1, NV):
-        need("G", ("arr%d" % k, NENG))
+    need("G", ("loc", NENG * len(ARR)))
+    for s in ARR:
+        need("G", (s, NENG))

@@ -6,6 +6,8 @@ AF = ActivationFunctionType
 NV = 6
 ZC = 2080
 TW = 2096
+KOFF = 4128.0
+EOFF = 264192.0
 FULL = [(0, 512), (512, 1024)]
 PART = [(0, 512)]
 SHARE = [PART, PART, FULL, PART, FULL, PART]
@@ -20,24 +22,25 @@ SCRATCH = {
     "pk_i": sb(128, I32), "po_i": sb(256, I32), "dm_i": sb(128, I32), "wt_i": sb(1, I32), "tab": sb(TW, B16),
     "ic": sb(240, F32), "i8": sb(128, F32), "iperm": sb(128, F32), "ipermf": sb(128, F32), "ienc": sb(128, F32),
     "ip": sb(1, I32), "pint": sb(4, I32), "pf": sb(4, F32), "pcol": sb(1, F32), "prev": sb(1, F32),
-    "eye16": sb(128, F16), "meye16": sb(128, F16), "r384": sb(384, F16), "perm16": sb(128, F16),
+    "eye16": sb(128, F16), "meye16": sb(128, F16), "r256": sb(256, F16), "perm16": sb(128, F16),
     "permf16": sb(128, F16), "zb": sb(240, F16), "zfp": sb(240, F16), "zfo": sb(240, F16),
     "enc16": sb(128, F16), "cpool": sb(256, B16), "onesn": sb(128, B16), "mb": sb(8, F32), "mf": sb(8, F32),
-    "bc": sb(8, U16), "eyeb": sb(128, B16), "m4eye": sb(128, B16), "ones": sb(128, B16),
+    "bc": sb(16, U16), "eyeb": sb(128, B16), "m4eye": sb(128, B16), "ones": sb(128, B16),
     "sel": sb(2048, B16), "wsel": sb(2048, B16), "wcol": sb(1, F32),
     "pk16": sb(128, F16), "poa16": sb(128, F16), "pob16": sb(128, F16),
     "q3": sb(384, F16), "rw3": sb(3072, F16), "ya": sb(2048, B16), "yb": sb(2048, B16),
-    "o16": sb(512, F16), "dt_": sb(128, B16), "dt2": sb(512, B16),
-    "e1": sb(8, I32), "e2": sb(8, I32), "e33": sb(64, F32),
-    "kf": sb(1, F32), "kr": sb(1, I32), "cnt": sb(1, F32), "cscr": sb(128, F32),
+    "o16": sb(256, F16), "to16": sb(256 * NV, F16),
+    "dt_": sb(128, B16), "dt2": sb(512, B16),
+    "e1": sb(8, B16), "e2": sb(8, F32), "e33": sb(64, F32), "e33w": sb(256, F32),
+    "kf": sb(1, F32), "kr": sb(1, B16), "cnt": sb(1, F32), "cscr": sb(128, F32),
     "oq": sb(256, I32), "of": sb(256, I32), "ou": sb(256, U16),
     "pq": sb(128, I32), "pfc": sb(128, I32), "pu": sb(128, U16),
     "xo": sb(4096, B16), "yo_": sb(4096, B16), "xp": sb(2048, B16), "yp": sb(2080, B16),
     "losb": sb(64, F32), "w64": sb(64, F32), "w32": sb(32, F32), "w16": sb(16, F32), "m1": sb(8, F32),
     "sohi": sb(128, F32), "p128": sb(128, F32), "p64": sb(64, F32), "p32": sb(32, F32), "p16": sb(16, F32),
     "omin": sb(8, F32),
-    "thi": sb(8, I32), "offi": sb(8, I32), "offu": sb(8, U16), "thf": sb(8, F32), "th2": sb(8, F32),
-    "thr": sb(128, F32), "thr2": sb(128, F32), "gt": sb(128, B16),
+    "thi": sb(8, I32), "offi": sb(8, I32), "offu": sb(8, U16), "thf": sb(8, F32), "tco": sb(128, F32), "rf": sb(128, F32),
+    "thr": sb(128, F32), "thr2": sb(256, F32), "gt": sb(128, B16),
     "oh": sb(384, B16), "com": sb(384, F16), "tc16": sb(128, F16),
     "mq": sb(128, I32), "mfc": sb(128, I32), "mu": sb(128, U16), "mz": sb(128, F32),
     "stay": sb(128, F32), "sz": sb(128, F32), "au": sb(128, U16),
@@ -57,10 +60,13 @@ STORES = ["st_yc", "st_yo", "st_yd"]
 ARR = ["arr%d" % t for t in range(1, NV)]
 SEMAPHORES = ["sv", "sa", "sp", "sg", "loc"] + LOADS + STORES + ARR
 
-CYC, PCYC, CALL, HOP, GATH, WIRE = 0.00091, 0.00079, 0.05, 0.06, 1.5, 3.0
+CYC, PCYC, CALL, HOP, GATH, WIRE = 0.00091, 0.00079, 0.05, 0.06, 1.5, 4.0
 
 
 EARLY = 4.0
+BOOST = {"cb": -8, "B2.w": 4, "rf": -1, "B2.k": 1, "B7.e": 4, "B5.d": 1, "mu": -2, "up": 1, "B3.o": -1, "B1.s": 2,
+         "obf": -8, "e": -4, "thi": 2, "omin": 4, "thf": -8, "dt": -4, "eye16": -2, "c": 4, "p": 4, "perm16": -2,
+         "offi": -4, "zfo": 2}
 
 
 def rank_program(g, core, T, topo):
@@ -77,7 +83,7 @@ def rank_program(g, core, T, topo):
 
     def do(eng, call, reads, writes, dur, lat=0.0, tok=None):
         ops.append((eng, call, reads, writes, dur, lat, tok))
-        boosts.append(boost[0])
+        boosts.append(boost[0] + BOOST.get(writes[0].rstrip("012345") if writes else "", 0.0))
 
     def vec(n):
         return CALL + max(64, n) * CYC
@@ -103,8 +109,8 @@ def rank_program(g, core, T, topo):
     def fill(ap, c, w, n):
         do("V", lambda: v.memset(ap, c), [], w, vec(n))
 
-    def act(out, x, r, w, n, acc=None, scale=1.0, bias=0.0):
-        do("A", lambda: a_.activation(out, x, AF.Copy, bias=bias, scale=scale, accum_out=acc), r, w, vec(n))
+    def act(out, x, r, w, n, acc=None, scale=1.0, bias=0.0, func=AF.Copy):
+        do("A", lambda: a_.activation(out, x, func, bias=bias, scale=scale, accum_out=acc), r, w, vec(n))
 
     def actg(out, x, r, w, n):
         do("A", lambda: a_.activation(out, x, AF.Copy), r, w, gat(n) + 0.015)
@@ -137,7 +143,7 @@ def rank_program(g, core, T, topo):
     iota(T.cpool[:], [[2, 32], [0, 8]], 0, 0, ["cpool"], 256)
     iota(T.ipermf[:], [[1, 16], [16, 8]], 0, 0, ["ipermf"], 128)
     fill(T.wsel[:], 0.0, ["wsel"], 1024)
-    fill(T.kf[:], 0.0, ["kf"], 1)
+    fill(T.kf[:], -KOFF, ["kf"], 1)
     for j, (op, s) in enumerate([(OP.bitwise_and, 15), (OP.bitwise_and, 7),
                                  (OP.arith_shift_right, 4), (OP.arith_shift_right, 3)]):
         ts(T.pint[:, j:j + 1], T.ip[:], s, None, op, None, ["ip"], ["pint%d" % j], 1)
@@ -148,9 +154,10 @@ def rank_program(g, core, T, topo):
     PC, EQ = T.pcol[:], OP.is_equal
     ts(T.mb[:], T.i8[:, 0:8], D16, None, EQ, None, ["i8", "pf"], ["mb"], 8)
     ts(T.zb[:], T.ic[:], P16, None, EQ, None, ["ic", "pf"], ["zb"], 240)
-    ts(T.eyeb[:], ic0, PC, None, EQ, None, ["ic", "pcol"], ["eyeb"], 128)
+    act(T.ones[:], T.ic[:, 0:128], ["ic"], ["ones"], 128, None, 0.0, 1.0)
+    do("G", lambda: g.affine_select(T.eyeb[:], T.ones[:], [[-1, 128]], EQ, 0.0, 0, 1), ["ones"], ["eyeb"], 0.4)
     ts(T.eye16[:], ic0, PC, None, EQ, None, ["ic", "pcol"], ["eye16"], 128)
-    ts(T.bc[:], T.i8[:, 0:8], 0.0, P8, OP.mult, OP.add, ["i8", "pf"], ["bc"], 8)
+    ts(T.bc[:], T.i8[:, 0:16], 0.0, P8, OP.mult, OP.add, ["i8", "pf"], ["bc"], 16)
     ts(T.perm16[:], T.iperm[:], PC, None, EQ, None, ["iperm", "pcol"], ["perm16"], 128)
     selz = ["selz%d" % i for i in range(0, 2048, 240)]
     for i in range(0, 2048, 240):
@@ -158,16 +165,16 @@ def rank_program(g, core, T, topo):
         act(T.sel[:, i:i + n], T.ic[:, 0:n], ["ic"], ["selz%d" % i], n, None, 0.0)
     act(T.tab[:, 2080:TW], T.ic[:, 0:16], ["ic"], ["tabz"], 16, None, 0.0)
     act(T.yp[:, 2048:2080], T.ic[:, 0:32], ["ic"], ["ypz"], 32, None, 0.0)
-    act(T.ones[:], T.ic[:, 0:128], ["ic"], ["ones"], 128, None, 0.0, 1.0)
     act(T.onesn[:], T.ic[:, 0:128], ["ic"], ["onesn"], 128, None, 0.0, 0.0078125)
     act(T.cpool[0:64, 0:240], T.ic[0:64, :], ["ic"], ["cpool"], 240, None, 0.0, 4096.0)
     act(T.cpool[0:64, 240:256], T.ic[0:64, 0:16], ["ic"], ["cpool"], 16, None, 0.0, 4096.0)
     act(T.m4eye[:], T.eyeb[:], ["eyeb"], ["m4eye"], 128, None, -4.0)
     ts(T.sel[:, 0:2048:16], T.i8[:], D16, 4096.0, EQ, OP.mult, ["i8", "pf"] + selz, ["sel"], 128)
     ts(T.enc16[:], T.ienc[:], P16, None, OP.add, None, ["ienc", "pf"], ["enc16"], 128)
-    ts(T.meye16[:], ic0, PC, -1.0, EQ, OP.mult, ["ic", "pcol"], ["meye16"], 128)
-    for j in range(3):
-        ts(T.r384[:, 128 * j:128 * j + 128], T.i8[:], P8, -1.0 if j else 1.0, EQ, OP.mult, ["i8", "pf"], ["r384"], 128)
+    ts(T.meye16[:], T.eye16[:], -1.0, None, OP.mult, None, ["eye16"], ["meye16"], 64)
+    ts(T.rf[:], T.i8[:], P8, None, EQ, None, ["i8", "pf"], ["rf"], 128)
+    for j in range(2):
+        ts(T.r256[:, 128 * j:128 * j + 128], T.rf[:], -1.0, None, OP.mult, None, ["rf"], ["r256"], 128)
     boost[0] = EARLY
     cp(T.dt_[:], T.dm_i[:], ["dm_i"], ["dt"], 128)
     ts(T.wcol[:], T.wt_i[:], 2.0, None, OP.mult, None, ["wt_i"], ["wcol"], 1)
@@ -181,12 +188,12 @@ def rank_program(g, core, T, topo):
         for a in range(16):
             mm(T.b7[:, 128:136], T.wsel[:, 127 * a:127 * a + 128], T.dt_[:, a:128:16], a == 0, a == 15,
                ["wsel", "dt"], ["B7.e"], 8)
-        cp(T.e1[:], T.b7[:, 128:136], ["B7.e"], ["e1"], 8)
-        ts(T.e2[:], T.e1[:], 2046, None, OP.bitwise_and, None, ["e1"], ["e2"], 8)
-        do("V", lambda: v.tensor_scalar(T.e33[:], T.e2[:].indirect(T.bc[:, 0:4]), 1.0, 33.0, OP.mult, OP.add),
+        act(T.e1[:], T.b7[:, 128:136], ["B7.e"], ["e1"], 8, None, 1.0, EOFF - 1023.0)
+        tt(T.e2[:], T.b7[:, 128:136], T.e1[:], OP.subtract, ["B7.e", "e1"], ["e2"], 8)
+        do("V", lambda: v.tensor_scalar(T.e33[:], T.e2[:].indirect(T.bc[:, 0:4]), 1.0, EOFF + 33.0, OP.mult, OP.add),
            ["e2", "bc"], ["e33"], gat(64))
         for i in range(4):
-            act(T.b7[:, 144 + 64 * i:208 + 64 * i], T.e33[:], ["e33"], ["B7.e%d" % i], 64)
+            act(T.e33w[:, 64 * i:64 * i + 64], T.e33[:], ["e33"], ["e33w%d" % i], 64)
 
     def spread_d(fused=True):
         for i in range(4):
@@ -196,20 +203,15 @@ def rank_program(g, core, T, topo):
 
     def index(cards, ck, qb, fb, n0, n1, outs, nm):
         s, n = slice(n0, n1), n1 - n0
-        ek = ["B7.e%d" % i for i in range((n + 63) // 64)]
-        if nm == "oa":
-            tt(qb[:, s], cards, T.e33[:], OP.mult, [ck, "e33"], [nm + "q"], 2 * n)
+        ek = ["e33w%d" % i for i in range((n + 63) // 64)]
+        cyc = n if ck[0] == "B" else 2 * n
+        if n == 64:
+            tt(qb[:, s], cards, T.e33[:], OP.mult, [ck, "e33"], [nm + "q"], cyc)
         else:
-            tt(qb[:, s], cards, T.b7[:, 144:144 + n], OP.mult, [ck] + ek, [nm + "q"], n)
+            tt(qb[:, s], cards, T.e33w[:, 0:n], OP.mult, [ck] + ek, [nm + "q"], cyc)
         ts(fb[:, s], qb[:, s], 5, 2047, OP.arith_shift_right, OP.bitwise_and, [nm + "q"], [nm + "f"], n)
         for out, z, key in outs:
-            if z is None:
-                ts(out[:, s], fb[:, s], T.kf[:], None, OP.add, None, [nm + "f", "kf"], [key], n)
-            else:
-                ts(out[:, s], fb[:, s], T.kf[:], z, OP.add, OP.add, [nm + "f", "kf"], [key], n)
-
-    def ocards(t):
-        return T.o16[:, 256 * (t % 2):256 * (t % 2) + 256], "o16.%d" % (t % 2)
+            ts(out[:, s], fb[:, s], T.kf[:], KOFF + z, OP.add, OP.add, [nm + "f", "kf"], [key], n)
 
     def block(x, y, off, base, pieces, nm, uk):
         keys = []
@@ -233,9 +235,8 @@ def rank_program(g, core, T, topo):
             mm(out, T.sel[:, 127 * a:127 * a + 128], y[:, base + a:base + 1024:16], False, a == 15, ["sel"] + keys, [k], 64)
 
     def pools(t, share):
-        o, ok = ocards(t)
-        index(o[:, 0:64], ok, T.oq, T.of, 0, 64, [(T.ou, None, "oua")], "oa")
-        index(o[:, 64:256], ok, T.oq, T.of, 64, 256, [(T.ou, None, "oub")], "ob")
+        index(T.b3[:, 0:64], "B3.o", T.oq, T.of, 0, 64, [(T.ou, 0.0, "oua")], "oa")
+        index(T.b3[:, 64:256], "B3.o", T.oq, T.of, 64, 256, [(T.ou, 0.0, "oub")], "ob")
         for c in range(4):
             keys = block(T.xo, T.yo_, T.ou, 1024 * c, share[c], "o", "oub" if c else "oua")
             scores(T.b0[:, 64 * c:64 * c + 64], "B0.s", T.cpool[:, 64 * c:64 * c + 64], T.onesn[:], ["onesn", "cpool"],
@@ -249,9 +250,24 @@ def rank_program(g, core, T, topo):
         tt(T.p16[:], T.p32[:, 0:16], T.p32[:, 16:32], OP.min, ["p32"], ["p16"], 32)
         tt(T.omin[:], T.p16[:, 0:8], T.p16[:, 8:16], OP.min, ["p16"], ["omin"], 16)
 
+    def pool_card(t):
+        actg(T.thr2[:], T.omin[:].indirect(T.bc[:]), ["omin", "bc"], ["thr2"], 256)
+        tt(T.oh[:, 128:384], T.b0[:, 0:256], T.thr2[:], EQ, ["B0.s", "thr2"], ["oho"], 256)
+        tt(T.com[:, 128:384], T.oh[:, 128:384], T.b3[:, 0:256], OP.mult, ["oho", "B3.o"], ["com"], 256)
+        mm(T.b3[:, 0:256], T.eye16[:], T.o16[:], True, False, ["eye16", "o16"], ["B3.o"], 256)
+        for u in range(t):
+            mm(T.b3[:, 0:256], T.eye16[:], T.to16[:, 256 * u:256 * u + 256], False, False, ["eye16", "to%d" % u],
+               ["B3.o"], 256)
+        for j in range(2):
+            mm(T.b6[:, 0:128], T.com[:, 128 + 128 * j:256 + 128 * j], T.eye16[:], j == 0, j == 1, ["com", "eye16"],
+               ["B6.t0"], 128)
+        act(T.tco[:], T.b6[:, 0:128], ["B6.t0"], ["tco"], 128)
+        mm(T.b2[:, 128:256], T.tco[:], T.rf[:], True, False, ["tco", "rf"], ["B2.w"], 512)
+        mm(T.b2[:, 128:256], T.meye16[:], T["c%d" % t][:], False, True, ["meye16", "c%d" % t], ["B2.w"], 128)
+
     def pack_index(t):
         boost[0] = 5.0
-        index(T["c%d" % t][:], "c%d" % t, T.pq, T.pfc, 0, 128, [(T.pu, None, "pu")], "p")
+        index(T.b4[:, 0:128], "B4.c", T.pq, T.pfc, 0, 128, [(T.pu, 0.0, "pu")], "p")
         boost[0] = 0.0
 
     def packs(t, share):
@@ -272,10 +288,6 @@ def rank_program(g, core, T, topo):
     def pack_to_psum(t):
         mm(T.b4[:, 0:128], T.eye16[:], T["c%d" % t][:], True, True, ["eye16", "c%d" % t], ["B4.c"], 128)
 
-    def pools_to_psum(t):
-        o, ok = ocards(t)
-        mm(T.b4[:, 128:384], T.eye16[:], o, True, True, ["eye16", ok], ["B4.o"], 256)
-
     def send(t):
         rid, pid, _ = topo.addr(nxt)
         m = 0
@@ -291,11 +303,9 @@ def rank_program(g, core, T, topo):
         mo = ["m1", "omin"]
         tt(T.thi[:], T.m1[:], T.omin[:], OP.max, mo, ["thi"], 16)
         tt(T.thf[:], T.m1[:], T.omin[:], OP.max, mo, ["thf"], 16)
-        tt(T.th2[:], T.m1[:], T.omin[:], OP.min, mo, ["th2"], 16)
         ts(T.offi[:], T.thi[:], 4095, None, OP.bitwise_and, None, ["thi"], ["offi"], 8)
         cp(T.offu[:], T.offi[:], ["offi"], ["offu"], 8)
-        actg(T.thr[:], T.thf[:].indirect(T.bc[:]), ["thf", "bc"], ["thr"], 128)
-        actg(T.thr2[:], T.th2[:].indirect(T.bc[:]), ["th2", "bc"], ["thr2"], 128)
+        actg(T.thr[:], T.thf[:].indirect(T.bc[:, 0:8]), ["thf", "bc"], ["thr"], 128)
         ttg(T.gt[:], T.yp[:].indirect(T.offu[:]), T.dt_[:], OP.is_ge, ykeys + ["ypz", "offu", "dt"], ["gt"], 128)
         mm(T.b7[:, 0:128], T.eyeb[:], T.dt_[:], True, False, ["eyeb", "dt"], ["B7.d"], 128)
         mm(T.b7[:, 0:128], T.m4eye[:], T.gt[:], False, True, ["m4eye", "gt"], ["B7.d"], 128)
@@ -304,31 +314,25 @@ def rank_program(g, core, T, topo):
             act(T.yd_f[:], T.dt_[:], ["dt"], ["yd_f"], 128)
             store("Y", "st_yd", T.yd[:], T.yd_f[:], ["yd_f"])
         tt(T.oh[:, 0:128], T.b1[:, 0:128], T.thr[:], OP.is_ge, ["B1.s0", "B1.s1", "thr"], ["ohc"], 128)
-        for c in range(2):
-            tt(T.oh[:, 128 + 128 * c:256 + 128 * c], T.b0[:, 128 * c:128 * c + 128], T.thr2[:], OP.is_le,
-               ["B0.s", "thr2"], ["oho%d" % c], 128)
-        ohk = ["ohc", "oho0", "oho1"]
-        tt(T.com[:], T.oh[:], T.b4[:, 0:384], OP.mult, ohk + ["B4.c", "B4.o"], ["com"], 384)
-        for j in range(3):
-            mm(T.b6[:, 0:128], T.com[:, 128 * j:128 * j + 128], (T.eye16 if j else T.meye16)[:], j == 0, j == 2,
-               ["com", "eye16", "meye16"], ["B6.t"], 128)
+        tt(T.com[:, 0:128], T.oh[:, 0:128], T.b2[:, 128:256], OP.mult, ["ohc", "B2.w"], ["tuc"], 128)
+        tt(T["n%d" % t][:], T.com[:, 0:128], T.b4[:, 0:128], OP.add, ["tuc", "B4.c"], ["n%d" % t], 128)
+        if not last:
+            send(t)
+        mm(T.b6[:, 128:256], T.com[:, 0:128], T.eye16[:], True, True, ["tuc", "eye16"], ["B6.t"], 128)
         if not last:
             mm(T.b2[:, 0:128], T.ones[:], T.oh[:, 0:128], True, True, ["ones", "ohc"], ["B2.k"], 128)
             act(T.cscr[:], T.b2[:, 0:128], ["B2.k"], ["cnt", "cscr"], 128, T.cnt[:])
-            ts(T.kr[:], T.cnt[:], 0.03125, -0.484375, OP.mult, OP.add, ["cnt"], ["kr"], 1)
-            ts(T.kf[:], T.kr[:], -32.0, T.cnt[:], OP.mult, OP.add, ["kr", "cnt"], ["kf"], 1)
+            act(T.kr[:], T.cnt[:], ["cnt"], ["kr"], 1, None, 1.0, KOFF - 15.5)
+            do("A", lambda: a_.activation(T.kf[:], T.kr[:], AF.Identity, bias=T.cnt[:], scale=-1.0), ["kr", "cnt"],
+               ["kf"], vec(1))
             seats_e()
-        cp(T.tc16[:], T.b6[:, 0:128], ["B6.t"], ["tc16"], 128)
-        mm(T.b6[:, 128:512], T.tc16[:], T.r384[:], True, True, ["tc16", "r384"], ["B6.d"], 384)
-        tt(T.b3[:, 0:384], T.oh[:], T.b6[:, 128:512], OP.mult, ohk + ["B6.d"], ["B3.u"], 384)
-        tt(T["n%d" % t][:], T["c%d" % t][:], T.b3[:, 0:128], OP.add, ["c%d" % t, "B3.u"], ["n%d" % t], 128)
-        o, ok = ocards(t)
-        on, onk = ocards(t + 1)
-        tt(on, o, T.b3[:, 128:384], OP.add, [ok, "B3.u"], [onk], 256)
+        cp(T.tc16[:], T.b6[:, 128:256], ["B6.t"], ["tc16"], 128)
+        mm(T.b6[:, 256:512], T.tc16[:], T.r256[:], True, True, ["tc16", "r256"], ["B6.d"], 256)
+        to = T.to16[:, 256 * t:256 * t + 256]
+        tt(to, T.oh[:, 128:384], T.b6[:, 256:512], OP.mult, ["oho", "B6.d"], ["to%d" % t], 256)
+        mm(T.b3[:, 0:256], T.eye16[:], to, False, True, ["eye16", "to%d" % t], ["B3.o"], 256)
         if not last:
-            send(t)
             spread_d(t < NV - 2)
-            pools_to_psum(t + 1)
 
     Q = [T.q3[:, 128 * i:128 * i + 128] for i in range(3)]
     RW = [T.rw3[:, 1024 * i:1024 * i + 1024] for i in range(3)]
@@ -344,54 +348,61 @@ def rank_program(g, core, T, topo):
     cp(T.q3[:], T.b0[:, 0:384], ["B0.q0", "B0.q1", "B0.q2"], ["q3"], 384)
     for b in range(8):
         ts(T.rw3[:, b:3072:8], T.q3[:], T.mb[:, b:b + 1], None, OP.mult, None, ["q3", "mb"], ["rw%d" % b], 192)
-    for i, (out, k) in enumerate([(T.b4[:, 0:128], "B4.c"), (T.b3[:, 0:128], "B3.a"), (T.b3[:, 128:256], "B3.b")]):
+    for i, (out, k) in enumerate([(T.b4[:, 0:128], "B4.c"), (T.b3[:, 0:128], "B3.o"), (T.b3[:, 128:256], "B3.o")]):
         for x in range(8):
             mm(out, T.zb[:, 112 - 16 * x:240 - 16 * x], T.rw3[:, 1024 * i + 128 * x:1024 * i + 128 * x + 128],
                x == 0, x == 7, ["zb"] + ["rw%d" % b for b in range(8)], [k], 128)
     cp(T.c0[:], T.b4[:, 0:128], ["B4.c"], ["c0"], 128)
     spread_d()
     pack_index(0)
-    cp(T.o16[:, 0:256], T.b3[:, 0:256], ["B3.a", "B3.b"], ["o16.0"], 256)
-    pools_to_psum(0)
+    cp(T.o16[:], T.b3[:, 0:256], ["B3.o"], ["o16"], 256)
 
     for t in range(NV - 1):
         share = SHARE
-        if t:
-            pack_to_psum(t)
         pools(t, share)
         pool_min()
+        pool_card(t)
         if t:
+            pack_to_psum(t)
             pack_index(t)
         exchange(t, packs(t, share))
 
     t = NV - 1
 
     def chain(off, okey, y, acc, half, out, key):
-        for i in range(3):
+        two = key == "cb"
+        for i in range(2 if two else 3):
             actg(y[:, 512 * i:512 * i + 512], win.indirect(off[:, 32 * i:32 * i + 32]), tabk + [okey], [key + "g%d" % i], 512)
         ttg(acc[0][:], win.indirect(off[:, 96:128]), y[:, 0:512], OP.max, tabk + [okey, key + "g0"], [key + "0"], 512)
-        for i, b in ((1, T.b2), (2, T.b3)):
-            bk = "B%d.%s" % (i + 1, key)
-            mm(b[:], T.eyeb[:], y[:, 512 * i:512 * i + 512], True, True, ["eyeb", key + "g%d" % i], [bk], 512)
-            tt(acc[i % 2][:], acc[1 - i % 2][:], b[:], OP.max, [key + str(1 - i % 2), bk], [key + str(i % 2)], 512)
-        acc = [acc[1], acc[0]]
-        tt(half[:], acc[1][:, 0:256], acc[1][:, 256:512], OP.max, [key + "0"], [key + "h"], 512)
-        tt(out[:], half[:, 0:128], half[:, 128:256], OP.max, [key + "h"], [key + "m"], 256)
-    index(T.n0[:], "n0", T.mq, T.mfc, 0, 128, [(T.mu, None, "mu"), (T.mz, -float(ZC), "mz")], "m")
-    chain(T.mu, "mu", T.yb, [T.acc0, T.acc1], T.bh, T.bmax, "cb")
+        if two:
+            ttg(acc[1][:], win.indirect(off[:, 64:96]), acc[0][:], OP.max, tabk + [okey, key + "0"], [key + "1"], 512)
+        for i, b in ((2, T.b6),) if two else ((1, T.b2), (2, T.b6)):
+            bk = ("B2." if i == 1 else "B6.") + key
+            q = i - 1 if two else i
+            mm(b[:], T.eyeb[:], y[:, 512 * q:512 * q + 512], True, True, ["eyeb", key + "g%d" % q], [bk], 512)
+            if i == 1:
+                tt(acc[1][:], acc[0][:], b[:], OP.max, [key + "0", bk], [key + "1"], 512)
+            else:
+                tt(acc[0][:, 0:256], acc[1][:, 0:256], b[:, 0:256], OP.max, [key + "1", bk], [key + "2"], 256)
+                tt(T.b0[:, 0:256], acc[1][:, 256:512], b[:, 256:512], OP.max, [key + "1", bk], ["B0." + key], 256)
+        tt(half[:], acc[0][:, 0:256], T.b0[:, 0:256], OP.max, [key + "2", "B0." + key], [key + "h"], 256)
+        tt(out[0], half[:, 0:128], half[:, 128:256], OP.max, [key + "h"], [out[1]], 256)
+    index(T.n0[:], "n0", T.mq, T.mfc, 0, 128, [(T.mu, 0.0, "mu"), (T.mz, -float(ZC), "mz")], "m")
+    chain(T.mu, "mu", T.yb, [T.acc0, T.acc1], T.bh, (T.b1[:, 0:128], "B1.bm"), "cb")
     pack_to_psum(t)
     pack_index(t)
-    tt(T.stay[:], T.n0[:], T.b4[:, 0:128], EQ, ["n0", "B4.c"], ["stay"], 128)
-    tt(T.sz[:], T.stay[:], T.mz[:], OP.mult, ["stay", "mz"], ["sz"], 256)
+    tt(T.b4[:, 128:256], T.n0[:], T.b4[:, 0:128], EQ, ["n0", "B4.c"], ["B4.stay"], 128)
+    tt(T.sz[:], T.b4[:, 128:256], T.mz[:], OP.mult, ["B4.stay", "mz"], ["sz"], 128)
     ts(T.au[:], T.sz[:], float(ZC), None, OP.add, None, ["sz"], ["au"], 128)
-    chain(T.au, "au", T.ya, [T.acc2, T.acc3], T.ah, T.amax, "ca")
-    tt(T.up[:], T.amax[:], T.bmax[:], OP.is_ge, ["cam", "cbm"], ["up"], 256)
-    ts(T.up8[:], T.up[:], 16.0, -8.0, OP.mult, OP.add, ["up"], ["up8"], 64)
-    tt(T.dsum[:], T.dt_[:], T.up8[:], OP.add, ["dt", "up8"], ["dsum"], 256)
+    chain(T.au, "au", T.ya, [T.acc2, T.acc3], T.ah, (T.amax[:], "cam"), "ca")
+    tt(T.up[:], T.amax[:], T.b1[:, 0:128], OP.is_ge, ["cam", "B1.bm"], ["up"], 128)
+    ts(T.b4[:, 384:512], T.up[:], 16.0, -8.0, OP.mult, OP.add, ["up"], ["B4.up8"], 128)
+    tt(T.dsum[:], T.dt_[:], T.b4[:, 384:512], OP.add, ["dt", "B4.up8"], ["dsum"], 128)
     ts(T.dt_[:], T.dsum[:], 1.0, 255.0, OP.max, OP.min, ["dsum"], ["dt"], 128)
     spread_d(False)
     pools(t, [FULL] * 6)
     pool_min()
+    pool_card(t)
     exchange(t, packs(t, [FULL] * 6))
 
     ts(T.permf16[:], T.ipermf[:], PC, None, EQ, None, ["ipermf", "pcol"], ["permf16"], 128)
@@ -411,7 +422,8 @@ def rank_program(g, core, T, topo):
             mm(out, z[:, 112 - 16 * x:240 - 16 * x], RW[i][:, x:1024:8], x == 0, x == 7,
                [zk] + ["rx%d%d" % (i, b) for b in range(8)], [ok], 128)
         act(dst, out, [ok], [dk], 128)
-    oe, oek = ocards(NV)
+    oe, oek = T.o16[:], "o16"
+    cp(oe, T.b3[:, 0:256], ["B3.o"], [oek], 256)
     seats_to_list(0, T["n%d" % t][:], "n%d" % t, T.zfp, "zfp", T.b4[:, 0:128], "B4.y", T.yc_f[:], "yc_f")
     seats_to_list(1, oe[:, 0:128], oek, T.zfo, "zfo", T.b5[:, 0:128], "B5.y", T.yo_f[:, 0:256:2], "yo_f0")
     seats_to_list(2, oe[:, 128:256], oek, T.zfo, "zfo", T.b7[:, 0:128], "B7.y", T.yo_f[:, 1:256:2], "yo_f1")

from concourse.bass import DstId, RemoteDMATransfer
from concourse.mybir import dt, AluOpType, AxisListType, ActivationFunctionType

OP = AluOpType
AF = ActivationFunctionType
NV = 6
ZC = 2080
TW = 2096
KOFF = 4128.0
EOFF = 264192.0
FULL = [(0, 512), (512, 1024)]
PART = [(0, 512)]
SHARE = [PART, PART, FULL, PART, FULL, PART]


def sb(n, d):
    return ("sbuf", [128, n], d)


F32, B16, F16, I32, U16 = "float32", "bfloat16", "float16", "int32", "uint16"
SCRATCH = {
    "pk_i": sb(128, I32), "po_i": sb(256, I32), "dm_i": sb(128, I32), "wt_i": sb(1, I32), "tab": sb(TW, B16),
    "ic": sb(240, F32), "i8": sb(128, F32), "iperm": sb(128, F32), "ipermf": sb(128, F32), "ienc": sb(128, F32),
    "ip": sb(1, I32), "pint": sb(4, I32), "pf": sb(4, F32), "pcol": sb(1, F32), "prev": sb(1, F32),
    "eye16": sb(128, F16), "meye16": sb(128, F16), "r256": sb(256, F16), "perm16": sb(128, F16),
    "permf16": sb(128, F16), "zb": sb(240, F16), "zfp": sb(240, F16), "zfo": sb(240, F16),
    "enc16": sb(128, F16), "cpool": sb(256, B16), "onesn": sb(128, B16), "mb": sb(8, F32), "mf": sb(8, F32),
    "bc": sb(16, U16), "eyeb": sb(128, B16), "m4eye": sb(128, B16), "ones": sb(128, B16),
    "sel": sb(2048, B16), "wsel": sb(2048, B16), "wcol": sb(1, F32),
    "pk16": sb(128, F16), "poa16": sb(128, F16), "pob16": sb(128, F16),
    "q3": sb(384, F16), "rw3": sb(3072, F16), "ya": sb(2048, B16), "yb": sb(2048, B16),
    "o16": sb(256, F16), "to16": sb(256 * NV, F16),
    "dt_": sb(128, B16), "dt2": sb(512, B16),
    "e1": sb(8, B16), "e2": sb(8, F32), "e33": sb(64, F32), "e33w": sb(256, F32),
    "kf": sb(1, F32), "kr": sb(1, B16), "cnt": sb(1, F32), "cscr": sb(128, F32),
    "oq": sb(256, I32), "of": sb(256, I32), "ou": sb(256, U16),
    "pq": sb(128, I32), "pfc": sb(128, I32), "pu": sb(128, U16),
    "xo": sb(4096, B16), "yo_": sb(4096, B16), "xp": sb(2048, B16), "yp": sb(2080, B16),
    "losb": sb(64, F32), "w64": sb(64, F32), "w32": sb(32, F32), "w16": sb(16, F32), "m1": sb(8, F32),
    "sohi": sb(128, F32), "p128": sb(128, F32), "p64": sb(64, F32), "p32": sb(32, F32), "p16": sb(16, F32),
    "omin": sb(8, F32),
    "thi": sb(8, I32), "offi": sb(8, I32), "offu": sb(8, U16), "thf": sb(8, F32), "tco": sb(128, F32), "rf": sb(128, F32),
    "thr": sb(128, F32), "thr2": sb(256, F32), "gt": sb(128, B16),
    "oh": sb(384, B16), "com": sb(384, F16), "tc16": sb(128, F16),
    "mq": sb(128, I32), "mfc": sb(128, I32), "mu": sb(128, U16), "mz": sb(128, F32),
    "stay": sb(128, F32), "sz": sb(128, F32), "au": sb(128, U16),
    "acc0": sb(512, B16), "acc1": sb(512, B16), "acc2": sb(512, B16), "acc3": sb(512, B16),
    "ah": sb(256, B16), "bh": sb(256, B16), "amax": sb(128, B16), "bmax": sb(128, B16),
    "up": sb(128, B16), "up8": sb(128, B16), "dsum": sb(128, F32),
    "yc_f": sb(128, F32), "yo_f": sb(256, F32), "yd_f": sb(128, F32),
}
for _t in range(NV):
    SCRATCH["c%d" % _t] = sb(128, F16)
    SCRATCH["n%d" % _t] = sb(128, F16)
for _b in range(8):
    SCRATCH["b%d" % _b] = ("psum", [128, 512], F32)

LOADS = ["ld_pk", "ld_po", "ld_dm", "ld_wt", "ld_xt"]
STORES = ["st_yc", "st_yo", "st_yd"]
ARR = ["arr%d" % t for t in range(1, NV)]
SEMAPHORES = ["sv", "sa", "sp", "sg", "loc"] + LOADS + STORES + ARR

CYC, PCYC, CALL, HOP, GATH, WIRE = 0.00091, 0.00079, 0.05, 0.06, 1.5, 4.0


EARLY = 4.0
BOOST = {"cb": -8, "B2.w": 4, "rf": -1, "B2.k": 1, "B7.e": 4, "B5.d": 1, "mu": -2, "up": 1, "B3.o": -1, "B1.s": 2,
         "obf": -8, "e": -4, "thi": 2, "omin": 4, "thf": -8, "dt": -4, "eye16": -2, "c": 4, "p": 4, "perm16": -2,
         "offi": -4, "zfo": 2}


def rank_program(g, core, T, topo):
    rank = T.rank_of(core)
    if rank is None:
        return
    nxt = T.cores[(rank + 1) % len(T.cores)]
    NENG = 8
    queues = {"V": g.vector, "A": g.scalar, "P": g.tensor, "G": g, "Y": g.sync}
    counters = {"V": "sv", "A": "sa", "P": "sp", "G": "sg"}
    v, a_, pe = g.vector, g.scalar, g.tensor
    boost, boosts = [0.0], []
    ops = []

    def do(eng, call, reads, writes, dur, lat=0.0, tok=None):
        ops.append((eng, call, reads, writes, dur, lat, tok))
        boosts.append(boost[0] + BOOST.get(writes[0].rstrip("012345") if writes else "", 0.0))

    def vec(n):
        return CALL + max(64, n) * CYC

    def gat(n):
        return 0.05 + n * GATH * CYC

    def tt(out, x, y, op, r, w, n):
        do("V", lambda: v.tensor_tensor(out, x, y, op), r, w, vec(n))

    def ttg(out, x, y, op, r, w, n):
        do("V", lambda: v.tensor_tensor(out, x, y, op), r, w, gat(n))

    def ts(out, x, s1, s2, op0, op1, r, w, n):
        if op1 is None:
            do("V", lambda: v.tensor_scalar(out, x, s1, None, op0), r, w, vec(n))
        else:
            do("V", lambda: v.tensor_scalar(out, x, s1, s2, op0, op1), r, w, vec(n))

    def cp(out, x, r, w, n):
        do("V", lambda: v.tensor_copy(out, x), r, w, vec(n))

    def fill(ap, c, w, n):
        do("V", lambda: v.memset(ap, c), [], w, vec(n))

    def act(out, x, r, w, n, acc=None, scale=1.0, bias=0.0, func=AF.Copy):
        do("A", lambda: a_.activation(out, x, func, bias=bias, scale=scale, accum_out=acc), r, w, vec(n))

    def actg(out, x, r, w, n):
        do("A", lambda: a_.activation(out, x, AF.Copy), r, w, gat(n) + 0.015)

    def mm(out, l, x, st, sp, r, w, n):
        do("P", lambda: pe.matmul(out, l, x, st, sp), r, w, max(64, n) * PCYC)

    def load(eng, sem, out, x, w, lat):
        do(eng, lambda: queues[eng].dma_start(out, x).then_inc(T.sem[sem], 16), [], [w], 0.1, lat, (sem, 16))

    def store(eng, sem, out, x, r):
        do(eng, lambda: queues[eng].dma_start(out, x).then_inc(T.sem[sem], 16), r, [], 0.1, 2.0, (sem, 16))

    load("Y", "ld_pk", T.pk_i[:], T.pk[:], "pk_i", 2.0)
    load("A", "ld_po", T.po_i[:], T.po[:], "po_i", 2.3)
    load("Y", "ld_dm", T.dm_i[:], T.dm[:], "dm_i", 2.0)
    load("A", "ld_wt", T.wt_i[:], T.wt[:], "wt_i", 2.0)
    load("Y", "ld_xt", T.tab[:, 0:2048], T.xt[:], "tab", 3.5)

    def iota(out, pat, base, cm, w, n, small=True):
        if small:
            do("G", lambda: g.iota(out, pat, base, cm, allow_small_or_imprecise_dtypes=True), [], w, 0.13 + 2 * n * CYC)
        else:
            do("G", lambda: g.iota(out, pat, base, cm), [], w, 0.13 + 2 * n * CYC)
    iota(T.ip[:], [[0, 1]], 0, 1, ["ip"], 1, False)
    iota(T.i8[:], [[0, 16], [1, 8]], 0, 0, ["i8"], 128)
    iota(T.ic[:], [[1, 240]], -112, 0, ["ic"], 240)
    iota(T.iperm[:], [[16, 8], [-1, 16]], 15, 0, ["iperm"], 128)
    iota(T.ienc[:], [[128, 16], [16, 8]], 0, 0, ["ienc"], 128)
    iota(T.cpool[:], [[2, 32], [0, 8]], 0, 0, ["cpool"], 256)
    iota(T.ipermf[:], [[1, 16], [16, 8]], 0, 0, ["ipermf"], 128)
    fill(T.wsel[:], 0.0, ["wsel"], 1024)
    fill(T.kf[:], -KOFF, ["kf"], 1)
    for j, (op, s) in enumerate([(OP.bitwise_and, 15), (OP.bitwise_and, 7),
                                 (OP.arith_shift_right, 4), (OP.arith_shift_right, 3)]):
        ts(T.pint[:, j:j + 1], T.ip[:], s, None, op, None, ["ip"], ["pint%d" % j], 1)
    cp(T.pcol[:], T.ip[:], ["ip"], ["pcol"], 1)
    cp(T.pf[:], T.pint[:], ["pint%d" % j for j in range(4)], ["pf"], 4)
    ic0 = T.ic[:, 112:240]
    P16, P8, D16, D8 = (T.pf[:, j:j + 1] for j in range(4))
    PC, EQ = T.pcol[:], OP.is_equal
    ts(T.mb[:], T.i8[:, 0:8], D16, None, EQ, None, ["i8", "pf"], ["mb"], 8)
    ts(T.zb[:], T.ic[:], P16, None, EQ, None, ["ic", "pf"], ["zb"], 240)
    act(T.ones[:], T.ic[:, 0:128], ["ic"], ["ones"], 128, None, 0.0, 1.0)
    do("G", lambda: g.affine_select(T.eyeb[:], T.ones[:], [[-1, 128]], EQ, 0.0, 0, 1), ["ones"], ["eyeb"], 0.4)
    ts(T.eye16[:], ic0, PC, None, EQ, None, ["ic", "pcol"], ["eye16"], 128)
    ts(T.bc[:], T.i8[:, 0:16], 0.0, P8, OP.mult, OP.add, ["i8", "pf"], ["bc"], 16)
    ts(T.perm16[:], T.iperm[:], PC, None, EQ, None, ["iperm", "pcol"], ["perm16"], 128)
    selz = ["selz%d" % i for i in range(0, 2048, 240)]
    for i in range(0, 2048, 240):
        n = min(240, 2048 - i)
        act(T.sel[:, i:i + n], T.ic[:, 0:n], ["ic"], ["selz%d" % i], n, None, 0.0)
    act(T.tab[:, 2080:TW], T.ic[:, 0:16], ["ic"], ["tabz"], 16, None, 0.0)
    act(T.yp[:, 2048:2080], T.ic[:, 0:32], ["ic"], ["ypz"], 32, None, 0.0)
    act(T.onesn[:], T.ic[:, 0:128], ["ic"], ["onesn"], 128, None, 0.0, 0.0078125)
    act(T.cpool[0:64, 0:240], T.ic[0:64, :], ["ic"], ["cpool"], 240, None, 0.0, 4096.0)
    act(T.cpool[0:64, 240:256], T.ic[0:64, 0:16], ["ic"], ["cpool"], 16, None, 0.0, 4096.0)
    act(T.m4eye[:], T.eyeb[:], ["eyeb"], ["m4eye"], 128, None, -4.0)
    ts(T.sel[:, 0:2048:16], T.i8[:], D16, 4096.0, EQ, OP.mult, ["i8", "pf"] + selz, ["sel"], 128)
    ts(T.enc16[:], T.ienc[:], P16, None, OP.add, None, ["ienc", "pf"], ["enc16"], 128)
    ts(T.meye16[:], T.eye16[:], -1.0, None, OP.mult, None, ["eye16"], ["meye16"], 64)
    ts(T.rf[:], T.i8[:], P8, None, EQ, None, ["i8", "pf"], ["rf"], 128)
    for j in range(2):
        ts(T.r256[:, 128 * j:128 * j + 128], T.rf[:], -1.0, None, OP.mult, None, ["rf"], ["r256"], 128)
    boost[0] = EARLY
    cp(T.dt_[:], T.dm_i[:], ["dm_i"], ["dt"], 128)
    ts(T.wcol[:], T.wt_i[:], 2.0, None, OP.mult, None, ["wt_i"], ["wcol"], 1)
    ts(T.wsel[:, 0:2048:16], T.i8[:], D16, T.wcol[:], EQ, OP.mult, ["i8", "pf", "wcol", "wsel"], ["wsel"], 128)
    boost[0] = 0.0
    act(T.tab[:, 2048:2080], T.tab[:, 0:32], ["tab"], ["tabx"], 32)
    tabk = ["tab", "tabx", "tabz"]
    win = T.tab[:, 0:TW]

    def seats_e():
        for a in range(16):
            mm(T.b7[:, 128:136], T.wsel[:, 127 * a:127 * a + 128], T.dt_[:, a:128:16], a == 0, a == 15,
               ["wsel", "dt"], ["B7.e"], 8)
        act(T.e1[:], T.b7[:, 128:136], ["B7.e"], ["e1"], 8, None, 1.0, EOFF - 1023.0)
        tt(T.e2[:], T.b7[:, 128:136], T.e1[:], OP.subtract, ["B7.e", "e1"], ["e2"], 8)
        do("V", lambda: v.tensor_scalar(T.e33[:], T.e2[:].indirect(T.bc[:, 0:4]), 1.0, EOFF + 33.0, OP.mult, OP.add),
           ["e2", "bc"], ["e33"], gat(64))
        for i in range(4):
            act(T.e33w[:, 64 * i:64 * i + 64], T.e33[:], ["e33"], ["e33w%d" % i], 64)

    def spread_d(fused=True):
        for i in range(4):
            mm(T.b5[:, 128 * i:128 * i + 128], T.eyeb[:], T.dt_[:], True, True, ["eyeb", "dt"], ["B5.d"], 128)
        if fused:
            act(T.dt2[:], T.b5[:], ["B5.d", "e33"], ["dt2"], 512)

    def index(cards, ck, qb, fb, n0, n1, outs, nm):
        s, n = slice(n0, n1), n1 - n0
        ek = ["e33w%d" % i for i in range((n + 63) // 64)]
        cyc = n if ck[0] == "B" else 2 * n
        if n == 64:
            tt(qb[:, s], cards, T.e33[:], OP.mult, [ck, "e33"], [nm + "q"], cyc)
        else:
            tt(qb[:, s], cards, T.e33w[:, 0:n], OP.mult, [ck] + ek, [nm + "q"], cyc)
        ts(fb[:, s], qb[:, s], 5, 2047, OP.arith_shift_right, OP.bitwise_and, [nm + "q"], [nm + "f"], n)
        for out, z, key in outs:
            ts(out[:, s], fb[:, s], T.kf[:], KOFF + z, OP.add, OP.add, [nm + "f", "kf"], [key], n)

    def block(x, y, off, base, pieces, nm, uk):
        keys = []
        end = base + pieces[-1][1]
        for lo, hi in pieces:
            lo, hi = lo + base, hi + base
            actg(x[:, lo:hi], win.indirect(off[:, lo // 16:hi // 16]), tabk + [uk], [nm + "x%d" % lo], hi - lo)
        if end < base + 1024:
            ttg(y[:, end:base + 1024], win.indirect(off[:, end // 16:(base + 1024) // 16]),
                T.dt2[:, 0:base + 1024 - end], OP.min, tabk + [uk, "dt2"], [nm + "f%d" % end], base + 1024 - end)
            keys.append(nm + "f%d" % end)
        for lo, hi in pieces:
            lo, hi = lo + base, hi + base
            tt(y[:, lo:hi], x[:, lo:hi], T.b5[:, 0:hi - lo], OP.min, [nm + "x%d" % lo, "B5.d"], [nm + "y%d" % lo], hi - lo)
            keys.append(nm + "y%d" % lo)
        return keys

    def scores(out, k, const, l, ck, y, base, keys):
        mm(out, l, const, True, False, ck, [k], 64)
        for a in range(16):
            mm(out, T.sel[:, 127 * a:127 * a + 128], y[:, base + a:base + 1024:16], False, a == 15, ["sel"] + keys, [k], 64)

    def pools(t, share):
        index(T.b3[:, 0:64], "B3.o", T.oq, T.of, 0, 64, [(T.ou, 0.0, "oua")], "oa")
        index(T.b3[:, 64:256], "B3.o", T.oq, T.of, 64, 256, [(T.ou, 0.0, "oub")], "ob")
        for c in range(4):
            keys = block(T.xo, T.yo_, T.ou, 1024 * c, share[c], "o", "oub" if c else "oua")
            scores(T.b0[:, 64 * c:64 * c + 64], "B0.s", T.cpool[:, 64 * c:64 * c + 64], T.onesn[:], ["onesn", "cpool"],
                   T.yo_, 1024 * c, keys)

    def pool_min():
        act(T.sohi[:], T.b0[:, 128:256], ["B0.s"], ["sohi"], 128)
        tt(T.p128[:], T.b0[:, 0:128], T.sohi[:], OP.min, ["B0.s", "sohi"], ["p128"], 128)
        tt(T.p64[:], T.p128[:, 0:64], T.p128[:, 64:128], OP.min, ["p128"], ["p64"], 128)
        tt(T.p32[:], T.p64[:, 0:32], T.p64[:, 32:64], OP.min, ["p64"], ["p32"], 64)
        tt(T.p16[:], T.p32[:, 0:16], T.p32[:, 16:32], OP.min, ["p32"], ["p16"], 32)
        tt(T.omin[:], T.p16[:, 0:8], T.p16[:, 8:16], OP.min, ["p16"], ["omin"], 16)

    def pool_card(t):
        actg(T.thr2[:], T.omin[:].indirect(T.bc[:]), ["omin", "bc"], ["thr2"], 256)
        tt(T.oh[:, 128:384], T.b0[:, 0:256], T.thr2[:], EQ, ["B0.s", "thr2"], ["oho"], 256)
        tt(T.com[:, 128:384], T.oh[:, 128:384], T.b3[:, 0:256], OP.mult, ["oho", "B3.o"], ["com"], 256)
        mm(T.b3[:, 0:256], T.eye16[:], T.o16[:], True, False, ["eye16", "o16"], ["B3.o"], 256)
        for u in range(t):
            mm(T.b3[:, 0:256], T.eye16[:], T.to16[:, 256 * u:256 * u + 256], False, False, ["eye16", "to%d" % u],
               ["B3.o"], 256)
        for j in range(2):
            mm(T.b6[:, 0:128], T.com[:, 128 + 128 * j:256 + 128 * j], T.eye16[:], j == 0, j == 1, ["com", "eye16"],
               ["B6.t0"], 128)
        act(T.tco[:], T.b6[:, 0:128], ["B6.t0"], ["tco"], 128)
        mm(T.b2[:, 128:256], T.tco[:], T.rf[:], True, False, ["tco", "rf"], ["B2.w"], 512)
        mm(T.b2[:, 128:256], T.meye16[:], T["c%d" % t][:], False, True, ["meye16", "c%d" % t], ["B2.w"], 128)

    def pack_index(t):
        boost[0] = 5.0
        index(T.b4[:, 0:128], "B4.c", T.pq, T.pfc, 0, 128, [(T.pu, 0.0, "pu")], "p")
        boost[0] = 0.0

    def packs(t, share):
        all_keys = []
        for c in range(2):
            keys = block(T.xp, T.yp, T.pu, 1024 * c, share[4 + c], "p", "pu")
            scores(T.b1[:, 64 * c:64 * c + 64], "B1.s%d" % c, T.enc16[:, 64 * c:64 * c + 64], T.eye16[:],
                   ["eye16", "enc16"], T.yp, 1024 * c, keys)
            all_keys += keys
            if c == 0:
                act(T.losb[:], T.b1[:, 0:64], ["B1.s0"], ["losb"], 64)
        tt(T.w64[:], T.b1[:, 64:128], T.losb[:], OP.max, ["B1.s1", "losb"], ["w64"], 64)
        tt(T.w32[:], T.w64[:, 0:32], T.w64[:, 32:64], OP.max, ["w64"], ["w32"], 64)
        tt(T.w16[:], T.w32[:, 0:16], T.w32[:, 16:32], OP.max, ["w32"], ["w16"], 32)
        tt(T.m1[:], T.w16[:, 0:8], T.w16[:, 8:16], OP.max, ["w16"], ["m1"], 16)
        return all_keys

    def pack_to_psum(t):
        mm(T.b4[:, 0:128], T.eye16[:], T["c%d" % t][:], True, True, ["eye16", "c%d" % t], ["B4.c"], 128)

    def send(t):
        rid, pid, _ = topo.addr(nxt)
        m = 0
        for en in topo.engines(core, nxt)[:NENG]:
            m |= 1 << en
        sem = "arr%d" % (t + 1)
        src, dst = T["n%d" % t][:], T["c%d" % (t + 1)][:]
        do("G", lambda: g.remote_dma(dst, src, T.sem[sem], T.sem.loc, pid, rid, m), ["n%d" % t], ["c%d" % (t + 1)],
           1.0, WIRE, (sem, NENG))

    def exchange(t, ykeys):
        last = t == NV - 1
        mo = ["m1", "omin"]
        tt(T.thi[:], T.m1[:], T.omin[:], OP.max, mo, ["thi"], 16)
        tt(T.thf[:], T.m1[:], T.omin[:], OP.max, mo, ["thf"], 16)
        ts(T.offi[:], T.thi[:], 4095, None, OP.bitwise_and, None, ["thi"], ["offi"], 8)
        cp(T.offu[:], T.offi[:], ["offi"], ["offu"], 8)
        actg(T.thr[:], T.thf[:].indirect(T.bc[:, 0:8]), ["thf", "bc"], ["thr"], 128)
        ttg(T.gt[:], T.yp[:].indirect(T.offu[:]), T.dt_[:], OP.is_ge, ykeys + ["ypz", "offu", "dt"], ["gt"], 128)
        mm(T.b7[:, 0:128], T.eyeb[:], T.dt_[:], True, False, ["eyeb", "dt"], ["B7.d"], 128)
        mm(T.b7[:, 0:128], T.m4eye[:], T.gt[:], False, True, ["m4eye", "gt"], ["B7.d"], 128)
        ts(T.dt_[:], T.b7[:, 0:128], 1.0, None, OP.max, None, ["B7.d"], ["dt"], 128)
        if last:
            act(T.yd_f[:], T.dt_[:], ["dt"], ["yd_f"], 128)
            store("Y", "st_yd", T.yd[:], T.yd_f[:], ["yd_f"])
        tt(T.oh[:, 0:128], T.b1[:, 0:128], T.thr[:], OP.is_ge, ["B1.s0", "B1.s1", "thr"], ["ohc"], 128)
        tt(T.com[:, 0:128], T.oh[:, 0:128], T.b2[:, 128:256], OP.mult, ["ohc", "B2.w"], ["tuc"], 128)
        tt(T["n%d" % t][:], T.com[:, 0:128], T.b4[:, 0:128], OP.add, ["tuc", "B4.c"], ["n%d" % t], 128)
        if not last:
            send(t)
        mm(T.b6[:, 128:256], T.com[:, 0:128], T.eye16[:], True, True, ["tuc", "eye16"], ["B6.t"], 128)
        if not last:
            mm(T.b2[:, 0:128], T.ones[:], T.oh[:, 0:128], True, True, ["ones", "ohc"], ["B2.k"], 128)
            act(T.cscr[:], T.b2[:, 0:128], ["B2.k"], ["cnt", "cscr"], 128, T.cnt[:])
            act(T.kr[:], T.cnt[:], ["cnt"], ["kr"], 1, None, 1.0, KOFF - 15.5)
            do("A", lambda: a_.activation(T.kf[:], T.kr[:], AF.Identity, bias=T.cnt[:], scale=-1.0), ["kr", "cnt"],
               ["kf"], vec(1))
            seats_e()
        cp(T.tc16[:], T.b6[:, 128:256], ["B6.t"], ["tc16"], 128)
        mm(T.b6[:, 256:512], T.tc16[:], T.r256[:], True, True, ["tc16", "r256"], ["B6.d"], 256)
        to = T.to16[:, 256 * t:256 * t + 256]
        tt(to, T.oh[:, 128:384], T.b6[:, 256:512], OP.mult, ["oho", "B6.d"], ["to%d" % t], 256)
        mm(T.b3[:, 0:256], T.eye16[:], to, False, True, ["eye16", "to%d" % t], ["B3.o"], 256)
        if not last:
            spread_d(t < NV - 2)

    Q = [T.q3[:, 128 * i:128 * i + 128] for i in range(3)]
    RW = [T.rw3[:, 1024 * i:1024 * i + 1024] for i in range(3)]
    BK = [T.b0, T.b1, T.b2]
    cp(T.pk16[:], T.pk_i[:], ["pk_i"], ["pk16"], 128)
    cp(T.poa16[:], T.po_i[:, 0:256:2], ["po_i"], ["poa16"], 128)
    cp(T.pob16[:], T.po_i[:, 1:256:2], ["po_i"], ["pob16"], 128)
    boost[0] = EARLY
    seats_e()
    boost[0] = 0.0
    for i, (src, p) in enumerate([("pk16", "perm16"), ("poa16", "eye16"), ("pob16", "eye16")]):
        mm(T.b0[:, 128 * i:128 * i + 128], T[src][:], T[p][:], True, True, [src, p], ["B0.q%d" % i], 128)
    cp(T.q3[:], T.b0[:, 0:384], ["B0.q0", "B0.q1", "B0.q2"], ["q3"], 384)
    for b in range(8):
        ts(T.rw3[:, b:3072:8], T.q3[:], T.mb[:, b:b + 1], None, OP.mult, None, ["q3", "mb"], ["rw%d" % b], 192)
    for i, (out, k) in enumerate([(T.b4[:, 0:128], "B4.c"), (T.b3[:, 0:128], "B3.o"), (T.b3[:, 128:256], "B3.o")]):
        for x in range(8):
            mm(out, T.zb[:, 112 - 16 * x:240 - 16 * x], T.rw3[:, 1024 * i + 128 * x:1024 * i + 128 * x + 128],
               x == 0, x == 7, ["zb"] + ["rw%d" % b for b in range(8)], [k], 128)
    cp(T.c0[:], T.b4[:, 0:128], ["B4.c"], ["c0"], 128)
    spread_d()
    pack_index(0)
    cp(T.o16[:], T.b3[:, 0:256], ["B3.o"], ["o16"], 256)

    for t in range(NV - 1):
        share = SHARE
        pools(t, share)
        pool_min()
        pool_card(t)
        if t:
            pack_to_psum(t)
            pack_index(t)
        exchange(t, packs(t, share))

    t = NV - 1

    def chain(off, okey, y, acc, half, out, key):
        two = key == "cb"
        for i in range(2 if two else 3):
            actg(y[:, 512 * i:512 * i + 512], win.indirect(off[:, 32 * i:32 * i + 32]), tabk + [okey], [key + "g%d" % i], 512)
        ttg(acc[0][:], win.indirect(off[:, 96:128]), y[:, 0:512], OP.max, tabk + [okey, key + "g0"], [key + "0"], 512)
        if two:
            ttg(acc[1][:], win.indirect(off[:, 64:96]), acc[0][:], OP.max, tabk + [okey, key + "0"], [key + "1"], 512)
        for i, b in ((2, T.b6),) if two else ((1, T.b2), (2, T.b6)):
            bk = ("B2." if i == 1 else "B6.") + key
            q = i - 1 if two else i
            mm(b[:], T.eyeb[:], y[:, 512 * q:512 * q + 512], True, True, ["eyeb", key + "g%d" % q], [bk], 512)
            if i == 1:
                tt(acc[1][:], acc[0][:], b[:], OP.max, [key + "0", bk], [key + "1"], 512)
            else:
                tt(acc[0][:, 0:256], acc[1][:, 0:256], b[:, 0:256], OP.max, [key + "1", bk], [key + "2"], 256)
                tt(T.b0[:, 0:256], acc[1][:, 256:512], b[:, 256:512], OP.max, [key + "1", bk], ["B0." + key], 256)
        tt(half[:], acc[0][:, 0:256], T.b0[:, 0:256], OP.max, [key + "2", "B0." + key], [key + "h"], 256)
        tt(out[0], half[:, 0:128], half[:, 128:256], OP.max, [key + "h"], [out[1]], 256)
    index(T.n0[:], "n0", T.mq, T.mfc, 0, 128, [(T.mu, 0.0, "mu"), (T.mz, -float(ZC), "mz")], "m")
    chain(T.mu, "mu", T.yb, [T.acc0, T.acc1], T.bh, (T.b1[:, 0:128], "B1.bm"), "cb")
    pack_to_psum(t)
    pack_index(t)
    tt(T.b4[:, 128:256], T.n0[:], T.b4[:, 0:128], EQ, ["n0", "B4.c"], ["B4.stay"], 128)
    tt(T.sz[:], T.b4[:, 128:256], T.mz[:], OP.mult, ["B4.stay", "mz"], ["sz"], 128)
    ts(T.au[:], T.sz[:], float(ZC), None, OP.add, None, ["sz"], ["au"], 128)
    chain(T.au, "au", T.ya, [T.acc2, T.acc3], T.ah, (T.amax[:], "cam"), "ca")
    tt(T.up[:], T.amax[:], T.b1[:, 0:128], OP.is_ge, ["cam", "B1.bm"], ["up"], 128)
    ts(T.b4[:, 384:512], T.up[:], 16.0, -8.0, OP.mult, OP.add, ["up"], ["B4.up8"], 128)
    tt(T.dsum[:], T.dt_[:], T.b4[:, 384:512], OP.add, ["dt", "B4.up8"], ["dsum"], 128)
    ts(T.dt_[:], T.dsum[:], 1.0, 255.0, OP.max, OP.min, ["dsum"], ["dt"], 128)
    spread_d(False)
    pools(t, [FULL] * 6)
    pool_min()
    pool_card(t)
    exchange(t, packs(t, [FULL] * 6))

    ts(T.permf16[:], T.ipermf[:], PC, None, EQ, None, ["ipermf", "pcol"], ["permf16"], 128)
    ts(T.prev[:], D8, -1.0, 15.0, OP.mult, OP.add, ["pf"], ["prev"], 1)
    ts(T.mf[:], T.i8[:, 0:8], P8, None, EQ, None, ["i8", "pf"], ["mf"], 8)
    ts(T.zfo[:], T.ic[:], D8, None, EQ, None, ["ic", "pf"], ["zfo"], 240)
    ts(T.zfp[:], T.ic[:], T.prev[:], None, EQ, None, ["ic", "prev"], ["zfp"], 240)

    def seats_to_list(i, src, skey, z, zk, out, ok, dst, dk):
        k = "B%d.f" % i
        mm(BK[i][:, 384:512], src, T.permf16[:], True, True, [skey, "permf16"], [k], 128)
        cp(Q[i], BK[i][:, 384:512], [k], ["q%d" % i], 128)
        for b in range(8):
            ts(RW[i][:, 128 * b:128 * b + 128], Q[i], T.mf[:, b:b + 1], None, OP.mult, None, ["q%d" % i, "mf"],
               ["rx%d%d" % (i, b)], 64)
        for x in range(8):
            mm(out, z[:, 112 - 16 * x:240 - 16 * x], RW[i][:, x:1024:8], x == 0, x == 7,
               [zk] + ["rx%d%d" % (i, b) for b in range(8)], [ok], 128)
        act(dst, out, [ok], [dk], 128)
    oe, oek = T.o16[:], "o16"
    cp(oe, T.b3[:, 0:256], ["B3.o"], [oek], 256)
    seats_to_list(0, T["n%d" % t][:], "n%d" % t, T.zfp, "zfp", T.b4[:, 0:128], "B4.y", T.yc_f[:], "yc_f")
    seats_to_list(1, oe[:, 0:128], oek, T.zfo, "zfo", T.b5[:, 0:128], "B5.y", T.yo_f[:, 0:256:2], "yo_f0")
    seats_to_list(2, oe[:, 128:256], oek, T.zfo, "zfo", T.b7[:, 0:128], "B7.y", T.yo_f[:, 1:256:2], "yo_f1")
    store("Y", "st_yc", T.yc[:], T.yc_f[:], ["yc_f"])
    store("Y", "st_yo", T.yo[:], T.yo_f[:], ["yo_f0", "yo_f1"])

    n = len(ops)
    preds = [{} for _ in range(n)]
    lastw, readers, bankacc = {}, {}, {}
    for i, (eng, call, reads, writes, dur, lat, tok) in enumerate(ops):
        def edge(j, wait, i=i):
            if j != i:
                preds[i][j] = preds[i].get(j, False) or wait
        for k in reads:
            if k in lastw:
                edge(lastw[k], True)
        for k in writes:
            if k in lastw:
                edge(lastw[k], ops[lastw[k]][0] != eng)
            for j in readers.get(k, []):
                edge(j, ops[j][0] != eng or ops[j][6] is not None)
        for k in sorted({k[:2] for k in reads + writes if k[0] == "B"}):
            turn = bankacc.setdefault(k, [eng, [], []])
            if turn[0] != eng:
                turn[0], turn[1], turn[2] = eng, turn[2], []
            for j in turn[1]:
                edge(j, True)
            if eng == "P" and turn[2]:
                edge(turn[2][-1], False)
            turn[2].append(i)
        for k in reads:
            readers.setdefault(k, []).append(i)
        for k in writes:
            lastw[k] = i
            readers[k] = []
    succs = [[] for _ in range(n)]
    for i in range(n):
        for j in preds[i]:
            succs[j].append(i)
    prio = [0.0] * n
    for i in range(n - 1, -1, -1):
        own = ops[i][4] + ops[i][5]
        best = 0.0
        for s in succs[i]:
            best = max(best, prio[s] + (own + HOP if preds[s][i] else ops[i][4]))
        prio[i] = max(best, own)

    left = [len(p) for p in preds]
    est = [0.0] * n
    ready = {e: [] for e in queues}
    free = {e: 0.0 for e in queues}
    for i in range(n):
        if left[i] == 0:
            ready[ops[i][0]].append(i)
    sequence = []
    for _ in range(n):
        pick = None
        for e in queues:
            if ready[e]:
                st = max(free[e], min(est[i] for i in ready[e]))
                i = max((i for i in ready[e] if est[i] <= st + 1e-9), key=lambda i: (prio[i] + boosts[i], -i))
                if pick is None or st < pick[0]:
                    pick = (st, e, i)
        st, e, i = pick
        ready[e].remove(i)
        sequence.append(i)
        free[e] = st + ops[i][4]
        for s in succs[i]:
            est[s] = max(est[s], free[e] + (ops[i][5] + HOP if preds[s][i] else 0.0))
            left[s] -= 1
            if left[s] == 0:
                ready[ops[s][0]].append(s)

    count = {e: 0 for e in counters}
    waited = {e: {} for e in queues}
    token = {}

    def need(e, tok):
        s, c = tok
        if waited[e].get(s, 0) < c:
            queues[e].wait_ge(T.sem[s], c)
            waited[e][s] = c

    for i in sequence:
        eng, call, reads, writes, dur, lat, tok = ops[i]
        toks = {}
        for j, w in preds[i].items():
            if w and token[j][1] > toks.get(token[j][0], 0):
                toks[token[j][0]] = token[j][1]
        for s in toks:
            need(eng, (s, toks[s]))
        if tok is None:
            count[eng] += 1
            call().then_inc(T.sem[counters[eng]], 1)
            token[i] = (counters[eng], count[eng])
        else:
            call()
            token[i] = tok
    for e in counters:
        need("G", (counters[e], count[e]))
    for s in LOADS + STORES:
        need("G", (s, 16))
    need("G", ("loc", NENG * len(ARR)))
    for s in ARR:
        need("G", (s, NENG))
